import numpy as np, ml_dtypes
CORES = [8,136,40,168]
N = 4
BF = ml_dtypes.bfloat16
def gentries(a):
    return np.ascontiguousarray(a.reshape(8, 16, -1).transpose(0, 2, 1)).reshape(8, -1)
def gtable(e):
    e = np.asarray(e); return np.ascontiguousarray(e.reshape(8, -1, 16).transpose(0, 2, 1)).reshape(128, -1).astype(np.int32)
D, NB, S, NEED, RO = 2048, 256, 8, 2, 5
P = S // 2; M = NB * P; W = D + M
TOP, NEAR = 255, 16
def parts(rng):
    pat = 2 * rng.integers(0, 2, (N, 8, 16, 1)) - 1; sgn = 2 * rng.integers(0, 2, (N, 8, 1, D)) - 1
    amp = rng.random((N, 8, 1, D)) * np.where(rng.random((N, 8, 1, D)) < 0.88, 49.5, 126.5)
    x = np.clip(np.rint(127.5 + pat * sgn * amp + 8.8 * rng.standard_normal((N, 8, 16, D))), 0, TOP).astype(np.int64)
    return x, rng.integers(0, 2 * W, (N, 8, D)), rng.integers(0, 2 * W, (N, 8, D)), rng.integers(0, 2 * W, (N, 8, NB, S)), rng.integers(0, 2, (N, 8, NB))
def pack(x, k0, k1, L, f):
    return {"faces": np.ascontiguousarray(x.reshape(N, 128, D)).astype(np.float32).astype(BF), "kid0": k0.astype(np.int32), "kid1": k1.astype(np.int32),
            "belts": np.stack([gtable(a.reshape(8, -1)) for a in L]), "flip": f.astype(np.int32)}
def planted(rng, z, n, few):
    x, k0, k1, L, f = z; cs = np.array([0, 1, 7, 8, 9, 10, 15, 16])
    hit = np.argsort(np.argsort(rng.random((N, 8, NB, P)), axis=-1), axis=-1) < n[..., None]
    for g in range(8):
        o = rng.permutation(D); sen = rng.integers(0, 2, D); c = np.zeros(D, np.int64); c[o] = cs[(np.arange(D) // 4) % 8]
        bl, fa, pt = o[1::4], o[2::4], o[3::4]; hi = fa[c[fa] >= 9]; lo = fa[c[fa] < 9]; sh = (N, 16, len(fa))
        close = np.where(rng.random(sh) < 0.5, NEAR, rng.integers(0, NEAR + 1, sh)); far = np.where(rng.random(sh) < 0.5, NEAR + 1, rng.integers(NEAR + 1, TOP + 1, sh))
        v = np.where(np.argsort(rng.random(sh), axis=1) < c[fa], close, far)
        y = x[:, g]; y[:, :, fa] = np.where(sen[fa] == 1, TOP - v, v); y[:, :, bl] = TOP * sen[bl]
        def twin(a):
            return 2 * D * ((a < M) & (rng.random(a.shape) < 0.5))
        def good(a):
            return 2 * a + sen[a] + twin(a)
        def some(a):
            return np.full((N, NB, P), a[int(rng.integers(0, len(a)))]) if few[g] else a[rng.integers(0, len(a), (N, NB, P))]
        q0 = k0[:, g]; q1 = k1[:, g]
        q0[:, pt] = good(bl[rng.integers(0, len(bl), (N, len(pt)))]); q1[:, pt] = good(bl[rng.integers(0, len(bl), (N, len(pt)))]) ^ 1
        lh = good(np.where(hit[:, g], some(hi), some(lo))); pk = some(pt); lk = 2 * pk + rng.integers(0, 2, pk.shape) + twin(pk)
        k = (2 * np.arange(P) + f[:, g, :, None]) % S; l = L[:, g]
        np.put_along_axis(l, k, lk, 2); np.put_along_axis(l, (k + 1) % S, lh, 2)
    return x, k0, k1, L, f
def setup_inputs(rng):
    return pack(*parts(rng))
def setup_inputs_spread(rng):
    x, k0, k1, L, f = parts(rng)
    pat = 2 * rng.integers(0, 2, (N, 8, 16, 1)) - 1; sgn = 2 * rng.integers(0, 2, (N, 8, 1, D)) - 1; amp = np.exp2(7.5 * rng.random((N, 8, 1, D)) - 0.5)
    x = np.clip(np.rint(127.5 + pat * sgn * amp + 5.5 * rng.standard_normal((N, 8, 16, D))), 0, TOP).astype(np.int64)
    x = np.where(rng.random((N, 8, 1, D)) < 0.125, rng.integers(0, TOP + 1, x.shape), x)
    z = []
    for a in (k0, k1, L):
        e = np.minimum((2 * W * rng.random(a.shape) ** 3).astype(np.int64), 2 * W - 1); e[:, 1::2] = 2 * W - 1 - e[:, 1::2]; z.append(e)
    f = (rng.random((N, 8, NB)) < 0.1 + 0.8 * rng.random((N, 8, 1))).astype(np.int64)
    return pack(x, z[0], z[1], z[2], f)
def mixends(rng, shape):
    return np.where(rng.random(shape) < 0.75, (2 * W - 1) * rng.integers(0, 2, shape), rng.integers(0, 2 * W, shape))
def setup_inputs_ends(rng):
    kind = rng.integers(0, 3, (N, 8, 1, D)); x = TOP * np.where(kind == 2, rng.integers(0, 2, (N, 8, 16, D)), kind)
    k0 = mixends(rng, (N, 8, D)); k1 = mixends(rng, (N, 8, D)); k0[..., M - 1] = 0; k1[..., 0] = 0
    f = rng.integers(0, 2, (N, 8, NB)); f[..., 0] = 0; f[..., NB - 1] = 1
    for q in (0, 1, N - 1): x[q, :, :, M - 1] = TOP - x[q, :, :, 0]
    L = mixends(rng, (N, 8, NB, S)); ks = ((np.arange(S) - f[..., None]) & 1) == 0; hs = (2 * W - 1) * rng.integers(0, 2, L.shape)
    calm = np.where(ks, 0, hs); wild = np.where(ks, 2 * W - 1, hs); full = np.where(ks, 2 * W - 1, 0)
    L[:, :, NB - 1] = full[:, :, NB - 1]; L[:, :, NB - 2] = 0
    L[0] = calm[0]; L[1] = calm[1]; L[1, 7, NB - 1] = full[1, 7, NB - 1]; L[N - 1] = wild[N - 1]
    return pack(x, k0, k1, L, f)
def setup_inputs_corners(rng):
    x, k0, k1, L, f = parts(rng); own = 2 * np.arange(D)
    for a in (k0, k1):
        w = rng.integers(0, 8, a.shape); e = rng.integers(0, 2, a.shape)
        a[...] = np.where(w == 0, own + e, np.where(w == 1, e, np.where(w == 2, 2 * W - 2 + e, np.where(w == 3, own[::-1] + e, a))))
    w = rng.integers(0, 6, (N, 8, NB, 1)); one = rng.integers(0, 2 * W, (N, 8, NB, 1))
    old = np.where(w == 0, one, np.where(w == 1, 0, np.where(w == 2, 2 * W - 1, L)))
    n = rng.choice(np.array([0, 1, NEED - 1, NEED, NEED + 1, P]), (N, 8, NB)); n[N - 1, 7, NB - 1] = P; n[0, 0, 0] = NEED; n[1, 0, 0] = NEED - 1
    x, k0, k1, L, f = planted(rng, (x, k0, k1, L, f), n, np.zeros(8, np.int64))
    m = rng.random((N, 8, NB, 1)) < 0.25; m[N - 1, 7, NB - 1] = False; m[:2, 0, 0] = False
    return pack(x, k0, k1, np.where(m, old, L), f)
def setup_inputs_crowd(rng):
    n = np.zeros((N, 8, NB), np.int64); low = np.array([0, NEED - 1]); top = np.array([NEED, P])
    for q in range(N):
        n[q] = rng.choice(low if q % 4 < 2 else top, (8, NB))
        if q % 4 == 1: n[q, 7, NB - 1] = P
        if q % 4 == 2: n[q, 7, NB - 1] = NEED - 1
    return pack(*planted(rng, parts(rng), n, 1 - np.arange(8) % 2))
def setup_inputs_stale(rng):
    x, k0, k1, L, f = parts(rng); z = int(rng.integers(0, N)); y = (z + 2) % N
    sh = (N, 16, D)
    for g in range(8):
        o = rng.permutation(D); sen = rng.integers(0, 2, D); bl, h1, h2, al, pt = o[0::5], o[1::5], o[2::5], o[3::5], o[4::5]
        c = rng.choice(np.array([0, 1, 7, 8]), (N, D)); c[:, al] = 16
        c[z, pt] = rng.choice(np.array([10, 16]), len(pt)); c[y, pt] = 9; c[z, h2] = 9; c[y, h1] = 9
        close = np.where(rng.random(sh) < 0.5, NEAR, rng.integers(0, NEAR + 1, sh)); far = np.where(rng.random(sh) < 0.5, NEAR + 1, rng.integers(NEAR + 1, TOP + 1, sh))
        v = np.where(np.argsort(rng.random(sh), axis=1) < c[:, None, :], close, far); v[:, :, bl] = 0
        x[:, g] = np.where(sen == 1, TOP - v, v)
        b0 = bl[rng.integers(0, len(bl), (N, D))]; b1 = bl[rng.integers(0, len(bl), (N, D))]
        k0[:, g] = 2 * b0 + sen[b0]; k1[:, g] = (2 * b1 + sen[b1]) ^ 1
        hp = h2[rng.integers(0, len(h2), (N, NB, P))]; hp[z] = h1[rng.integers(0, len(h1), (NB, P))]
        if 1 <= g <= 5:
            for q in (z, y):
                i = NB - 1 if g == 5 else int(rng.integers(0, NB))
                hp[q, i] = al[rng.integers(0, len(al), P)]
        pk = pt[rng.integers(0, len(pt), (N, NB, P))]
        k = (2 * np.arange(P) + f[:, g, :, None]) % S; l = L[:, g]
        np.put_along_axis(l, k, (2 * pk + sen[pk]) ^ 1, 2); np.put_along_axis(l, (k + 1) % S, 2 * hp + sen[hp], 2)
    return pack(x, k0, k1, L, f)
def check_inputs(d):
    bad = []
    for k, lo, hi in (("faces", 0, TOP), ("kid0", 0, 2 * W - 1), ("kid1", 0, 2 * W - 1), ("belts", 0, 2 * W - 1), ("flip", 0, 1)):
        v = np.asarray(d[k]).astype(np.float64)
        if not (np.min(v) >= lo and np.max(v) <= hi): bad.append("range of " + k)
        if np.any(v != np.floor(v)): bad.append("whole numbers in " + k)
    return bad
def values(x, e):
    v = np.take_along_axis(x, (e >> 1)[:, :, None, :], 3)
    return np.where((e & 1)[:, :, None, :] == 1, TOP - v, v)
def reference(faces, kid0, kid1, belts, flip):
    x = faces.astype(np.float32).astype(np.int32).reshape(N, 8, 16, D); x = np.concatenate([x, x[..., :M]], axis=3)
    k0 = kid0.astype(np.int64); k0 = np.concatenate([k0, k0[..., :M]], axis=2)
    k1 = kid1.astype(np.int64); k1 = np.concatenate([k1, k1[..., :M]], axis=2)
    L = np.stack([gentries(a) for a in belts]).astype(np.int64).reshape(N, 8, NB, S); f = flip.astype(np.int64)
    A = np.zeros(N, np.int64); new = 2 * (D + np.arange(M)).reshape(NB, P)
    for t in range(RO):
        if t > 0:
            L = np.roll(L, 1, axis=0); f = np.roll(f, 1, axis=0)
        k = (2 * np.arange(P) + f[..., None]) % S; h = (k + 1) % S
        lk = np.take_along_axis(L, k, 3); lh = np.take_along_axis(L, h, 3)
        e = lk.reshape(N, 8, M); w = lh.reshape(N, 8, M); odd = (e & 1) == 1
        c0 = np.take_along_axis(k0, e >> 1, 2); c1 = np.take_along_axis(k1, e >> 1, 2)
        a = np.where(odd, c1 ^ 1, c0); b = np.where(odd, c0 ^ 1, c1); u = b ^ 1
        fu = values(x, u); fw = values(x, w)
        near = np.add.reduce((np.abs(fu - fw) <= NEAR).astype(np.int64), axis=2)
        split = (near >= 9 + (A & 1)[:, None, None]).reshape(N, 8, NB, P)
        opens = np.add.reduce(split.astype(np.int64), axis=3) >= NEED
        go = split & opens[..., None]; gm = go.reshape(N, 8, M)
        x = np.concatenate([x[..., :D], np.where(gm[:, :, None, :], (fu + fw) >> 1, x[..., D:])], axis=3)
        k0 = np.concatenate([k0[..., :D], np.where(gm, u, k0[..., D:])], axis=2)
        k1 = np.concatenate([k1[..., :D], np.where(gm, w, k1[..., D:])], axis=2)
        l2 = np.array(L)
        np.put_along_axis(l2, k, np.where(go, a.reshape(N, 8, NB, P), lk), 3); np.put_along_axis(l2, h, np.where(go, new, lh), 3)
        L = np.where(opens[..., None], l2, L ^ 1); f = np.where(opens, f, 1 - f)
        A = np.add.reduce((~opens).astype(np.int64).reshape(N, 8 * NB), axis=1)
    return {"yx": x.reshape(N, 128, W).astype(np.float32).astype(BF), "y0": k0.astype(np.float32), "y1": k1.astype(np.float32),
            "yb": np.stack([gtable(q.reshape(8, -1)) for q in L]).astype(np.float32), "yf": f.astype(np.float32)}

@@ -1,0 +1,527 @@
+from concourse.mybir import AluOpType, AxisListType, ActivationFunctionType
+
+RO = 5
+SCRATCH = {
+    "FA": ("sbuf", [128, 2048], "bfloat16"), "FT": ("sbuf", [128, 6144], "bfloat16"),
+    "KT": ("sbuf", [128, 6144], "bfloat16"), "VW": ("sbuf", [128, 6144], "float32"),
+    "GK": ("sbuf", [128, 1024], "bfloat16"), "FW": ("sbuf", [128, 1024], "bfloat16"),
+    "DD": ("sbuf", [128, 1024], "bfloat16"), "NR": ("sbuf", [128, 1024], "bfloat16"),
+    "YX": ("sbuf", [128, 1024], "bfloat16"),
+    "K0": ("sbuf", [128, 128], "int32"), "K1": ("sbuf", [128, 128], "int32"), "KO": ("sbuf", [128, 128], "int32"),
+    "K0F": ("sbuf", [128, 128], "float32"), "K1F": ("sbuf", [128, 128], "float32"),
+    "BI": ("sbuf", [128, 128], "int32"), "BF": ("sbuf", [128, 128], "float32"), "AB": ("sbuf", [128, 128], "float32"),
+    "FI": ("sbuf", [128, 256], "int32"), "FB": ("sbuf", [128, 256], "bfloat16"), "FO": ("sbuf", [128, 256], "float32"),
+    "HI": ("sbuf", [128, 256], "bfloat16"), "LO": ("sbuf", [128, 256], "bfloat16"),
+    "YS": ("sbuf", [128, 512], "bfloat16"), "Y0": ("sbuf", [128, 512], "bfloat16"), "Y1": ("sbuf", [128, 512], "bfloat16"),
+    "D0": ("sbuf", [128, 256], "bfloat16"), "D2": ("sbuf", [128, 128], "bfloat16"),
+    "NL": ("sbuf", [128, 256], "float32"), "XX": ("sbuf", [128, 256], "float32"), "M2": ("sbuf", [128, 256], "bfloat16"),
+    "SE": ("sbuf", [128, 256], "float32"), "SW": ("sbuf", [128, 256], "float32"),
+    "AH": ("sbuf", [128, 64], "float32"), "UU": ("sbuf", [128, 128], "float32"), "SP": ("sbuf", [128, 64], "bfloat16"),
+    "UO": ("sbuf", [128, 64], "uint16"), "LC": ("sbuf", [128, 64], "uint16"), "E0": ("sbuf", [128, 64], "uint16"),
+    "TM": ("sbuf", [128, 128], "float32"), "TN": ("sbuf", [128, 128], "float32"), "OUT": ("sbuf", [128, 128], "float32"),
+    "OB": ("sbuf", [128, 128], "float32"),
+    "CC": ("sbuf", [128, 640], "float32"), "CI": ("sbuf", [128, 384], "float32"), "MH": ("sbuf", [128, 64], "float32"),
+    "IK": ("sbuf", [128, 8], "int32"), "IJ": ("sbuf", [128, 8], "int32"), "MK": ("sbuf", [128, 8], "float32"),
+    "COL": ("sbuf", [128, 16], "float32"),
+    "ZF": ("sbuf", [128, 128], "float32"), "ZB": ("sbuf", [128, 576], "bfloat16"), "ONE": ("sbuf", [128, 144], "bfloat16"),
+    "Q4": ("sbuf", [128, 64], "bfloat16"), "Q8": ("sbuf", [128, 128], "bfloat16"), "O4": ("sbuf", [128, 128], "bfloat16"),
+    "KM": ("sbuf", [128, 128], "float32"),
+    "RT": ("sbuf", [128, 512], "float32"), "RR": ("sbuf", [128, 1024], "float32"),
+    "I32": ("sbuf", [128, 128], "float32"), "N32": ("sbuf", [128, 128], "float32"), "UP": ("sbuf", [128, 128], "float32"),
+    "DN": ("sbuf", [128, 128], "float32"), "IU": ("sbuf", [128, 128], "float32"), "DI": ("sbuf", [128, 128], "float32"),
+    "IB": ("sbuf", [128, 128], "bfloat16"), "I2": ("sbuf", [128, 128], "bfloat16"), "NB": ("sbuf", [128, 128], "bfloat16"),
+    "B4": ("sbuf", [128, 128], "bfloat16"), "Z1": ("sbuf", [128, 128], "bfloat16"),
+    "BM": ("sbuf", [128, 144], "bfloat16"), "WA": ("sbuf", [128, 144], "bfloat16"), "WO": ("sbuf", [128, 144], "bfloat16"),
+    "WB": ("sbuf", [128, 132], "bfloat16"), "WD": ("sbuf", [128, 576], "bfloat16"), "W2": ("sbuf", [128, 576], "bfloat16"),
+    "RP": ("sbuf", [128, 512], "bfloat16"), "FF": ("sbuf", [128, 144], "bfloat16"), "FQ": ("sbuf", [128, 32], "bfloat16"),
+}
+for _t in range(RO):
+    SCRATCH["MI%d" % _t] = ("sbuf", [128, 192], "uint16")
+for _t in range(1, RO):
+    SCRATCH["MO%d" % _t] = ("sbuf", [128, 192], "uint16")
+for _b in "ABCDEFGH":
+    SCRATCH["P" + _b] = ("psum", [128, 512], "float32")
+SEMAPHORES = (["sv", "sa", "sp", "sg", "sent"] + ["d%d" % _i for _i in range(16)]
+              + ["ae%d" % _t for _t in range(1, RO)] + ["aw%d" % _t for _t in range(1, RO)])
+
+BIG = 1.5 * 2 ** 23
+B2 = 1.5 * 2 ** 24
+B32 = 1.5 * 2 ** 28
+B64 = 1.5 * 2 ** 29
+KS, C0 = 16384.0, 24576
+NV, NV1 = 4, 3
+QSEM = {"v": "sv", "a": "sa", "p": "sp", "g": "sg"}
+
+
+def emit(g, T, ops):
+    queue = {"v": g.vector, "a": g.scalar, "p": g.tensor, "g": g, "s": g.sync}
+    clock = {q: {} for q in queue}
+    writers, readers, bank = {}, {}, {}
+    seq = {}
+    for op in ops:
+        q, kind = op["q"], op["kind"]
+        op["key"] = q if kind == "c" else op["sem"]
+        seq[op["key"]] = seq.get(op["key"], 0) + 1
+        op["seq"] = seq[op["key"]]
+        deps = []
+        for r in op["r"]:
+            deps += [(o, True) for o in writers.get(r, [])]
+        for w in op["w"]:
+            deps += [(o, True) for o in writers.get(w, []) + readers.get(w, [])]
+        for b in op["b"]:
+            deps += [(o, False) for o in bank.get(b, {}).values()]
+        need = {}
+        if kind != "arr":
+            for o, data in deps:
+                if kind == "c" and o["kind"] == "c" and o["q"] == q and (not data or q == "p"):
+                    continue
+                if clock[q].get(o["key"], 0) < o["seq"] and (o["key"] not in need or need[o["key"]]["seq"] < o["seq"]):
+                    need[o["key"]] = o
+            waits = []
+            for o in sorted(need.values(), key=lambda z: -z["n"]):
+                if clock[q].get(o["key"], 0) >= o["seq"]:
+                    continue
+                waits.append(o)
+                o["used"] = True
+                for k, s in o["clk"].items():
+                    clock[q][k] = max(clock[q].get(k, 0), s)
+            op["waits"] = waits
+            op["clk"] = dict(clock[q])
+        else:
+            op["clk"] = {}
+        op["clk"][op["key"]] = op["seq"]
+        for r in op["r"]:
+            readers.setdefault(r, []).append(op)
+        for w in op["w"]:
+            writers[w] = [op]
+            readers[w] = []
+        for b in op["b"]:
+            bank.setdefault(b, {})[q] = op
+    count = {}
+    for op in ops:
+        kind = op["kind"]
+        if kind == "c":
+            if op["q"] == "p" and not op.get("used"):
+                continue
+            s = QSEM[op["q"]]
+            count[s] = count.get(s, 0) + 1
+            op["done"] = (s, count[s])
+        else:
+            count[op["sem"]] = count.get(op["sem"], 0) + op["inc"]
+            op["done"] = (op["sem"], count[op["sem"]])
+    for op in ops:
+        if op["kind"] == "arr":
+            continue
+        e = queue[op["q"]]
+        for o in op["waits"]:
+            e.wait_ge(T.sem[o["done"][0]], o["done"][1])
+        ins = op["f"]()
+        if op["kind"] == "c" and "done" in op:
+            ins.then_inc(T.sem[op["done"][0]], 1)
+        elif op["kind"] == "dma":
+            ins.then_inc(T.sem[op["sem"]], 16)
+    for s in count:
+        g.wait_ge(T.sem[s], count[s])
+
+
+def rank_program(g, core, T, topo):
+    rank = T.rank_of(core)
+    if rank is None:
+        return
+    n = len(T.cores)
+    nxt = T.cores[(rank + 1) % n]
+    prv = T.cores[(rank - 1) % n]
+    rid, pid = topo.addr(nxt, core)
+    mask = topo.mask(core, nxt)
+    n_out, n_in = len(topo.engines(core, nxt)), len(topo.engines(prv, core))
+    A, AF = AluOpType, ActivationFunctionType
+    V, S, PE = g.vector, g.scalar, g.tensor
+    ops, nd = [], [0]
+
+    def add(q, f, r=(), w=(), b=(), kind="c", sem=None, inc=0):
+        ops.append({"q": q, "f": f, "r": list(r), "w": list(w), "b": list(b), "kind": kind, "sem": sem, "inc": inc,
+                    "n": len(ops)})
+
+    def dma(q, out, in_, r=(), w=()):
+        e = {"s": g.sync, "a": g.scalar}[q]
+        add(q, lambda: e.dma_start(out, in_), r, w, kind="dma", sem="d%d" % nd[0], inc=16)
+        nd[0] += 1
+
+    def ts(out, in0, s1, s2, o0, o1=None, r=(), w=(), b=()):
+        if o1 is None:
+            add("v", lambda: V.tensor_scalar(out, in0, s1, None, o0), r, w, b)
+        else:
+            add("v", lambda: V.tensor_scalar(out, in0, s1, s2, o0, o1), r, w, b)
+
+    def tt(out, in0, in1, o, r=(), w=(), b=()):
+        add("v", lambda: V.tensor_tensor(out, in0, in1, o), r, w, b)
+
+    def cp(out, in_, r=(), w=(), b=()):
+        add("v", lambda: V.tensor_copy(out, in_), r, w, b)
+
+    def ms(ap, val, w=(), b=()):
+        add("v", lambda: V.memset(ap, val), (), w, b)
+
+    def scan(out, d0, d1, r=(), w=(), b=()):
+        add("v", lambda: V.tensor_tensor_scan(out, d0, d1, 0.0, A.mult, A.add), r, w, b)
+
+    def act(out, in_, scale=1.0, bias=0.0, r=(), w=(), b=()):
+        if isinstance(bias, float) and bias == 0.0:
+            add("a", lambda: S.activation(out, in_, AF.Copy, scale=scale), r, w, b)
+        else:
+            add("a", lambda: S.activation(out, in_, AF.Identity, bias=bias, scale=scale), r, w, b)
+
+    def step(out, in_, scale, bias, r, w, b=()):
+        add("a", lambda: S.activation(out, in_, AF.Sigmoid, bias=bias, scale=scale), r, w, b)
+
+    def mm(out, terms, w, b):
+        for i, (lh, rh, r) in enumerate(terms):
+            add("p", lambda lh=lh, rh=rh, i=i: PE.matmul(out, lh, rh, i == 0, i == len(terms) - 1), r, w, b)
+
+    def iota(out, pat, base, cm, w, flt=True):
+        if flt:
+            add("g", lambda: g.iota(out, pat, base, cm, allow_small_or_imprecise_dtypes=True), (), w)
+        else:
+            add("g", lambda: g.iota(out, pat, base, cm), (), w)
+
+    def sel(out, in_, pat, op, fill, base, cm, r, w):
+        add("g", lambda: g.affine_select(out, in_, pat, op, fill, base, cm), r, w)
+
+    def point(out, zero, pat, base, val, w):
+        sel(out, zero, pat, A.not_equal, val, base, 1, ["Z"], w)
+
+    def band(out, pat, base, width, w):
+        cols = pat[0][1] * pat[1][1]
+        sel(out, T.ONE[:, 0:cols], pat, A.is_ge, 0.0, base, 1, ["ONE"], w)
+        sel(out, out, [[-s, c] for s, c in pat], A.is_ge, 0.0, width - 1 - base, -1, w, w)
+
+    col = lambda j: T.COL[:, j:j + 1]
+    SG, R16, AL, GA, WP, PAR, RED, RND, ODD = 0, 1, 2, 3, 4, 5, 6, 7, 8
+
+    dma("s", T.K1[:], T.kid1[:], w=["K1"])
+    dma("s", T.K0[:], T.kid0[:], w=["K0"])
+    dma("a", T.FA[:, 0:1024], T.faces[:, 0:1024], w=["FA0"])
+    dma("a", T.FA[:, 1024:2048], T.faces[:, 1024:2048], w=["FA1"])
+    dma("s", T.BI[:], T.belts[:], w=["BI"])
+    dma("s", T.FI[0:8, :], T.flip[:], w=["FI"])
+
+    ms(T.ZB[:], 0.0, ["Z"])
+    ms(T.ONE[:], 1.0, ["ONE"])
+    iota(T.IK[:, 0:5], [[-1, 5]], 4, 1, ["IK"], False)
+    iota(T.KM[:], [[-1, 128]], 0, 1, ["KM"])
+    point(T.WD[:], T.ZB[:], [[-16, 9], [-1000, 4], [-1, 16]], 3000, 1.0, ["WD"])
+    band(T.BM[:], [[-16, 9], [1000, 16]], -15000, 16, ["BM"])
+    iota(T.ZF[:], [[0, 128]], 0, 0, ["ZF"])
+    for k in range(4):
+        sel(T.RT[:, 128 * k:128 * k + 128], T.ZF[:], [[-16, 8], [-1000, 2], [-2, 8]], A.not_equal, 1.0,
+            1000 * (k // 2) - k % 2, 1, ["ZF"], ["RT%d" % k])
+    point(T.FF[0:8, :], T.ZB[0:8, 0:144], [[-1, 9], [-1000, 4], [0, 4]], 3000, 1.0, ["FF"])
+    iota(T.D2[:, 0::2], [[0, 64]], 0, 0, ["D2z"])
+    iota(T.M2[:], [[0, 128], [-2, 2]], 0, 0, ["M2"])
+    iota(T.CI[:], [[1024, 6], [16, 64]], C0, 0, ["CI"])
+    band(T.B4[:], [[-4, 32], [0, 4]], 0, 4, ["B4"])
+    band(T.WB[:], [[-4, 33], [1000, 4]], -3000, 4, ["WB"])
+    iota(T.D0[:, 0::4], [[0, 64]], 0, 0, ["D0z"])
+    sel(T.Q4[:], T.ZB[:, 0:64], [[0, 64]], A.not_equal, 0.25, 0, 0, ["Z"], ["Q4"])
+
+    ts(T.IJ[:, 0:4], T.IK[:, 0:4], 3, None, A.bitwise_and, r=["IK"], w=["IJ0"])
+    ts(T.IJ[:, 4:5], T.IK[:, 4:5], 8, None, A.bitwise_and, r=["IK"], w=["IJ1"])
+    ts(T.IJ[:, 5:6], T.IK[:, 4:5], 15, None, A.bitwise_and, r=["IK"], w=["IJ2"])
+    ts(T.I32[:], T.KM[:], 0.0, None, A.is_equal, r=["KM"], w=["I32"])
+    ts(T.UP[:], T.KM[:], 1.0, None, A.is_equal, r=["KM"], w=["UP"])
+    ts(T.DN[:], T.KM[:], -1.0, None, A.is_equal, r=["KM"], w=["DN"])
+    ts(T.UP[:, 3::4], T.KM[:, 3::4], -3.0, None, A.is_equal, r=["KM"], w=["UP"])
+    ts(T.DN[:, 0::4], T.KM[:, 0::4], 3.0, None, A.is_equal, r=["KM"], w=["DN"])
+    ts(T.MK[:, 0:4], T.IJ[:, 0:4], 0.0, None, A.is_equal, r=["IJ0"], w=["MKe"])
+    ts(col(SG), T.IJ[:, 4:5], -0.25, 1.0, A.mult, A.add, r=["IJ1"], w=["SG"])
+    ts(col(R16), T.IJ[:, 5:6], 1.0 / KS, None, A.mult, r=["IJ2"], w=["R16"])
+    tt(col(ODD), T.MK[:, 1:2], T.MK[:, 3:4], A.add, r=["MKe"], w=["ODD"])
+    ts(T.MK[:, 4:8], T.MK[:, 0:4], col(SG), None, A.mult, r=["MKe", "SG"], w=["MKo"])
+    act(T.N32[:], T.I32[:], -1.0, r=["I32"], w=["N32"])
+    step(T.IB[:], T.I32[:], 1000.0, -500.0, ["I32"], ["IB"])
+    act(T.I2[:], T.I32[:], 2.0, r=["I32"], w=["I2"])
+    act(T.NB[:], T.I32[:], -1.0, r=["I32"], w=["NB"])
+    mm(T.PG[:, 0:128], [(T.I32[:], T.DN[:], ["I32", "DN"]), (T.I32[:], T.N32[:], ["N32"])], ["PG0"], ["G"])
+    mm(T.PG[:, 128:256], [(T.N32[:], T.UP[:], ["UP"]), (T.I32[:], T.I32[:], [])], ["PG1"], ["G"])
+    mm(T.PH[:, 0::2], [(T.ZB[:, 0:128], T.ZB[:, 0:256], ["Z"])], ["PH0"], ["H"])
+    act(T.DI[:], T.PG[:, 0:128], r=["PG0"], w=["DI"], b=["G"])
+    act(T.IU[:], T.PG[:, 128:256], r=["PG1"], w=["IU"], b=["G"])
+    act(T.WA[:], T.BM[:], col(SG), r=["BM", "SG"], w=["WA"])
+
+    ts(T.KO[:], T.K1[:], 1, None, A.bitwise_and, r=["K1"], w=["KO"])
+    ts(T.PC[:, 0:128], T.KO[:], -2.0, 1.0, A.mult, A.add, r=["KO"], w=["PC0"], b=["C"])
+    tt(T.PC[:, 128:256], T.PC[:, 0:128], T.K1[:], A.add, r=["PC0", "K1"], w=["PC1"], b=["C"])
+    tt(T.PD[:, 0:128], T.PC[:, 128:256], T.K0[:], A.add, r=["PC1", "K0"], w=["PD0"], b=["C", "D"])
+    tt(T.PD[:, 128:256], T.PC[:, 128:256], T.K0[:], A.subtract, r=["PC1", "K0"], w=["PD1"], b=["C", "D"])
+    ts(T.HI[:], T.PD[:, 0:256], B64, B64, A.add, A.subtract, r=["PD0", "PD1"], w=["HI"], b=["D"])
+    tt(T.LO[:], T.PD[:, 0:256], T.HI[:], A.subtract, r=["PD0", "PD1", "HI"], w=["LO"], b=["D"])
+    cp(T.BF[:], T.BI[:], r=["BI"], w=["BF"])
+    cp(T.FB[0:8, :], T.FI[0:8, :], r=["FI"], w=["FB"])
+    act(T.FT[:, 1:2048:2], T.FA[:, 0:1024], -1.0, 255.0, r=["FA0"], w=["FTs1"])
+    cp(T.FT[:, 0:2048:2], T.FA[:, 0:1024], r=["FA0"], w=["FTs0"])
+    dma("s", T.FT[:, 4096:6144], T.FT[:, 0:2048], r=["FTs0", "FTs1"], w=["FTd0", "FTd1", "FTd2"])
+    act(T.FT[:, 2049:4096:2], T.FA[:, 1024:2048], -1.0, 255.0, r=["FA1"], w=["FTs3"])
+
+    def digit(dd, w):
+        src = T.HI if dd % 2 == 0 else T.LO
+        return src[:, w * (dd // 2):w * (dd // 2) + w], ["HI" if dd % 2 == 0 else "LO"]
+
+    for b in range(4):
+        terms = []
+        for dd in (0, 2, 1, 3):
+            s0 = 4 * (12 - 4 * dd) + b
+            rh, rr = digit(dd, 128)
+            terms.append((T.WD[:, s0:s0 + 509:4], rh, rr + ["WD"]))
+        mm(T.PF[:, 128 * b:128 * b + 128], terms, ["PF%d" % b], ["F"])
+    for e in range(2):
+        mm(T.PB[:, 64 * e:64 * e + 64],
+           [(T.RT[:, 128 * (2 * h + e):128 * (2 * h + e) + 128], T.BF[:, h::2], ["BF", "RT%d" % (2 * h + e)]) for h in range(2)],
+           ["PB%d" % e], ["B"])
+    mm(T.PA[:, 0:64], [(T.FF[0:8, 12 - 4 * q:140 - 4 * q], T.FB[0:8, q::4], ["FF", "FB"]) for q in range(4)], ["PA0"], ["A"])
+    act(T.YS[:], T.PF[:], r=["PF0", "PF1", "PF2", "PF3"], w=["YS"], b=["F"])
+    act(T.AB[:], T.PB[:, 0:128], r=["PB0", "PB1"], w=["AB"], b=["B"])
+    aa, bb = T.AB[:, 0:64], T.AB[:, 64:128]
+    mm(T.PE[:, 0:128:2], [(T.I32[:], bb, ["I32", "AB"]), (T.N32[:], aa, ["N32"])], ["PE0"], ["E"])
+    mm(T.PE[:, 1:128:2], [(T.I32[:], aa, [])], ["PE1"], ["E"])
+    mm(T.PE[:, 128:256:2], [(T.UP[:], aa, ["UP"]), (T.N32[:], bb, [])], ["PE2"], ["E"])
+    mm(T.PE[:, 129:256:2], [(T.I32[:], bb, [])], ["PE3"], ["E"])
+    cp(T.FT[:, 2048:4096:2], T.FA[:, 1024:2048], r=["FA1"], w=["FTs2"])
+    cp(T.D2[:, 1::2], T.PA[:, 0:64], r=["PA0", "D2z"], w=["D2"], b=["A"])
+    cp(T.MI0[:, 128:192], T.PA[:, 0:64], r=["PA0"], w=["MI0f"], b=["A"])
+
+    def expand(q, out, src, j, t, r, w):
+        m = T.MK[:, 4 * t + j:4 * t + j + 1]
+        if q == "v":
+            ts(out, src, m, None, A.mult, r=r + ["MKe", "MKo"], w=w)
+        else:
+            act(out, src, m, r=r + ["MKe", "MKo"], w=w)
+
+    kts = ["KTs%d" % k for k in range(8)]
+    ktd = ["KTd%d" % k for k in range(8)]
+    for k in range(8):
+        a, t = k // 2, k % 2
+        if k == 3:
+            scan(T.SE[:, 0:128], T.D2[:], T.PE[:, 0:128], r=["D2", "PE0", "PE1"], w=["SE"], b=["E"])
+            scan(T.SE[:, 128:256], T.D2[:], T.PE[:, 128:256], r=["D2", "PE2", "PE3"], w=["SE2"], b=["E"])
+            ts(T.TM[:, 0:64], T.SE[:, 1:128:2], 4096.0, -4096.0, A.is_ge, A.mult, r=["SE"], w=["TM"])
+            cp(T.MI0[:, 0:128], T.SE[:, 1::2], r=["SE", "SE2"], w=["MI0e", "MI0w"])
+            tt(T.TM[:, 64:128], T.TM[:, 0:64], T.SE[:, 1:128:2], A.add, r=["SE", "TM"], w=["TM2"])
+            cp(T.E0[:], T.TM[:, 64:128], r=["TM2"], w=["E0"])
+        expand("a" if k >= 4 else "v", T.KT[:, 1024 * a + t:1024 * a + 1024:2], T.YS[:], a, t, ["YS"], [kts[k]])
+
+    for q in range(4):
+        point(T.W2[:, 144 * q:144 * q + 144], T.ZB[:, 0:144], [[-16, 9], [-1000, 4], [-1, 4]], 3000 - 4 * q, 1.0, ["W2%d" % q])
+    for q in range(4):
+        point(T.RP[:, 128 * q:128 * q + 128], T.ZB[:, 0:128], [[-16, 8], [0, 4], [-1, 4]], -4 * q, -1.0, ["RP%d" % q])
+
+    ybuf = [T.Y0, T.Y1]
+    for t in range(RO):
+        last = t == RO - 1
+        MI = T["MI%d" % t]
+        e_, w_, f_ = "MI%de" % t, "MI%dw" % t, "MI%df" % t
+        yo, yn = ybuf[t % 2], ybuf[(t + 1) % 2]
+        yok, ynk = "Y%d" % (t % 2), "Y%d" % ((t + 1) % 2)
+        if t > 0:
+            add("g", None, w=[e_], kind="arr", sem="ae%d" % t, inc=n_in)
+            add("g", None, w=[w_, f_], kind="arr", sem="aw%d" % t, inc=n_in)
+        ft = ["FTs0", "FTs1", "FTs2", "FTs3", "FTd0", "FTd1", "FTd2"]
+        if t == 0:
+            kw, eo, kr = T.KT[:, 0:4096], T.E0, kts + ["E0"]
+        else:
+            kw, eo, kr = T.KT[:, 0:6144], MI, kts + ktd + [e_]
+        cp(T.GK[:, 0:512], kw.indirect(eo[:, 0:32]), r=kr, w=["GK0"])
+        act(T.GK[:, 512:1024], kw.indirect(eo[:, 32:64]), r=kr, w=["GK1"])
+        mm(T.PA[:, 0:64], [(T.BM[:, 15 - r:143 - r], T.GK[:, r::16], ["BM", "GK0", "GK1"]) for r in range(16)], ["PA0"], ["A"])
+        if t == 0:
+            act(T.Z1[:], T.B4[:], 0.5, r=["B4"], w=["Z1"])
+            sel(T.Z1[:], T.Z1[:], [[-1, 128]], A.not_equal, 1.5, 0, 1, ["Z1"], ["Z1"])
+            act(T.CC[:, 0::2], T.CI[:, 64:384], 1.0 / KS, col(R16), r=["CI", "R16"], w=["CC"])
+            act(T.CC[:, 1:128:2], T.CI[:, 0:64], 1.0 / KS, col(R16), r=["CI", "R16"], w=["LOC"])
+            act(T.MH[:], T.CC[:, 1:128:2], 2 * KS, 4095.5 - 2 * C0, r=["LOC"], w=["MH"])
+        for h in range(2):
+            act(T.FW[:, 512 * h:512 * h + 512], T.FT[:, 0:6144].indirect(MI[:, 64 + 32 * h:96 + 32 * h]), r=ft + [w_], w=["FW%d" % h])
+        if t > 0:
+            mm(T.PB[:, 64:128], [(T.O4[:], T.D0[:, 2::4], ["O4", "D0x"])], ["PBa"], ["B"])
+        mm(T.PB[:, 0:64], [(T.WA[:, 15 - r:143 - r], T.GK[:, r::16], ["WA", "GK0", "GK1"]) for r in range(16)], ["PB0"], ["B"])
+        ts(T.NL[:, 1::2], MI[:, 0:128], -1.0, 0.5, A.mult, A.add, r=[e_, w_], w=["NL1"])
+        ts(T.NL[:, 0::2], T.NL[:, 1::2], B2, B2, A.add, A.subtract, r=["NL1"], w=["NL0"])
+        scan(T.XX[:], T.M2[:], T.NL[:], r=["M2", "NL0", "NL1"], w=["XX"])
+        ts(T.UO[:], T.PA[:, 0:64], 0.5, None, A.mult, r=["PA0"], w=["UO"], b=["A"])
+        for h in range(2):
+            tt(T.DD[:, 512 * h:512 * h + 512], T.FT[:, 0:6144].indirect(T.UO[:, 32 * h:32 * h + 32]),
+               T.FW[:, 512 * h:512 * h + 512], A.subtract, r=ft + ["UO", "FW%d" % h], w=["DD%d" % h])
+        ts(T.NR[:], T.DD[:], B32, B32, A.add, A.is_equal, r=["DD0", "DD1"], w=["NR"])
+        act(T.UU[:, 0:64], T.PA[:, 0:64], 0.5, 0.5, r=["PA0"], w=["UU0"], b=["A"])
+        act(T.UU[:, 64:128], T.PA[:, 0:64], -0.5, 0.5, r=["PA0"], w=["UU1"], b=["A"])
+        act(T.AH[:], T.PB[:, 0:64], 0.5, -0.5, r=["PB0"], w=["AH"], b=["B"])
+        if t > 0:
+            act(T.CC[:, 128 * t + 1:128 * t + 128:2], T.TM[:, 1::2], r=["TM"], w=["LOC"])
+        if t > 0:
+            add("a", lambda: S.activation(T.TN[:, 0:64], T.PB[:, 64:128], AF.Copy, accum_out=col(RED)), ["PBa"], ["RED", "TN"], ["B"])
+        if t == 0:
+            act(T.VW[:, 0:1024], T.FA[:, 0:1024], 1.0, BIG, r=["FA0"], w=["VW0"])
+        if t == 1:
+            act(col(AL), col(ODD), -2.0, r=["ODD"], w=["AL"])
+            act(col(GA), col(ODD), 1.0, -0.5, r=["ODD"], w=["GA"])
+        if t == 2:
+            act(T.WO[:], T.BM[:], -0.5, r=["BM"], w=["WO"])
+            act(T.WO[:, 14::16], T.WA[:, 15::16], 0.5, r=["WA"], w=["WO"])
+        nE, nW = T.NL[:, 1:128:2], T.NL[:, 129:256:2]
+        xE, xW = T.XX[:, 1:128:2], T.XX[:, 129:256:2]
+        if last:
+            mm(T.PE[:, 0:256:4], [(T.ZB[:, 0:128], T.ZB[:, 0:64], [])], ["PE0"], ["E"])
+            mm(T.PG[:, 0:256:4], [(T.ZB[:, 0:128], T.ZB[:, 0:64], [])], ["PG0"], ["G"])
+        else:
+            mm(T.PE[:, 0:256:4], [(T.DI[:], xW, ["DI", "XX"])], ["PE0"], ["E"])
+        mm(T.PE[:, 1:256:4], [(T.I32[:], xE if last else xW, ["I32", "XX"]), (T.I32[:], nE, ["NL1"])], ["PE1"], ["E"])
+        if not last:
+            mm(T.PG[:, 0:256:4], [(T.IU[:], xE, ["IU", "XX"])], ["PG0"], ["G"])
+        mm(T.PG[:, 1:256:4], [(T.I32[:], xW, ["XX"]) if last else (T.UP[:], xE, ["UP", "XX"]), (T.I32[:], nW, ["NL1"])],
+           ["PG1"], ["G"])
+        if t == 0:
+            mm(T.PH[:, 1::2], [(T.WB[:, 3 - j:131 - j], T.KT[:, 2 * j:2048:8], ["WB"] + kts) for j in range(4)], ["PH1"], ["H"])
+            act(yo[:, 1::2], T.PH[:, 1::2], r=["PH1"], w=[yok + "o"], b=["H"])
+        else:
+            act(col(RND), col(RED), 1.0, B2, r=["RED"], w=["RND"])
+            act(col(RND), col(RND), -1.0, B2, r=["RND"], w=["RND"])
+            add("a", lambda: S.activation(col(PAR), col(RED), AF.Abs, bias=col(RND)), ["RED", "RND"], ["PAR"])
+        for h in range(2):
+            pb, bk = (T.PC, "C") if h == 0 else (T.PD, "D")
+            mm(pb[:], [(T.I2[:], T.FW[:, 512 * h:512 * h + 512], ["I2", "FW%d" % h]),
+                       (T.IB[:], T.DD[:, 512 * h:512 * h + 512], ["IB", "DD%d" % h])], ["S%d" % h], [bk])
+            c0 = 1024 * (t + 1) + 512 * h
+            act(T.VW[:, c0:c0 + 512], pb[:], 0.5 - 2.0 ** -10, BIG, r=["S%d" % h], w=["VW%d_%d" % (t + 1, h)], b=[bk])
+            if h == 0:
+                for hh in range(2):
+                    mm(T.PF[:, 64 * hh:64 * hh + 64],
+                       [(T.I32[:], xW, ["XX"]), (T.I32[:], T.UU[:, 64 * hh:64 * hh + 64], ["UU%d" % hh])], ["PF%d" % hh], ["F"])
+        mm(T.PA[:, 64:128], [(T.BM[:, 15 - r:143 - r], T.NR[:, r::16], ["NR"]) for r in range(16)], ["PA1"], ["A"])
+        ts(T.HI[:, 0:128], T.PF[:, 0:128], B64, B64, A.add, A.subtract, r=["PF0", "PF1"], w=["HI"], b=["F"])
+        cp(T.D0[:, 1::4], MI[:, 128:192], r=[f_], w=["D0f"])
+        tt(T.LO[:, 0:128], T.PF[:, 0:128], T.HI[:, 0:128], A.subtract, r=["PF0", "PF1", "HI"], w=["LO"], b=["F"])
+        if t == 0:
+            ts(T.SP[:], T.PA[:, 64:128], 9.0, None, A.is_ge, r=["PA1"], w=["SP"], b=["A"])
+        else:
+            if t < 3:
+                src, dst, out = (T.K0, T.K0F, T.y0) if t == 1 else (T.K1, T.K1F, T.y1)
+                cp(dst[:], src[:], r=["K%d" % (t - 1)], w=["KF%d" % t])
+                dma("s", out[:, 0:2048], dst[:], r=["KF%d" % t])
+            ts(T.SP[:], T.PA[:, 64:128], col(PAR), 9.0, A.subtract, A.is_ge, r=["PA1", "PAR"], w=["SP"], b=["A"])
+        mm(T.PA[:, 128:256:2], [(T.Z1[:], T.SP[:], ["Z1", "SP"])], ["PA2"], ["A"])
+        mm(T.PA[:, 129:256:2], [(T.Z1[:], T.SP[:], ["Z1", "SP"])], ["PA3"], ["A"])
+        mm(T.PB[:, 192:256], [(T.Z1[:], T.SP[:], ["Z1", "SP"])], ["PB3"], ["B"])
+        mm(T.PB[:, 128:192], [(T.B4[:], T.SP[:], ["B4", "SP"])], ["PB2"], ["B"])
+        if t == 0:
+            ts(T.D0[:, 3::4], T.PB[:, 192:256], 2.0, None, A.is_lt, r=["PB3", "PB2"], w=["D0g"], b=["B"])
+            ts(T.D0[:, 2::4], T.PB[:, 128:192], 2.0, None, A.is_lt, r=["PB2"], w=["D0x"], b=["B"])
+        else:
+            step(T.D0[:, 3::4], T.PB[:, 192:256], -1000.0, 1750.0, ["PB3", "PB2"], ["D0g"], ["B"])
+            step(T.D0[:, 2::4], T.PB[:, 128:192], -1000.0, 1500.0, ["PB2"], ["D0x"], ["B"])
+
+        def y_cands():
+            for q in range(4):
+                terms = [(T.NB[:], yo[:, 1 + 2 * q::8], ["NB", yok + "o"])]
+                for dd in range(4):
+                    rh, rr = digit(dd, 64)
+                    terms.append((T.W2[:, 144 * q + 12 - 4 * dd:144 * q + 140 - 4 * dd], rh, rr + ["W2%d" % q]))
+                mm(T.PF[:, 256 + q:512:4], terms, ["PY%d" % q], ["F"])
+            for q in range(4):
+                mm(T.PH[:, 1 + 2 * q::8], [(T.B4[:], T.Q4[:, 0:64], ["Q4"]),
+                                           (T.RP[:, 128 * q:128 * q + 128], T.D0[:, 3::4], ["RP%d" % q, "D0g"])], ["PH1"], ["H"])
+
+        def y_diff():
+            act(yo[:, 0::2], T.PF[:, 256:512], r=["PY0", "PY1", "PY2", "PY3"], w=[yok + "e"], b=["F"])
+
+        def y_scan():
+            scan(yn[:], T.PH[:], yo[:], r=["PH0", "PH1", yok + "e", yok + "o"], w=[ynk + "e", ynk + "o"], b=["H"])
+
+        if last:
+            y_cands()
+            y_diff()
+        mm(T.PE[:, 2:256:4], [(T.N32[:], nE, ["N32", "NL1"]), (T.N32[:], T.AH[:], ["AH"])], ["PE2"], ["E"])
+        mm(T.PE[:, 3:256:4], [(T.I32[:], T.AH[:], ["AH"])], ["PE3"], ["E"])
+        if t == 0:
+            mm(T.PG[:, 3:256:4], [(T.I32[:], T.MH[:], ["MH"])], ["PG3"], ["G"])
+        mm(T.PG[:, 2:256:4], [(T.N32[:], nW, ["NL1"]), (T.N32[:], T.MH[:], ["MH"])], ["PG2"], ["G"])
+        cc = T.CC[:, 128 * t:128 * t + 128]
+        add("v", lambda cc=cc: V.tensor_tensor_scan(T.TM[:], T.PA[:, 128:256], cc, 0.0, A.min, A.max),
+            ["PA2", "PA3", "CC", "LOC"], ["TM", "TM2"], ["A"])
+        ts(T.LC[:], T.TM[:, 1::2], KS, -float(C0), A.mult, A.add, r=["TM"], w=["LC"])
+        d0 = ["D0z", "D0f", "D0x", "D0g"]
+        if last:
+            tt(T.D2[:, 1::2], T.D0[:, 1::4], T.D0[:, 2::4], A.not_equal, r=d0, w=["D2"])
+            y_scan()
+            for j in range(4):
+                expand("v", T.GK[:, j::4], yn[:, 1::2], j, 0, [ynk + "o"], ["GX%d" % j] + ["GK0", "GK1"] * (j == 0))
+        scan(T.SE[:], T.D0[:], T.PE[:, 0:256], r=d0 + ["PE0", "PE1", "PE2", "PE3"], w=["SE", "SE2"], b=["E"])
+
+        def send(c0, c1, key, sem):
+            src, dst = T["MO%d" % (t + 1)][:, c0:c1], T["MI%d" % (t + 1)][:, c0:c1]
+            rs = T.sem[sem]
+            add("g", lambda: g.remote_dma(dst, src, rs, T.sem.sent, pid, rid, mask), r=[key], kind="rem", sem="sent", inc=n_out)
+
+        if not last:
+            ts(T["MO%d" % (t + 1)][:, 0:64], T.SE[:, 3::4], 0.5, None, A.add, r=["SE"], w=["MOe%d" % t])
+            send(0, 64, "MOe%d" % t, "ae%d" % (t + 1))
+            mm(T.PA[:, 256:320], [(T.IB[:], T.D0[:, 1::4], ["D0f"]), (T.IB[:], T.D0[:, 2::4], ["D0x"])], ["PA4"], ["A"])
+            y_cands()
+        vw = ["VW0"] + ["VW%d_%d" % (k + 1, h) for k in range(t + 1) for h in range(2)]
+        win = T.VW[:, 0:1024 * (t + 2)]
+        for h in range(2):
+            out = T.YX[:, 512 * h:512 * h + 512] if last else T.FT[:, 4096 + 1024 * h:5120 + 1024 * h:2]
+            act(out, win.indirect(T.LC[:, 32 * h:32 * h + 32]), 1.0, -BIG, r=vw + ["LC"], w=[("YX%d" if last else "FTd%d") % h])
+            if last:
+                dma("s", T.yx[:, 2048 + 512 * h:2560 + 512 * h], out, r=["YX%d" % h])
+            elif h == 0:
+                y_diff()
+        scan(T.SW[:, 0:256], T.D0[:], T.PG[:, 0:256], r=d0 + ["PG0", "PG1", "PG2", "PG3"], w=["SW"], b=["G"])
+        if not last:
+            ts(T["MO%d" % (t + 1)][:, 128:192], T.PA[:, 256:320], 1.0, None, A.is_equal, r=["PA4"], w=["MOf%d" % t], b=["A"])
+            ts(T["MO%d" % (t + 1)][:, 64:128], T.SW[:, 3:256:4], 0.5, None, A.add, r=["SW", "MOf%d" % t], w=["MOw%d" % t])
+            send(64, 192, "MOw%d" % t, "aw%d" % (t + 1))
+            y_scan()
+            for k in range(8):
+                if k == NV1:
+                    ts(T.FT[:, 4097::2], T.FT[:, 4096::2], -1.0, 255.0, A.mult, A.add, r=["FTd0", "FTd1"], w=["FTd2"])
+                expand("v" if k < NV else "a", T.KT[:, 4096 + k::8], yn[:, 1::2], k // 2, k % 2, [ynk + "o"], [ktd[k]])
+        if t == 0:
+            dma("s", T.yx[:, 0:2048], T.FA[:], r=["FA0", "FA1"])
+            sel(T.O4[:], T.ZB[:, 0:128], [[0, 128]], A.not_equal, 0.25, 0, 0, ["Z"], ["O4"])
+            sel(T.Q8[:], T.ZB[:, 0:128], [[0, 128]], A.not_equal, 0.125, 0, 0, ["Z"], ["Q8"])
+            point(T.FQ[:], T.ZB[:, 0:32], [[-4, 4], [-16, 8]], 0, 1.0, ["FQ"])
+        if t in (1, 2):
+            h = t - 1
+            p3, p2 = [[-16, 8], [-1, 8], [-1000, 2]], [[-16, 8], [-1, 8]]
+            m = [T.RR[:, 128 * (4 * h + k):128 * (4 * h + k) + 128] for k in range(4)]
+            c = [128 * (4 * h + k) for k in range(4)]
+            key = ["RR%d" % (4 * h + k) for k in range(4)]
+            for e in range(2):
+                sel(m[e], T.ZF[:], p3, A.not_equal, 1.0, 1000 * e - 8 * h, 1, ["ZF"], [key[e]])
+            sel(m[2], m[1], p3, A.not_equal, -1.0, -8 * h, 1, [key[1]], [key[2]])
+            sel(T.RR[:, c[3]:c[3] + 128:2], T.ZF[:, 0:64], p2, A.not_equal, 1.0, 1 - 8 * h, 1, ["ZF"], [key[3]])
+            sel(T.RR[:, c[3]:c[3] + 128:8], T.ZF[:, 0:16], [[-16, 8], [-4, 2]], A.not_equal, 1.0, -3 - 8 * h, 1, ["ZF"], [key[3]])
+            sel(T.RR[:, c[3] + 1:c[3] + 128:2], T.ZF[:, 0:64], p2, A.not_equal, -1.0, -8 * h, 1, ["ZF"], [key[3]])
+
+    eh, wh = T.SE[:, 3::4], T.SW[:, 3:256:4]
+    for q in range(4):
+        mm(T.PA[0:8, 256 + q:512:4], [(T.FQ[:, 8 * q:8 * q + 8], T.D2[:, 1::2], ["FQ", "D2"])], ["PAf%d" % q], ["A"])
+    gx = ["GX%d" % j for j in range(4)]
+    mm(T.PC[:, 0:128], [(T.B4[:], T.Q8[:], ["Q8"])]
+       + [(T.WO[:, 14 - 2 * ib:142 - 2 * ib], T.GK[:, 128 * ib:128 * ib + 128], ["WO"] + gx) for ib in range(8)], ["PC0"], ["C"])
+    tt(T.NL[:, 0:64], eh, T.D0[:, 1::4], A.mult, r=["SE", "D0f"], w=["NL0", "NL1"])
+    tt(T.NL[:, 64:128], wh, T.D0[:, 1::4], A.mult, r=["SW", "D0f"], w=["NL2"])
+    for h in range(2):
+        mm(T.PB[:, 256 + h:384:2],
+           [(T.RR[:, 128 * (4 * h + k):128 * (4 * h + k) + 128], rh, ["RR%d" % (4 * h + k), rk])
+            for k, (rh, rk) in enumerate([(eh, "SE"), (wh, "SW"), (T.NL[:, 0:64], "NL1"), (T.NL[:, 64:128], "NL2")])],
+           ["PBo%d" % h], ["B"])
+    act(T.FO[0:8, :], T.PA[0:8, 256:512], r=["PAf%d" % q for q in range(4)], w=["FO"], b=["A"])
+    dma("a", T.yf[:], T.FO[0:8, :], r=["FO"])
+    ts(T.TM[:], T.PC[:, 0:128], B2, B2, A.add, A.subtract, r=["PC0"], w=["TM", "TM2"], b=["C"])
+    ts(T.TN[:], T.TM[:], col(AL), col(GA), A.mult, A.add, r=["TM", "AL", "GA"], w=["TN"])
+    tt(T.OUT[:], T.PC[:, 0:128], T.TN[:], A.add, r=["PC0", "TN"], w=["OUT"], b=["C"])
+    dma("s", T.y0[:, 2048:3072], T.OUT[0::2, :], r=["OUT"])
+    dma("s", T.y1[:, 2048:3072], T.OUT[1::2, :], r=["OUT"])
+    act(T.OB[:], T.PB[:, 256:384], 1.0, 0.5, r=["PBo0", "PBo1"], w=["OB"], b=["B"])
+    dma("a", T.yb[:], T.OB[:], r=["OB"])
+    emit(g, T, ops)

@@ -14,8 +14,9 @@ SCRATCH = {
     "HI": ("sbuf", [128, 256], "bfloat16"), "LO": ("sbuf", [128, 256], "bfloat16"),
     "YS": ("sbuf", [128, 512], "bfloat16"), "Y0": ("sbuf", [128, 512], "bfloat16"), "Y1": ("sbuf", [128, 512], "bfloat16"),
     "D0": ("sbuf", [128, 256], "bfloat16"), "D2": ("sbuf", [128, 128], "bfloat16"),
-    "NL": ("sbuf", [128, 256], "float32"), "XX": ("sbuf", [128, 256], "float32"), "M2": ("sbuf", [128, 256], "bfloat16"),
-    "SE": ("sbuf", [128, 256], "float32"), "SW": ("sbuf", [128, 256], "float32"),
+    "D3": ("sbuf", [128, 64], "bfloat16"), "F0": ("sbuf", [128, 128], "bfloat16"),
+    "NL": ("sbuf", [128, 256], "float32"), "XX": ("sbuf", [128, 256], "float32"), "M2": ("sbuf", [128, 128], "bfloat16"),
+    "SE": ("sbuf", [128, 512], "float32"),
     "AH": ("sbuf", [128, 64], "float32"), "UU": ("sbuf", [128, 128], "float32"), "SP": ("sbuf", [128, 64], "bfloat16"),
     "UO": ("sbuf", [128, 64], "uint16"), "LC": ("sbuf", [128, 64], "uint16"), "E0": ("sbuf", [128, 64], "uint16"),
     "TM": ("sbuf", [128, 128], "float32"), "TN": ("sbuf", [128, 128], "float32"), "OUT": ("sbuf", [128, 128], "float32"),
@@ -24,7 +25,7 @@ SCRATCH = {
     "IK": ("sbuf", [128, 8], "int32"), "IJ": ("sbuf", [128, 8], "int32"), "MK": ("sbuf", [128, 8], "float32"),
     "COL": ("sbuf", [128, 16], "float32"),
     "ZF": ("sbuf", [128, 128], "float32"), "ZB": ("sbuf", [128, 576], "bfloat16"), "ONE": ("sbuf", [128, 144], "bfloat16"),
-    "Q4": ("sbuf", [128, 64], "bfloat16"), "Q8": ("sbuf", [128, 128], "bfloat16"), "O4": ("sbuf", [128, 128], "bfloat16"),
+    "Q4": ("sbuf", [128, 64], "bfloat16"), "Q9": ("sbuf", [128, 64], "bfloat16"), "Q8": ("sbuf", [128, 128], "bfloat16"), "O4": ("sbuf", [128, 128], "bfloat16"),
     "KM": ("sbuf", [128, 128], "float32"),
     "RT": ("sbuf", [128, 512], "float32"), "RR": ("sbuf", [128, 1024], "float32"),
     "I32": ("sbuf", [128, 128], "float32"), "N32": ("sbuf", [128, 128], "float32"), "UP": ("sbuf", [128, 128], "float32"),
@@ -41,7 +42,7 @@ for _t in range(1, RO):
     SCRATCH["MO%d" % _t] = ("sbuf", [128, 192], "uint16")
 for _b in "ABCDEFGH":
     SCRATCH["P" + _b] = ("psum", [128, 512], "float32")
-SEMAPHORES = (["sv", "sa", "sp", "sg", "sent"] + ["d%d" % _i for _i in range(16)]
+SEMAPHORES = (["sv", "sa", "sp", "sg", "sent", "af"] + ["d%d" % _i for _i in range(16)]
               + ["ae%d" % _t for _t in range(1, RO)] + ["aw%d" % _t for _t in range(1, RO)])
 
 BIG = 1.5 * 2 ** 23
@@ -50,6 +51,7 @@ B32 = 1.5 * 2 ** 28
 B64 = 1.5 * 2 ** 29
 KS, C0 = 16384.0, 24576
 NV, NV1 = 4, 3
+CUT = 24
 QSEM = {"v": "sv", "a": "sa", "p": "sp", "g": "sg"}
 
 
@@ -196,7 +198,7 @@ def rank_program(g, core, T, topo):
         sel(out, out, [[-s, c] for s, c in pat], A.is_ge, 0.0, width - 1 - base, -1, w, w)
 
     col = lambda j: T.COL[:, j:j + 1]
-    SG, R16, AL, GA, WP, PAR, RED, RND, ODD = 0, 1, 2, 3, 4, 5, 6, 7, 8
+    SG, R16, AL, GA, RM, PAR, RED, RND, ODD, THR = 0, 1, 2, 3, 4, 5, 6, 7, 8, 9
 
     dma("s", T.K1[:], T.kid1[:], w=["K1"])
     dma("s", T.K0[:], T.kid0[:], w=["K0"])
@@ -209,6 +211,7 @@ def rank_program(g, core, T, topo):
     ms(T.ONE[:], 1.0, ["ONE"])
     iota(T.IK[:, 0:5], [[-1, 5]], 4, 1, ["IK"], False)
     iota(T.KM[:], [[-1, 128]], 0, 1, ["KM"])
+    iota(T.CI[:], [[1024, 6], [16, 64]], C0, 0, ["CI"])
     point(T.WD[:], T.ZB[:], [[-16, 9], [-1000, 4], [-1, 16]], 3000, 1.0, ["WD"])
     band(T.BM[:], [[-16, 9], [1000, 16]], -15000, 16, ["BM"])
     iota(T.ZF[:], [[0, 128]], 0, 0, ["ZF"])
@@ -217,8 +220,7 @@ def rank_program(g, core, T, topo):
             1000 * (k // 2) - k % 2, 1, ["ZF"], ["RT%d" % k])
     point(T.FF[0:8, :], T.ZB[0:8, 0:144], [[-1, 9], [-1000, 4], [0, 4]], 3000, 1.0, ["FF"])
     iota(T.D2[:, 0::2], [[0, 64]], 0, 0, ["D2z"])
-    iota(T.M2[:], [[0, 128], [-2, 2]], 0, 0, ["M2"])
-    iota(T.CI[:], [[1024, 6], [16, 64]], C0, 0, ["CI"])
+    iota(T.M2[:], [[0, 64], [-2, 2]], 0, 0, ["M2"])
     band(T.B4[:], [[-4, 32], [0, 4]], 0, 4, ["B4"])
     band(T.WB[:], [[-4, 33], [1000, 4]], -3000, 4, ["WB"])
     iota(T.D0[:, 0::4], [[0, 64]], 0, 0, ["D0z"])
@@ -235,6 +237,7 @@ def rank_program(g, core, T, topo):
     ts(T.MK[:, 0:4], T.IJ[:, 0:4], 0.0, None, A.is_equal, r=["IJ0"], w=["MKe"])
     ts(col(SG), T.IJ[:, 4:5], -0.25, 1.0, A.mult, A.add, r=["IJ1"], w=["SG"])
     ts(col(R16), T.IJ[:, 5:6], 1.0 / KS, None, A.mult, r=["IJ2"], w=["R16"])
+    ts(col(RM), T.IJ[:, 5:6], 2.0, 4095.5 - 2 * C0, A.mult, A.add, r=["IJ2"], w=["RM"])
     tt(col(ODD), T.MK[:, 1:2], T.MK[:, 3:4], A.add, r=["MKe"], w=["ODD"])
     ts(T.MK[:, 4:8], T.MK[:, 0:4], col(SG), None, A.mult, r=["MKe", "SG"], w=["MKo"])
     act(T.N32[:], T.I32[:], -1.0, r=["I32"], w=["N32"])
@@ -244,22 +247,28 @@ def rank_program(g, core, T, topo):
     mm(T.PG[:, 0:128], [(T.I32[:], T.DN[:], ["I32", "DN"]), (T.I32[:], T.N32[:], ["N32"])], ["PG0"], ["G"])
     mm(T.PG[:, 128:256], [(T.N32[:], T.UP[:], ["UP"]), (T.I32[:], T.I32[:], [])], ["PG1"], ["G"])
     mm(T.PH[:, 0::2], [(T.ZB[:, 0:128], T.ZB[:, 0:256], ["Z"])], ["PH0"], ["H"])
+    act(T.CC[:, 0::2], T.CI[:, 64:384], 1.0 / KS, col(R16), r=["CI", "R16"], w=["CC"])
+    act(T.CC[:, 1:128:2], T.CI[:, 0:64], 1.0 / KS, col(R16), r=["CI", "R16"], w=["LOC"])
+    act(T.MH[:], T.CI[:, 0:64], 2.0, col(RM), r=["CI", "RM"], w=["MH"])
     act(T.DI[:], T.PG[:, 0:128], r=["PG0"], w=["DI"], b=["G"])
     act(T.IU[:], T.PG[:, 128:256], r=["PG1"], w=["IU"], b=["G"])
-    act(T.WA[:], T.BM[:], col(SG), r=["BM", "SG"], w=["WA"])
+    act(col(AL), col(ODD), -2.0, r=["ODD"], w=["AL"])
+    act(col(GA), col(ODD), 1.0, -0.5, r=["ODD"], w=["GA"])
 
     ts(T.KO[:], T.K1[:], 1, None, A.bitwise_and, r=["K1"], w=["KO"])
     ts(T.PC[:, 0:128], T.KO[:], -2.0, 1.0, A.mult, A.add, r=["KO"], w=["PC0"], b=["C"])
     tt(T.PC[:, 128:256], T.PC[:, 0:128], T.K1[:], A.add, r=["PC0", "K1"], w=["PC1"], b=["C"])
+    cp(T.BF[:], T.BI[:], r=["BI"], w=["BF"])
     tt(T.PD[:, 0:128], T.PC[:, 128:256], T.K0[:], A.add, r=["PC1", "K0"], w=["PD0"], b=["C", "D"])
     tt(T.PD[:, 128:256], T.PC[:, 128:256], T.K0[:], A.subtract, r=["PC1", "K0"], w=["PD1"], b=["C", "D"])
-    ts(T.HI[:], T.PD[:, 0:256], B64, B64, A.add, A.subtract, r=["PD0", "PD1"], w=["HI"], b=["D"])
-    tt(T.LO[:], T.PD[:, 0:256], T.HI[:], A.subtract, r=["PD0", "PD1", "HI"], w=["LO"], b=["D"])
-    cp(T.BF[:], T.BI[:], r=["BI"], w=["BF"])
-    cp(T.FB[0:8, :], T.FI[0:8, :], r=["FI"], w=["FB"])
+    ts(T.HI[:, 0:128], T.PD[:, 0:128], B64, B64, A.add, A.subtract, r=["PD0"], w=["HIa"], b=["D"])
+    ts(T.HI[:, 128:256], T.PD[:, 128:256], B64, B64, A.add, A.subtract, r=["PD1"], w=["HI"], b=["D"])
+    tt(T.LO[:, 0:128], T.PD[:, 0:128], T.HI[:, 0:128], A.subtract, r=["PD0", "HIa"], w=["LOa"], b=["D"])
+    tt(T.LO[:, 128:256], T.PD[:, 128:256], T.HI[:, 128:256], A.subtract, r=["PD1", "HI", "LOa"], w=["LO"], b=["D"])
     act(T.FT[:, 1:2048:2], T.FA[:, 0:1024], -1.0, 255.0, r=["FA0"], w=["FTs1"])
     cp(T.FT[:, 0:2048:2], T.FA[:, 0:1024], r=["FA0"], w=["FTs0"])
-    dma("s", T.FT[:, 4096:6144], T.FT[:, 0:2048], r=["FTs0", "FTs1"], w=["FTd0", "FTd1", "FTd2"])
+    cp(T.FB[0:8, :], T.FI[0:8, :], r=["FI"], w=["FB"])
+    dma("s", T.FT[:, 4096:6144], T.FT[:, 0:2048], r=["FTs0", "FTs1"], w=["FTd0", "FTd1", "FTd2", "FTd3", "FTd4"])
     act(T.FT[:, 2049:4096:2], T.FA[:, 1024:2048], -1.0, 255.0, r=["FA1"], w=["FTs3"])
 
     def digit(dd, w):
@@ -286,8 +295,10 @@ def rank_program(g, core, T, topo):
     mm(T.PE[:, 128:256:2], [(T.UP[:], aa, ["UP"]), (T.N32[:], bb, [])], ["PE2"], ["E"])
     mm(T.PE[:, 129:256:2], [(T.I32[:], bb, [])], ["PE3"], ["E"])
     cp(T.FT[:, 2048:4096:2], T.FA[:, 1024:2048], r=["FA1"], w=["FTs2"])
-    cp(T.D2[:, 1::2], T.PA[:, 0:64], r=["PA0", "D2z"], w=["D2"], b=["A"])
-    cp(T.MI0[:, 128:192], T.PA[:, 0:64], r=["PA0"], w=["MI0f"], b=["A"])
+    ts(T.WA[:], T.BM[:], col(SG), None, A.mult, r=["BM", "SG"], w=["WA"])
+    cp(T.K0F[:], T.K0[:], r=["K0"], w=["KF0"])
+
+    mm(T.PG[:, 3:256:4], [(T.I32[:], T.MH[:], ["MH"])], ["PG3", "PG0", "PG1"], ["G"])
 
     def expand(q, out, src, j, t, r, w):
         m = T.MK[:, 4 * t + j:4 * t + j + 1]
@@ -297,17 +308,20 @@ def rank_program(g, core, T, topo):
             act(out, src, m, r=r + ["MKe", "MKo"], w=w)
 
     kts = ["KTs%d" % k for k in range(8)]
-    ktd = ["KTd%d" % k for k in range(8)]
+    ktd = ["KTd%d" % k for k in range(9)]
     for k in range(8):
         a, t = k // 2, k % 2
+        if k == 2:
+            cp(T.D2[:, 1::2], T.PA[:, 0:64], r=["PA0", "D2z"], w=["D2"], b=["A"])
+            cp(T.MI0[:, 128:192], T.PA[:, 0:64], r=["PA0"], w=["MI0f"], b=["A"])
         if k == 3:
             scan(T.SE[:, 0:128], T.D2[:], T.PE[:, 0:128], r=["D2", "PE0", "PE1"], w=["SE"], b=["E"])
             scan(T.SE[:, 128:256], T.D2[:], T.PE[:, 128:256], r=["D2", "PE2", "PE3"], w=["SE2"], b=["E"])
             ts(T.TM[:, 0:64], T.SE[:, 1:128:2], 4096.0, -4096.0, A.is_ge, A.mult, r=["SE"], w=["TM"])
-            cp(T.MI0[:, 0:128], T.SE[:, 1::2], r=["SE", "SE2"], w=["MI0e", "MI0w"])
+            cp(T.MI0[:, 0:128], T.SE[:, 1:256:2], r=["SE", "SE2"], w=["MI0e", "MI0w"])
             tt(T.TM[:, 64:128], T.TM[:, 0:64], T.SE[:, 1:128:2], A.add, r=["SE", "TM"], w=["TM2"])
-            cp(T.E0[:], T.TM[:, 64:128], r=["TM2"], w=["E0"])
         expand("a" if k >= 4 else "v", T.KT[:, 1024 * a + t:1024 * a + 1024:2], T.YS[:], a, t, ["YS"], [kts[k]])
+    cp(T.E0[:], T.TM[:, 64:128], r=["TM2"], w=["E0"])
 
     for q in range(4):
         point(T.W2[:, 144 * q:144 * q + 144], T.ZB[:, 0:144], [[-16, 9], [-1000, 4], [-1, 4]], 3000 - 4 * q, 1.0, ["W2%d" % q])
@@ -324,20 +338,16 @@ def rank_program(g, core, T, topo):
         if t > 0:
             add("g", None, w=[e_], kind="arr", sem="ae%d" % t, inc=n_in)
             add("g", None, w=[w_, f_], kind="arr", sem="aw%d" % t, inc=n_in)
-        ft = ["FTs0", "FTs1", "FTs2", "FTs3", "FTd0", "FTd1", "FTd2"]
+        ft = ["FTs0", "FTs1", "FTs2", "FTs3", "FTd0", "FTd1", "FTd2", "FTd3", "FTd4"]
         if t == 0:
             kw, eo, kr = T.KT[:, 0:4096], T.E0, kts + ["E0"]
         else:
             kw, eo, kr = T.KT[:, 0:6144], MI, kts + ktd + [e_]
+        if t == 0:
+            mm(T.PH[:, 1::2], [(T.WB[:, 3 - j:131 - j], T.KT[:, 2 * j:2048:8], ["WB"] + kts) for j in range(4)], ["PH1"], ["H"])
         cp(T.GK[:, 0:512], kw.indirect(eo[:, 0:32]), r=kr, w=["GK0"])
         act(T.GK[:, 512:1024], kw.indirect(eo[:, 32:64]), r=kr, w=["GK1"])
         mm(T.PA[:, 0:64], [(T.BM[:, 15 - r:143 - r], T.GK[:, r::16], ["BM", "GK0", "GK1"]) for r in range(16)], ["PA0"], ["A"])
-        if t == 0:
-            act(T.Z1[:], T.B4[:], 0.5, r=["B4"], w=["Z1"])
-            sel(T.Z1[:], T.Z1[:], [[-1, 128]], A.not_equal, 1.5, 0, 1, ["Z1"], ["Z1"])
-            act(T.CC[:, 0::2], T.CI[:, 64:384], 1.0 / KS, col(R16), r=["CI", "R16"], w=["CC"])
-            act(T.CC[:, 1:128:2], T.CI[:, 0:64], 1.0 / KS, col(R16), r=["CI", "R16"], w=["LOC"])
-            act(T.MH[:], T.CC[:, 1:128:2], 2 * KS, 4095.5 - 2 * C0, r=["LOC"], w=["MH"])
         for h in range(2):
             act(T.FW[:, 512 * h:512 * h + 512], T.FT[:, 0:6144].indirect(MI[:, 64 + 32 * h:96 + 32 * h]), r=ft + [w_], w=["FW%d" % h])
         if t > 0:
@@ -345,12 +355,13 @@ def rank_program(g, core, T, topo):
         mm(T.PB[:, 0:64], [(T.WA[:, 15 - r:143 - r], T.GK[:, r::16], ["WA", "GK0", "GK1"]) for r in range(16)], ["PB0"], ["B"])
         ts(T.NL[:, 1::2], MI[:, 0:128], -1.0, 0.5, A.mult, A.add, r=[e_, w_], w=["NL1"])
         ts(T.NL[:, 0::2], T.NL[:, 1::2], B2, B2, A.add, A.subtract, r=["NL1"], w=["NL0"])
-        scan(T.XX[:], T.M2[:], T.NL[:], r=["M2", "NL0", "NL1"], w=["XX"])
+        scan(T.XX[:, 128:256], T.M2[:], T.NL[:, 128:256], r=["M2", "NL0", "NL1"], w=["XW"])
         ts(T.UO[:], T.PA[:, 0:64], 0.5, None, A.mult, r=["PA0"], w=["UO"], b=["A"])
         for h in range(2):
             tt(T.DD[:, 512 * h:512 * h + 512], T.FT[:, 0:6144].indirect(T.UO[:, 32 * h:32 * h + 32]),
                T.FW[:, 512 * h:512 * h + 512], A.subtract, r=ft + ["UO", "FW%d" % h], w=["DD%d" % h])
-        ts(T.NR[:], T.DD[:], B32, B32, A.add, A.is_equal, r=["DD0", "DD1"], w=["NR"])
+        for h, (c0, c1) in enumerate([(0, 512), (512, 1024)]):
+            ts(T.NR[:, c0:c1], T.DD[:, c0:c1], B32, B32, A.add, A.is_equal, r=["DD%d" % h], w=["NR%d" % h])
         act(T.UU[:, 0:64], T.PA[:, 0:64], 0.5, 0.5, r=["PA0"], w=["UU0"], b=["A"])
         act(T.UU[:, 64:128], T.PA[:, 0:64], -0.5, 0.5, r=["PA0"], w=["UU1"], b=["A"])
         act(T.AH[:], T.PB[:, 0:64], 0.5, -0.5, r=["PB0"], w=["AH"], b=["B"])
@@ -359,60 +370,87 @@ def rank_program(g, core, T, topo):
         if t > 0:
             add("a", lambda: S.activation(T.TN[:, 0:64], T.PB[:, 64:128], AF.Copy, accum_out=col(RED)), ["PBa"], ["RED", "TN"], ["B"])
         if t == 0:
+            act(T.Z1[:], T.B4[:], 0.5, r=["B4"], w=["Z1"])
+            sel(T.Z1[:], T.Z1[:], [[-1, 128]], A.not_equal, 1.5, 0, 1, ["Z1"], ["Z1"])
+            add("g", lambda: g.remote_dma(T.F0[:], T.D2[:], T.sem.af, T.sem.sent, pid, rid, mask), r=["D2", "D2z"],
+                kind="rem", sem="sent", inc=n_out)
             act(T.VW[:, 0:1024], T.FA[:, 0:1024], 1.0, BIG, r=["FA0"], w=["VW0"])
-        if t == 1:
-            act(col(AL), col(ODD), -2.0, r=["ODD"], w=["AL"])
-            act(col(GA), col(ODD), 1.0, -0.5, r=["ODD"], w=["GA"])
-        if t == 2:
-            act(T.WO[:], T.BM[:], -0.5, r=["BM"], w=["WO"])
-            act(T.WO[:, 14::16], T.WA[:, 15::16], 0.5, r=["WA"], w=["WO"])
         nE, nW = T.NL[:, 1:128:2], T.NL[:, 129:256:2]
         xE, xW = T.XX[:, 1:128:2], T.XX[:, 129:256:2]
         if last:
             mm(T.PE[:, 0:256:4], [(T.ZB[:, 0:128], T.ZB[:, 0:64], [])], ["PE0"], ["E"])
             mm(T.PG[:, 0:256:4], [(T.ZB[:, 0:128], T.ZB[:, 0:64], [])], ["PG0"], ["G"])
         else:
-            mm(T.PE[:, 0:256:4], [(T.DI[:], xW, ["DI", "XX"])], ["PE0"], ["E"])
-        mm(T.PE[:, 1:256:4], [(T.I32[:], xE if last else xW, ["I32", "XX"]), (T.I32[:], nE, ["NL1"])], ["PE1"], ["E"])
-        if not last:
-            mm(T.PG[:, 0:256:4], [(T.IU[:], xE, ["IU", "XX"])], ["PG0"], ["G"])
-        mm(T.PG[:, 1:256:4], [(T.I32[:], xW, ["XX"]) if last else (T.UP[:], xE, ["UP", "XX"]), (T.I32[:], nW, ["NL1"])],
-           ["PG1"], ["G"])
-        if t == 0:
-            mm(T.PH[:, 1::2], [(T.WB[:, 3 - j:131 - j], T.KT[:, 2 * j:2048:8], ["WB"] + kts) for j in range(4)], ["PH1"], ["H"])
-            act(yo[:, 1::2], T.PH[:, 1::2], r=["PH1"], w=[yok + "o"], b=["H"])
+            mm(T.PE[:, 0:256:4], [(T.DI[:], xW, ["DI", "XW"])], ["PE0"], ["E"])
+        if last:
+            mm(T.PG[:, 1:256:4], [(T.I32[:], xW, ["XW"]), (T.I32[:], nW, ["NL1"])], ["PG1"], ["G"])
         else:
-            act(col(RND), col(RED), 1.0, B2, r=["RED"], w=["RND"])
-            act(col(RND), col(RND), -1.0, B2, r=["RND"], w=["RND"])
-            add("a", lambda: S.activation(col(PAR), col(RED), AF.Abs, bias=col(RND)), ["RED", "RND"], ["PAR"])
-        for h in range(2):
+            mm(T.PE[:, 1:256:4], [(T.I32[:], xW, ["I32", "XW"]), (T.I32[:], nE, ["NL1"])], ["PE1"], ["E"])
+        mm(T.PG[:, 2:256:4], [(T.N32[:], nW, ["NL1"]), (T.N32[:], T.MH[:], ["MH"])], ["PG2"], ["G"])
+        if t == 0:
+            act(yo[:, 1::2], T.PH[:, 1::2], r=["PH1"], w=[yok + "o"], b=["H"])
+
+        def half_sum(h, first):
             pb, bk = (T.PC, "C") if h == 0 else (T.PD, "D")
-            mm(pb[:], [(T.I2[:], T.FW[:, 512 * h:512 * h + 512], ["I2", "FW%d" % h]),
-                       (T.IB[:], T.DD[:, 512 * h:512 * h + 512], ["IB", "DD%d" % h])], ["S%d" % h], [bk])
-            c0 = 1024 * (t + 1) + 512 * h
-            act(T.VW[:, c0:c0 + 512], pb[:], 0.5 - 2.0 ** -10, BIG, r=["S%d" % h], w=["VW%d_%d" % (t + 1, h)], b=[bk])
-            if h == 0:
-                for hh in range(2):
-                    mm(T.PF[:, 64 * hh:64 * hh + 64],
-                       [(T.I32[:], xW, ["XX"]), (T.I32[:], T.UU[:, 64 * hh:64 * hh + 64], ["UU%d" % hh])], ["PF%d" % hh], ["F"])
-        mm(T.PA[:, 64:128], [(T.BM[:, 15 - r:143 - r], T.NR[:, r::16], ["NR"]) for r in range(16)], ["PA1"], ["A"])
-        ts(T.HI[:, 0:128], T.PF[:, 0:128], B64, B64, A.add, A.subtract, r=["PF0", "PF1"], w=["HI"], b=["F"])
-        cp(T.D0[:, 1::4], MI[:, 128:192], r=[f_], w=["D0f"])
-        tt(T.LO[:, 0:128], T.PF[:, 0:128], T.HI[:, 0:128], A.subtract, r=["PF0", "PF1", "HI"], w=["LO"], b=["F"])
+            lh, src, k = (T.I2, T.FW, "FW%d" % h) if first else (T.IB, T.DD, "DD%d" % h)
+            rh = src[:, 512 * h:512 * h + 512]
+            add("p", lambda: PE.matmul(pb[:], lh[:], rh, first, not first), ["I2", "IB", k], ["S%d" % h], [bk])
+            if not first:
+                c0 = 1024 * (t + 1) + 512 * h
+                act(T.VW[:, c0:c0 + 512], pb[:], 0.5 - 2.0 ** -10, BIG, r=["S%d" % h], w=["VW%d_%d" % (t + 1, h)], b=[bk])
+
+        half_sum(0, True)
+        half_sum(0, False)
+        act(T.PE[:, 3:256:4], T.AH[:], r=["AH"], w=["PE3"], b=["E"])
+        for hh in range(2):
+            mm(T.PF[:, 64 * hh:64 * hh + 64],
+               [(T.I32[:], xW, ["XW"]), (T.I32[:], T.UU[:, 64 * hh:64 * hh + 64], ["UU%d" % hh])], ["PF%d" % hh], ["F"])
+        half_sum(1, True)
+        half_sum(1, False)
+        mm(T.PA[:, 64:128], [(T.B4[:], T.Q9[:], ["Q9"])] * (t > 0)
+           + [(T.BM[:, 15 - r:143 - r], T.NR[:, r::16], ["NR0", "NR1"]) for r in range(16)], ["PA1"], ["A"])
+        if t > 0:
+            ts(col(RND), col(RED), B2, B2, A.add, A.subtract, r=["RED"], w=["RND"])
+        scan(T.XX[:, 0:128], T.M2[:], T.NL[:, 0:128], r=["M2", "NL0", "NL1"], w=["XE"])
+        if t > 0:
+            ts(col(THR), col(RED), col(RND), 1000.0, A.is_equal, A.mult, r=["RED", "RND"], w=["THR"])
+        ts(T.HI[:, 0:128], T.PF[:, 0:128], B64, B64, A.add, A.subtract, r=["PF0", "PF1"], w=["HI", "HIa"], b=["F"])
+        if t == 1:
+            cp(T.D3[:], MI[:, 128:192], r=[f_], w=["D3"])
+        else:
+            cp(T.D0[:, 1::4], MI[:, 128:192], r=[f_], w=["D0f"])
         if t == 0:
             ts(T.SP[:], T.PA[:, 64:128], 9.0, None, A.is_ge, r=["PA1"], w=["SP"], b=["A"])
-        else:
-            if t < 3:
-                src, dst, out = (T.K0, T.K0F, T.y0) if t == 1 else (T.K1, T.K1F, T.y1)
-                cp(dst[:], src[:], r=["K%d" % (t - 1)], w=["KF%d" % t])
-                dma("s", out[:, 0:2048], dst[:], r=["KF%d" % t])
-            ts(T.SP[:], T.PA[:, 64:128], col(PAR), 9.0, A.subtract, A.is_ge, r=["PA1", "PAR"], w=["SP"], b=["A"])
-        mm(T.PA[:, 128:256:2], [(T.Z1[:], T.SP[:], ["Z1", "SP"])], ["PA2"], ["A"])
-        mm(T.PA[:, 129:256:2], [(T.Z1[:], T.SP[:], ["Z1", "SP"])], ["PA3"], ["A"])
-        mm(T.PB[:, 192:256], [(T.Z1[:], T.SP[:], ["Z1", "SP"])], ["PB3"], ["B"])
-        mm(T.PB[:, 128:192], [(T.B4[:], T.SP[:], ["B4", "SP"])], ["PB2"], ["B"])
+        tt(T.LO[:, 0:128], T.PF[:, 0:128], T.HI[:, 0:128], A.subtract, r=["PF0", "PF1", "HI"], w=["LO", "LOa"], b=["F"])
+        if t == 1:
+            add("g", None, w=["F0"], kind="arr", sem="af", inc=n_in)
+            tt(T.D0[:, 1::4], T.F0[:, 1::2], T.D3[:], A.not_equal, r=["F0", "D3"], w=["D0f"])
         if t == 0:
-            ts(T.D0[:, 3::4], T.PB[:, 192:256], 2.0, None, A.is_lt, r=["PB3", "PB2"], w=["D0g"], b=["B"])
+            cp(T.K1F[:], T.K1[:], r=["K1"], w=["KF1"])
+            dma("s", T.y0[:, 0:2048], T.K0F[:], r=["KF0", "KF1"])
+            dma("s", T.y1[:, 0:2048], T.K1F[:], r=["KF1"])
+        else:
+            step(T.SP[:], T.PA[:, 64:128], 1000.0, col(THR), ["PA1", "THR"], ["SP"], ["A"])
+        if last:
+            mm(T.PE[:, 1:256:4], [(T.I32[:], xE, ["I32", "XE"]), (T.I32[:], nE, ["NL1"])], ["PE1"], ["E"])
+        else:
+            mm(T.PG[:, 1:256:4], [(T.UP[:], xE, ["UP", "XE"]), (T.I32[:], nW, ["NL1"])], ["PG1"], ["G"])
+        if t == 0:
+            mm(T.PA[:, 128:256:2], [(T.Z1[:], T.SP[:], ["Z1", "SP"])], ["PA2"], ["A"])
+        mm(T.PA[:, 129:256:2], [(T.Z1[:], T.SP[:], ["Z1", "SP"])], ["PA3"], ["A"])
+        mm(T.PB[:, 128:192], [(T.B4[:], T.SP[:], ["B4", "SP"])], ["PB2"], ["B"])
+        if t > 0:
+            mm(T.PB[:, 192:256], [(T.Z1[:], T.SP[:], ["Z1", "SP"])], ["PB3"], ["B"])
+        mm(T.PE[:, 2:256:4], [(T.N32[:], nE, ["N32", "NL1"]), (T.N32[:], T.AH[:], ["AH"])], ["PE2"], ["E"])
+        if not last:
+            mm(T.PG[:, 0:256:4], [(T.IU[:], xE, ["IU", "XE"])], ["PG0"], ["G"])
+        cc = T.CC[:, 128 * t:128 * t + 128]
+        add("v", lambda cc=cc: V.tensor_tensor_scan(T.TM[:], T.PA[:, 128:256], cc, 0.0, A.min, A.max),
+            ["PA2", "PA3", "CC", "LOC"], ["TM", "TM2"], ["A"])
+        if t == 0:
+            ts(T.D0[:, 3::4], T.PA[:, 129:256:2], 2.0, None, A.is_lt, r=["PA3"], w=["D0g"], b=["A"])
+        ts(T.LC[:], T.TM[:, 1::2], KS, -float(C0), A.mult, A.add, r=["TM"], w=["LC"])
+        if t == 0:
             ts(T.D0[:, 2::4], T.PB[:, 128:192], 2.0, None, A.is_lt, r=["PB2"], w=["D0x"], b=["B"])
         else:
             step(T.D0[:, 3::4], T.PB[:, 192:256], -1000.0, 1750.0, ["PB3", "PB2"], ["D0g"], ["B"])
@@ -425,6 +463,8 @@ def rank_program(g, core, T, topo):
                     rh, rr = digit(dd, 64)
                     terms.append((T.W2[:, 144 * q + 12 - 4 * dd:144 * q + 140 - 4 * dd], rh, rr + ["W2%d" % q]))
                 mm(T.PF[:, 256 + q:512:4], terms, ["PY%d" % q], ["F"])
+            if 0 < t < RO - 1:
+                mm(T.PA[:, 256:320], [(T.IB[:], T.D0[:, 1::4], ["D0f"]), (T.IB[:], T.D0[:, 2::4], ["D0x"])], ["PA4"], ["A"])
             for q in range(4):
                 mm(T.PH[:, 1 + 2 * q::8], [(T.B4[:], T.Q4[:, 0:64], ["Q4"]),
                                            (T.RP[:, 128 * q:128 * q + 128], T.D0[:, 3::4], ["RP%d" % q, "D0g"])], ["PH1"], ["H"])
@@ -438,55 +478,64 @@ def rank_program(g, core, T, topo):
         if last:
             y_cands()
             y_diff()
-        mm(T.PE[:, 2:256:4], [(T.N32[:], nE, ["N32", "NL1"]), (T.N32[:], T.AH[:], ["AH"])], ["PE2"], ["E"])
-        mm(T.PE[:, 3:256:4], [(T.I32[:], T.AH[:], ["AH"])], ["PE3"], ["E"])
-        if t == 0:
-            mm(T.PG[:, 3:256:4], [(T.I32[:], T.MH[:], ["MH"])], ["PG3"], ["G"])
-        mm(T.PG[:, 2:256:4], [(T.N32[:], nW, ["NL1"]), (T.N32[:], T.MH[:], ["MH"])], ["PG2"], ["G"])
-        cc = T.CC[:, 128 * t:128 * t + 128]
-        add("v", lambda cc=cc: V.tensor_tensor_scan(T.TM[:], T.PA[:, 128:256], cc, 0.0, A.min, A.max),
-            ["PA2", "PA3", "CC", "LOC"], ["TM", "TM2"], ["A"])
-        ts(T.LC[:], T.TM[:, 1::2], KS, -float(C0), A.mult, A.add, r=["TM"], w=["LC"])
         d0 = ["D0z", "D0f", "D0x", "D0g"]
-        if last:
-            tt(T.D2[:, 1::2], T.D0[:, 1::4], T.D0[:, 2::4], A.not_equal, r=d0, w=["D2"])
-            y_scan()
-            for j in range(4):
-                expand("v", T.GK[:, j::4], yn[:, 1::2], j, 0, [ynk + "o"], ["GX%d" % j] + ["GK0", "GK1"] * (j == 0))
-        scan(T.SE[:], T.D0[:], T.PE[:, 0:256], r=d0 + ["PE0", "PE1", "PE2", "PE3"], w=["SE", "SE2"], b=["E"])
+        scan(T.SE[:, 0:256], T.D0[:], T.PE[:, 0:256], r=d0 + ["PE0", "PE1", "PE2", "PE3"], w=["SE", "SE2"], b=["E"])
 
         def send(c0, c1, key, sem):
             src, dst = T["MO%d" % (t + 1)][:, c0:c1], T["MI%d" % (t + 1)][:, c0:c1]
             rs = T.sem[sem]
-            add("g", lambda: g.remote_dma(dst, src, rs, T.sem.sent, pid, rid, mask), r=[key], kind="rem", sem="sent", inc=n_out)
+            add("g", lambda: g.remote_dma(dst, src, rs, T.sem.sent, pid, rid, mask), r=key, kind="rem", sem="sent", inc=n_out)
 
         if not last:
-            ts(T["MO%d" % (t + 1)][:, 0:64], T.SE[:, 3::4], 0.5, None, A.add, r=["SE"], w=["MOe%d" % t])
-            send(0, 64, "MOe%d" % t, "ae%d" % (t + 1))
-            mm(T.PA[:, 256:320], [(T.IB[:], T.D0[:, 1::4], ["D0f"]), (T.IB[:], T.D0[:, 2::4], ["D0x"])], ["PA4"], ["A"])
             y_cands()
+            ts(T["MO%d" % (t + 1)][:, 0:64], T.SE[:, 3:256:4], 0.5, None, A.add, r=["SE"], w=["MOe%d" % t])
+            send(0, 64, ["MOe%d" % t], "ae%d" % (t + 1))
+            scan(T.SE[:, 256:512], T.D0[:], T.PG[:, 0:256], r=d0 + ["PG0", "PG1", "PG2", "PG3"], w=["SW"], b=["G"])
         vw = ["VW0"] + ["VW%d_%d" % (k + 1, h) for k in range(t + 1) for h in range(2)]
         win = T.VW[:, 0:1024 * (t + 2)]
-        for h in range(2):
-            out = T.YX[:, 512 * h:512 * h + 512] if last else T.FT[:, 4096 + 1024 * h:5120 + 1024 * h:2]
-            act(out, win.indirect(T.LC[:, 32 * h:32 * h + 32]), 1.0, -BIG, r=vw + ["LC"], w=[("YX%d" if last else "FTd%d") % h])
+        cut = 32 if last else CUT
+        for h, (c0, c1) in enumerate([(0, cut), (cut, 64)]):
+            out = T.YX[:, 16 * c0:16 * c1] if last else T.FT[:, 4096 + 32 * c0:4096 + 32 * c1:2]
+            act(out, win.indirect(T.LC[:, c0:c1]), 1.0, -BIG, r=vw + ["LC"], w=[("YX%d" if last else "FTd%d") % h])
             if last:
-                dma("s", T.yx[:, 2048 + 512 * h:2560 + 512 * h], out, r=["YX%d" % h])
+                dma("s", T.yx[:, 2048 + 16 * c0:2048 + 16 * c1], out, r=["YX%d" % h])
             elif h == 0:
                 y_diff()
-        scan(T.SW[:, 0:256], T.D0[:], T.PG[:, 0:256], r=d0 + ["PG0", "PG1", "PG2", "PG3"], w=["SW"], b=["G"])
+        if last:
+            scan(T.SE[:, 256:512], T.D0[:], T.PG[:, 0:256], r=d0 + ["PG0", "PG1", "PG2", "PG3"], w=["SW"], b=["G"])
         if not last:
-            ts(T["MO%d" % (t + 1)][:, 128:192], T.PA[:, 256:320], 1.0, None, A.is_equal, r=["PA4"], w=["MOf%d" % t], b=["A"])
-            ts(T["MO%d" % (t + 1)][:, 64:128], T.SW[:, 3:256:4], 0.5, None, A.add, r=["SW", "MOf%d" % t], w=["MOw%d" % t])
-            send(64, 192, "MOw%d" % t, "aw%d" % (t + 1))
+            if t == 0:
+                cp(T.MO1[:, 128:192], T.D0[:, 2::4], r=["D0x"], w=["MOf0"])
+            else:
+                ts(T["MO%d" % (t + 1)][:, 128:192], T.PA[:, 256:320], 1.0, None, A.is_equal, r=["PA4"], w=["MOf%d" % t], b=["A"])
+            ts(T["MO%d" % (t + 1)][:, 64:128], T.SE[:, 259::4], 0.5, None, A.add, r=["SW"], w=["MOw%d" % t])
+            send(64, 192, ["MOw%d" % t, "MOf%d" % t], "aw%d" % (t + 1))
+
+            def turn(c0, c1, r, w):
+                ts(T.FT[:, c0 + 1:c1:2], T.FT[:, c0:c1:2], -1.0, 255.0, A.mult, A.add, r=[r], w=[w])
+
             y_scan()
+            turn(4096, 4096 + 32 * CUT, "FTd0", "FTd2")
             for k in range(8):
                 if k == NV1:
-                    ts(T.FT[:, 4097::2], T.FT[:, 4096::2], -1.0, 255.0, A.mult, A.add, r=["FTd0", "FTd1"], w=["FTd2"])
-                expand("v" if k < NV else "a", T.KT[:, 4096 + k::8], yn[:, 1::2], k // 2, k % 2, [ynk + "o"], [ktd[k]])
+                    turn(4096 + 32 * CUT, 6144, "FTd1", "FTd3")
+                if k == NV:
+                    expand("v", T.KT[:, 4096 + k:5120:8], yn[:, 1:256:2], k // 2, k % 2, [ynk + "o"], [ktd[8]])
+                    expand("a", T.KT[:, 5120 + k::8], yn[:, 257::2], k // 2, k % 2, [ynk + "o"], [ktd[k]])
+                else:
+                    expand("v" if k < NV else "a", T.KT[:, 4096 + k::8], yn[:, 1::2], k // 2, k % 2, [ynk + "o"], [ktd[k]])
         if t == 0:
-            dma("s", T.yx[:, 0:2048], T.FA[:], r=["FA0", "FA1"])
+            dma("s", T.yx[:, 0:2048], T.FA[:], r=["FA0", "FA1", "FW1"])
             sel(T.O4[:], T.ZB[:, 0:128], [[0, 128]], A.not_equal, 0.25, 0, 0, ["Z"], ["O4"])
+            sel(T.Q9[:], T.ZB[:, 0:64], [[0, 64]], A.not_equal, -2.375, 0, 0, ["Z"], ["Q9"])
+            iota(T.WO[:], [[0, 144]], 0, 0, ["WO"])
+            for c0 in (14, 15):
+                wo = T.WO[:, c0::16]
+                sel(wo, T.ZB[:, 0:9], [[0, 9]], A.not_equal, -0.5, 0, 0, ["Z"], ["WO"])
+                if c0 == 14:
+                    sel(wo, wo, [[-16, 9]], A.is_ge, 0.5, -8, 1, ["WO"], ["WO"])
+                sel(wo, wo, [[-16, 9]], A.is_ge, 0.0, 0, 1, ["WO"], ["WO"])
+                sel(wo, wo, [[16, 9]], A.is_ge, 0.0, 15, -1, ["WO"], ["WO"])
             sel(T.Q8[:], T.ZB[:, 0:128], [[0, 128]], A.not_equal, 0.125, 0, 0, ["Z"], ["Q8"])
             point(T.FQ[:], T.ZB[:, 0:32], [[-4, 4], [-16, 8]], 0, 1.0, ["FQ"])
         if t in (1, 2):
@@ -502,26 +551,36 @@ def rank_program(g, core, T, topo):
             sel(T.RR[:, c[3]:c[3] + 128:8], T.ZF[:, 0:16], [[-16, 8], [-4, 2]], A.not_equal, 1.0, -3 - 8 * h, 1, ["ZF"], [key[3]])
             sel(T.RR[:, c[3] + 1:c[3] + 128:2], T.ZF[:, 0:64], p2, A.not_equal, -1.0, -8 * h, 1, ["ZF"], [key[3]])
 
-    eh, wh = T.SE[:, 3::4], T.SW[:, 3:256:4]
-    for q in range(4):
-        mm(T.PA[0:8, 256 + q:512:4], [(T.FQ[:, 8 * q:8 * q + 8], T.D2[:, 1::2], ["FQ", "D2"])], ["PAf%d" % q], ["A"])
+    eh, wh = T.SE[:, 3:256:4], T.SE[:, 259:512:4]
+    tt(T.NL[:, 0:64], eh, T.D0[:, 1::4], A.mult, r=["SE", "D0f"], w=["NL0", "NL1"])
+    y_scan()
+    tt(T.NL[:, 64:128], wh, T.D0[:, 1::4], A.mult, r=["SW", "D0f"], w=["NL2"])
+    for j in range(4):
+        expand("v", T.GK[:, j::4], yn[:, 1::2], j, 0, [ynk + "o"], ["GX%d" % j] + ["GK0", "GK1"] * (j == 0))
+    tt(T.D3[:], T.D0[:, 1::4], T.D0[:, 2::4], A.not_equal, r=d0, w=["D3"])
+    back = [[(T.RR[:, 128 * (4 * h + k):128 * (4 * h + k) + 128], rh, ["RR%d" % (4 * h + k), rk])
+             for k, (rh, rk) in enumerate([(eh, "SE"), (wh, "SW"), (T.NL[:, 0:64], "NL1"), (T.NL[:, 64:128], "NL2")])]
+            for h in range(2)]
+    for h, (pb, bk) in enumerate([(T.PB, "B"), (T.PD, "D")]):
+        for i in range(3):
+            lh, rh, r = back[h][i]
+            add("p", lambda pb=pb, lh=lh, rh=rh, i=i: PE.matmul(pb[:, 256:320], lh, rh, i == 0, False), r, ["PBo%d" % h], [bk])
+    for h, (pb, bk) in enumerate([(T.PB, "B"), (T.PD, "D")]):
+        lh, rh, r = back[h][3]
+        add("p", lambda pb=pb, lh=lh, rh=rh: PE.matmul(pb[:, 256:320], lh, rh, False, True), r, ["PBo%d" % h], [bk])
     gx = ["GX%d" % j for j in range(4)]
     mm(T.PC[:, 0:128], [(T.B4[:], T.Q8[:], ["Q8"])]
        + [(T.WO[:, 14 - 2 * ib:142 - 2 * ib], T.GK[:, 128 * ib:128 * ib + 128], ["WO"] + gx) for ib in range(8)], ["PC0"], ["C"])
-    tt(T.NL[:, 0:64], eh, T.D0[:, 1::4], A.mult, r=["SE", "D0f"], w=["NL0", "NL1"])
-    tt(T.NL[:, 64:128], wh, T.D0[:, 1::4], A.mult, r=["SW", "D0f"], w=["NL2"])
-    for h in range(2):
-        mm(T.PB[:, 256 + h:384:2],
-           [(T.RR[:, 128 * (4 * h + k):128 * (4 * h + k) + 128], rh, ["RR%d" % (4 * h + k), rk])
-            for k, (rh, rk) in enumerate([(eh, "SE"), (wh, "SW"), (T.NL[:, 0:64], "NL1"), (T.NL[:, 64:128], "NL2")])],
-           ["PBo%d" % h], ["B"])
+    for q in range(4):
+        mm(T.PA[0:8, 256 + q:512:4], [(T.FQ[:, 8 * q:8 * q + 8], T.D3[:], ["FQ", "D3"])], ["PAf%d" % q], ["A"])
+    act(T.OB[:, 0::2], T.PB[:, 256:320], 1.0, 0.5, r=["PBo0"], w=["OB0"], b=["B"])
+    act(T.OB[:, 1::2], T.PD[:, 256:320], 1.0, 0.5, r=["PBo1"], w=["OB1"], b=["D"])
+    dma("s", T.yb[:], T.OB[:], r=["OB0", "OB1"])
     act(T.FO[0:8, :], T.PA[0:8, 256:512], r=["PAf%d" % q for q in range(4)], w=["FO"], b=["A"])
-    dma("a", T.yf[:], T.FO[0:8, :], r=["FO"])
+    dma("s", T.yf[:], T.FO[0:8, :], r=["FO"])
     ts(T.TM[:], T.PC[:, 0:128], B2, B2, A.add, A.subtract, r=["PC0"], w=["TM", "TM2"], b=["C"])
     ts(T.TN[:], T.TM[:], col(AL), col(GA), A.mult, A.add, r=["TM", "AL", "GA"], w=["TN"])
     tt(T.OUT[:], T.PC[:, 0:128], T.TN[:], A.add, r=["PC0", "TN"], w=["OUT"], b=["C"])
     dma("s", T.y0[:, 2048:3072], T.OUT[0::2, :], r=["OUT"])
-    dma("s", T.y1[:, 2048:3072], T.OUT[1::2, :], r=["OUT"])
-    act(T.OB[:], T.PB[:, 256:384], 1.0, 0.5, r=["PBo0", "PBo1"], w=["OB"], b=["B"])
-    dma("a", T.yb[:], T.OB[:], r=["OB"])
+    dma("a", T.y1[:, 2048:3072], T.OUT[1::2, :], r=["OUT"])
     emit(g, T, ops)

@@ -1,61 +1,123 @@
 from concourse.mybir import AluOpType, AxisListType, ActivationFunctionType
 
 RO = 5
-SCRATCH = {
-    "FA": ("sbuf", [128, 2048], "bfloat16"), "FT": ("sbuf", [128, 6144], "bfloat16"),
-    "KT": ("sbuf", [128, 6144], "bfloat16"), "VW": ("sbuf", [128, 6144], "float32"),
-    "GK": ("sbuf", [128, 1024], "bfloat16"), "FW": ("sbuf", [128, 1024], "bfloat16"),
-    "DD": ("sbuf", [128, 1024], "bfloat16"), "NR": ("sbuf", [128, 1024], "bfloat16"),
-    "YX": ("sbuf", [128, 1024], "bfloat16"),
-    "K0": ("sbuf", [128, 128], "int32"), "K1": ("sbuf", [128, 128], "int32"), "KO": ("sbuf", [128, 128], "int32"),
-    "K0F": ("sbuf", [128, 128], "float32"), "K1F": ("sbuf", [128, 128], "float32"),
-    "BI": ("sbuf", [128, 128], "int32"), "BF": ("sbuf", [128, 128], "float32"), "AB": ("sbuf", [128, 128], "float32"),
-    "FI": ("sbuf", [128, 256], "int32"), "FB": ("sbuf", [128, 256], "bfloat16"), "FO": ("sbuf", [128, 256], "float32"),
-    "HI": ("sbuf", [128, 256], "bfloat16"), "LO": ("sbuf", [128, 256], "bfloat16"),
-    "YS": ("sbuf", [128, 512], "bfloat16"), "Y0": ("sbuf", [128, 512], "bfloat16"), "Y1": ("sbuf", [128, 512], "bfloat16"),
-    "D0": ("sbuf", [128, 256], "bfloat16"), "D2": ("sbuf", [128, 128], "bfloat16"),
-    "D3": ("sbuf", [128, 64], "bfloat16"), "F0": ("sbuf", [128, 128], "bfloat16"),
-    "NL": ("sbuf", [128, 256], "float32"), "XX": ("sbuf", [128, 256], "float32"), "M2": ("sbuf", [128, 128], "bfloat16"),
-    "SE": ("sbuf", [128, 512], "float32"),
-    "AH": ("sbuf", [128, 64], "float32"), "UU": ("sbuf", [128, 128], "float32"), "SP": ("sbuf", [128, 64], "bfloat16"),
-    "UO": ("sbuf", [128, 64], "uint16"), "LC": ("sbuf", [128, 64], "uint16"), "E0": ("sbuf", [128, 64], "uint16"),
-    "TM": ("sbuf", [128, 128], "float32"), "TN": ("sbuf", [128, 128], "float32"), "OUT": ("sbuf", [128, 128], "float32"),
-    "OB": ("sbuf", [128, 128], "float32"),
-    "CC": ("sbuf", [128, 640], "float32"), "CI": ("sbuf", [128, 384], "float32"), "MH": ("sbuf", [128, 64], "float32"),
-    "IK": ("sbuf", [128, 8], "int32"), "IJ": ("sbuf", [128, 8], "int32"), "MK": ("sbuf", [128, 8], "float32"),
-    "COL": ("sbuf", [128, 16], "float32"),
-    "ZF": ("sbuf", [128, 128], "float32"), "ZB": ("sbuf", [128, 576], "bfloat16"), "ONE": ("sbuf", [128, 144], "bfloat16"),
-    "Q4": ("sbuf", [128, 64], "bfloat16"), "Q9": ("sbuf", [128, 64], "bfloat16"), "Q8": ("sbuf", [128, 128], "bfloat16"), "O4": ("sbuf", [128, 128], "bfloat16"),
-    "KM": ("sbuf", [128, 128], "float32"),
-    "RT": ("sbuf", [128, 512], "float32"), "RR": ("sbuf", [128, 1024], "float32"),
-    "I32": ("sbuf", [128, 128], "float32"), "N32": ("sbuf", [128, 128], "float32"), "UP": ("sbuf", [128, 128], "float32"),
-    "DN": ("sbuf", [128, 128], "float32"), "IU": ("sbuf", [128, 128], "float32"), "DI": ("sbuf", [128, 128], "float32"),
-    "IB": ("sbuf", [128, 128], "bfloat16"), "I2": ("sbuf", [128, 128], "bfloat16"), "NB": ("sbuf", [128, 128], "bfloat16"),
-    "B4": ("sbuf", [128, 128], "bfloat16"), "Z1": ("sbuf", [128, 128], "bfloat16"),
-    "BM": ("sbuf", [128, 144], "bfloat16"), "WA": ("sbuf", [128, 144], "bfloat16"), "WO": ("sbuf", [128, 144], "bfloat16"),
-    "WB": ("sbuf", [128, 132], "bfloat16"), "WD": ("sbuf", [128, 576], "bfloat16"), "W2": ("sbuf", [128, 576], "bfloat16"),
-    "RP": ("sbuf", [128, 512], "bfloat16"), "FF": ("sbuf", [128, 144], "bfloat16"), "FQ": ("sbuf", [128, 32], "bfloat16"),
-}
-for _t in range(RO):
-    SCRATCH["MI%d" % _t] = ("sbuf", [128, 192], "uint16")
+F32, B16, I32, U16 = "float32", "bfloat16", "int32", "uint16"
+SCRATCH = {}
+for _dt, _bufs in (
+    (B16, {"FT": 6144, "KT": 6144, "GK": 1024, "FW": 1024, "DD": 1024, "NR": 1024, "YX": 1024, "FB": 256, "HI": 256,
+           "LO": 256, "YS": 512, "Y0": 512, "Y1": 512, "D0": 256, "D2": 128, "F0": 128, "F1": 64, "F2": 64, "N4": 128, "SP": 64, "ZB": 528,
+           "ONE": 144, "NEG": 128, "ALT": 64, "HLF": 64, "MD": 128, "IB": 152, "I2": 128, "I3": 128, "NB": 128, "BM": 144,
+           "WA": 144, "NB4": 128, "Z1": 128, "ZK": 128, "ZM": 128, "WD": 528, "WU": 528, "WW": 528,
+           "RP": 512, "FF": 144, "FQ": 32, "QM": 256, "O4": 128, "Q9": 64, "WK": 272}),
+    (F32, {"VW": 6144, "E5": 384, "KF": 256, "BF": 256, "AB": 256, "FO": 256, "SE": 512, "TA": 128, "TB": 128,
+           "TN": 128, "OUT": 256, "OU2": 256, "OB": 128, "OB2": 128, "MH": 64, "MK": 8, "COL": 16, "KM": 152,
+           "RM": 288, "RR": 1024, "ZF": 128, "ID": 152, "NI": 128, "NDN": 128, "UP": 128, "DNI": 128, "IUP": 128,
+           "EW": 128, "UU": 64}),
+    (I32, {"KI": 384, "KO": 384, "FI": 256, "IK": 8, "IJ": 8}),
+    (U16, {"UO": 64, "LC": 64, "E0": 64, "MI0": 128}),
+):
+    for _n, _c in _bufs.items():
+        SCRATCH[_n] = ("sbuf", [128, _c], _dt)
 for _t in range(1, RO):
-    SCRATCH["MO%d" % _t] = ("sbuf", [128, 192], "uint16")
+    for _n, _c, _dt in (("MI", 192, U16), ("MO", 192, U16)):
+        SCRATCH["%s%d" % (_n, _t)] = ("sbuf", [128, _c], _dt)
 for _b in "ABCDEFGH":
-    SCRATCH["P" + _b] = ("psum", [128, 512], "float32")
-SEMAPHORES = (["sv", "sa", "sp", "sg", "sent", "af"] + ["d%d" % _i for _i in range(16)]
-              + ["ae%d" % _t for _t in range(1, RO)] + ["aw%d" % _t for _t in range(1, RO)])
+    SCRATCH["P" + _b] = ("psum", [128, 512], F32)
+SEMAPHORES = (["sv", "sa", "sp", "sg", "sent", "af"] + ["d%d" % _i for _i in range(24)]
+              + ["a%s%d" % (_k, _t) for _k in "e" for _t in range(1, RO)])
 
 BIG = 1.5 * 2 ** 23
 B2 = 1.5 * 2 ** 24
+B4 = 1.5 * 2 ** 25 + 4
 B32 = 1.5 * 2 ** 28
 B64 = 1.5 * 2 ** 29
+B4K = 1.5 * 2 ** 35
+OFF = 12288.0
+MID = 3071.5
 KS, C0 = 16384.0, 24576
-NV, NV1 = 4, 3
-CUT = 24
+CYC, GATHER, PCYC, WAKE, HOP, FIRST = 0.83, 1.4, 0.5, 160, 1000, 1900
+SFIX, GCUT, FWV, FWCUT, FCUT = 15, 32, False, (0, 32, 64), ((0, 32, 64, 64), (0, 32, 64, 64))
+XS = 64
+SUMS = 0
+KB = True
+BK = (0, 1)
+YD = 0
+EARLY = 0
+PAR = 2
+H5 = 0
+TMF = 2
+WC = True
+MO2 = True
+PASSES = 1
+NS = 0
+LAZY = ("spare",)
 QSEM = {"v": "sv", "a": "sa", "p": "sp", "g": "sg"}
 
 
+def order(ops):
+    writers, readers, sent = {}, {}, {}
+    for op in ops:
+        r = op["r"] + ["#" + b for b in op["b"] if op["q"] != "p" and b != "E"]
+        w = op["w"] + ["#" + b for b in op["b"] if op["q"] == "p"]
+        pre = [writers[k] for k in r + w if k in writers] + [o for k in w for o in readers.get(k, [])]
+        if op["kind"] == "arr":
+            pre.append(sent[op["sem"]])
+        if op["kind"] == "rem":
+            sent[op["to"]] = op
+        op["pre"], op["rest"] = [o for o in pre if o is not op], 0.0
+        for k in r:
+            readers.setdefault(k, []).append(op)
+        for k in w:
+            writers[k], readers[k] = op, []
+    for op in ops:
+        op["post"] = []
+        op["alt"].append((op["q"], op["f"], op["ns"]))
+    for op in reversed(ops):
+        op["rest"] += op["ns"] + op["lat"]
+        for o in op["pre"]:
+            o["post"].append(op)
+            o["rest"] = max(o["rest"], op["rest"] + (0 if o["q"] == op["q"] == "p" else WAKE))
+
+    def place(back):
+        busy = {q: [] for q in "vapgs"}
+        for op in sorted(ops, key=lambda z: (-z["rest"], -z["n"] if back else z["n"])):
+            best = None
+            for q, f, ns in op["alt"]:
+                t0 = max([o["end"] + (0 if o["q"] == q == "p" else WAKE) for o in op["post" if back else "pre"]] + [0.0])
+                t0 += op["lat"] if back else 0
+                if op["kind"] != "arr":
+                    for s, e in busy[q]:
+                        if t0 + ns <= s:
+                            break
+                        t0 = max(t0, e)
+                if best is None or t0 + ns < best[0] + best[3]:
+                    best = (t0, q, f, ns)
+            op["at"], op["q"], op["f"], op["ns"] = best
+            op["end"] = op["at"] + op["ns"] + (0 if back else op["lat"])
+            if op["kind"] != "arr":
+                busy[op["q"]].append((op["at"], op["at"] + op["ns"]))
+                busy[op["q"]].sort()
+        for op in ops:
+            op["rest"] = op["end"]
+        return max(op["end"] for op in ops)
+
+    kept = None
+    for op in reversed(ops):
+        op["rest"] = max(o["rest"] for o in op["post"]) + 1e-6 if op["lazy"] and op["post"] else -op["n"]
+    for _ in range(PASSES):
+        total = place(False)
+        if kept is None or total < kept[0]:
+            kept = (total, [(op["at"], op["q"], op["f"], op["ns"]) for op in ops])
+        place(True)
+    for op, k in zip(ops, kept[1]):
+        op["at"], op["q"], op["f"], op["ns"] = k
+    ops.sort(key=lambda z: (z["at"], z["n"]))
+    for i, op in enumerate(ops):
+        op["n"] = i
+
+
 def emit(g, T, ops):
+    order(ops)
     queue = {"v": g.vector, "a": g.scalar, "p": g.tensor, "g": g, "s": g.sync}
     clock = {q: {} for q in queue}
     writers, readers, bank = {}, {}, {}
@@ -138,406 +200,548 @@ def rank_program(g, core, T, topo):
     n_out, n_in = len(topo.engines(core, nxt)), len(topo.engines(prv, core))
     A, AF = AluOpType, ActivationFunctionType
     V, S, PE = g.vector, g.scalar, g.tensor
-    ops, nd = [], [0]
+    ops, nd, part = [], [0], [""]
 
-    def add(q, f, r=(), w=(), b=(), kind="c", sem=None, inc=0):
+    def add(q, f, ns, r=(), w=(), b=(), kind="c", sem=None, inc=0, lat=0.0, to=None):
         ops.append({"q": q, "f": f, "r": list(r), "w": list(w), "b": list(b), "kind": kind, "sem": sem, "inc": inc,
-                    "n": len(ops)})
+                    "n": len(ops), "ns": ns, "lat": lat, "to": to, "alt": [], "lazy": part[0] in LAZY})
+
+    def either():
+        o = ops.pop()
+        ops[-1]["alt"].append((o["q"], o["f"], o["ns"]))
+
+    wide = lambda *aps: any(SCRATCH[a.name][2] in (F32, I32) for a in aps)
+
+    def vns(out, per, gather=False):
+        return 50 + CYC * (GATHER * out.shape[1] if gather else max(64, per * out.shape[1]))
 
     def dma(q, out, in_, r=(), w=()):
         e = {"s": g.sync, "a": g.scalar}[q]
-        add(q, lambda: e.dma_start(out, in_), r, w, kind="dma", sem="d%d" % nd[0], inc=16)
+        add(q, lambda: e.dma_start(out, in_), 50, r, w, kind="dma", sem="d%d" % nd[0], inc=16, lat=1600 + out.shape[1])
         nd[0] += 1
 
-    def ts(out, in0, s1, s2, o0, o1=None, r=(), w=(), b=()):
+    def send(dst, src, r, sem):
+        add("g", lambda: g.remote_dma(dst, src, T.sem[sem], T.sem.sent, pid, rid, mask), FIRST if sem == "af" else 1200, r=r,
+            kind="rem", sem="sent", inc=n_out, lat=HOP, to=sem)
+
+    def arrive(w, sem):
+        add("g", None, 1, w=w, kind="arr", sem=sem, inc=n_in)
+
+    def ts(out, in0, s1, s2, o0, o1=None, r=(), w=(), b=(), gather=False, stepped=False):
+        ns = vns(out, 1 if gather or stepped or wide(out, in0) else 0.5, gather)
         if o1 is None:
-            add("v", lambda: V.tensor_scalar(out, in0, s1, None, o0), r, w, b)
+            add("v", lambda: V.tensor_scalar(out, in0, s1, None, o0), ns, r, w, b)
         else:
-            add("v", lambda: V.tensor_scalar(out, in0, s1, s2, o0, o1), r, w, b)
+            add("v", lambda: V.tensor_scalar(out, in0, s1, s2, o0, o1), ns, r, w, b)
 
-    def tt(out, in0, in1, o, r=(), w=(), b=()):
-        add("v", lambda: V.tensor_tensor(out, in0, in1, o), r, w, b)
+    def tt(out, in0, in1, o, r=(), w=(), b=(), gather=False):
+        psum = any(SCRATCH[a.name][0] == "psum" for a in (out if gather else in0, in1))
+        add("v", lambda: V.tensor_tensor(out, in0, in1, o), vns(out, 1 if psum else 2, gather), r, w, b)
 
-    def cp(out, in_, r=(), w=(), b=()):
-        add("v", lambda: V.tensor_copy(out, in_), r, w, b)
+    def cp(out, in_, r=(), w=(), b=(), gather=False):
+        add("v", lambda: V.tensor_copy(out, in_), vns(out, 1, gather), r, w, b)
 
     def ms(ap, val, w=(), b=()):
-        add("v", lambda: V.memset(ap, val), (), w, b)
+        add("v", lambda: V.memset(ap, val), vns(ap, 1 if wide(ap) else 0.5), (), w, b)
 
-    def scan(out, d0, d1, r=(), w=(), b=()):
-        add("v", lambda: V.tensor_tensor_scan(out, d0, d1, 0.0, A.mult, A.add), r, w, b)
+    def scan(out, d0, d1, r=(), w=(), b=(), o0=A.mult, o1=A.add):
+        add("v", lambda: V.tensor_tensor_scan(out, d0, d1, 0.0, o0, o1), vns(out, 1 if wide(out, d0, d1) else 0.5), r, w, b)
 
-    def act(out, in_, scale=1.0, bias=0.0, r=(), w=(), b=()):
-        if isinstance(bias, float) and bias == 0.0:
-            add("a", lambda: S.activation(out, in_, AF.Copy, scale=scale), r, w, b)
+    def act(out, in_, scale=1.0, bias=0.0, r=(), w=(), b=(), f=None, gather=False, more=0):
+        ns = (15 if gather else SFIX) + more + vns(out, 1, gather)
+        if f is None:
+            f = AF.Copy if isinstance(bias, float) and bias == 0.0 else AF.Identity
+        if f == AF.Copy:
+            add("a", lambda: S.activation(out, in_, f, scale=scale), ns, r, w, b)
         else:
-            add("a", lambda: S.activation(out, in_, AF.Identity, bias=bias, scale=scale), r, w, b)
+            add("a", lambda: S.activation(out, in_, f, bias=bias, scale=scale), ns, r, w, b)
 
-    def step(out, in_, scale, bias, r, w, b=()):
-        add("a", lambda: S.activation(out, in_, AF.Sigmoid, bias=bias, scale=scale), r, w, b)
+    def step(out, in_, thr, r, w, b=(), more=0):
+        act(out, in_, 1000.0, -1000.0 * thr, r, w, b, AF.Sigmoid, more=more)
 
-    def mm(out, terms, w, b):
+    def mm(out, terms, w, b, start=True, stop=True):
         for i, (lh, rh, r) in enumerate(terms):
-            add("p", lambda lh=lh, rh=rh, i=i: PE.matmul(out, lh, rh, i == 0, i == len(terms) - 1), r, w, b)
+            st, sp = start and i == 0, stop and i == len(terms) - 1
+            add("p", lambda lh=lh, rh=rh, st=st, sp=sp: PE.matmul(out, lh, rh, st, sp),
+                PCYC * max(64, out.shape[1]) * (4 if wide(lh) else 1), r + [lh.name, "Z"], w, b)
 
     def iota(out, pat, base, cm, w, flt=True):
+        ns = 130 + 2 * CYC * out.shape[1]
         if flt:
-            add("g", lambda: g.iota(out, pat, base, cm, allow_small_or_imprecise_dtypes=True), (), w)
+            add("g", lambda: g.iota(out, pat, base, cm, allow_small_or_imprecise_dtypes=True), ns, (), w)
         else:
-            add("g", lambda: g.iota(out, pat, base, cm), (), w)
+            add("g", lambda: g.iota(out, pat, base, cm), ns, (), w)
 
     def sel(out, in_, pat, op, fill, base, cm, r, w):
-        add("g", lambda: g.affine_select(out, in_, pat, op, fill, base, cm), r, w)
+        add("g", lambda: g.affine_select(out, in_, pat, op, fill, base, cm), 170 + 2 * CYC * out.shape[1], r, w)
 
     def point(out, zero, pat, base, val, w):
-        sel(out, zero, pat, A.not_equal, val, base, 1, ["Z"], w)
+        sel(out, zero, pat, A.not_equal, val, base, 1, ["Z", "ZF"], w)
 
-    def band(out, pat, base, width, w):
+    def const(out, val, w):
+        c = out.shape[1]
+        sel(out, T.ZB[:, 0:c], [[0, c]], A.not_equal, val, 0, 0, ["Z"], w)
+
+    def band(out, src, pat, base, width, w):
         cols = pat[0][1] * pat[1][1]
-        sel(out, T.ONE[:, 0:cols], pat, A.is_ge, 0.0, base, 1, ["ONE"], w)
+        sel(out, src[:, 0:cols], pat, A.is_ge, 0.0, base, 1, [src.name], w)
         sel(out, out, [[-s, c] for s, c in pat], A.is_ge, 0.0, width - 1 - base, -1, w, w)
 
-    col = lambda j: T.COL[:, j:j + 1]
-    SG, R16, AL, GA, RM, PAR, RED, RND, ODD, THR = 0, 1, 2, 3, 4, 5, 6, 7, 8, 9
+    def rev(hi, cnt, st):
+        lo = hi - cnt * st
+        return slice(hi, lo if lo >= 0 else None, -st)
 
-    dma("s", T.K1[:], T.kid1[:], w=["K1"])
-    dma("s", T.K0[:], T.kid0[:], w=["K0"])
-    dma("a", T.FA[:, 0:1024], T.faces[:, 0:1024], w=["FA0"])
-    dma("a", T.FA[:, 1024:2048], T.faces[:, 1024:2048], w=["FA1"])
-    dma("s", T.BI[:], T.belts[:], w=["BI"])
-    dma("s", T.FI[0:8, :], T.flip[:], w=["FI"])
+    col = lambda j: T.COL[:, j:j + 1]
+    SG, SH, G16, RM5, RED, RND, YB, YH = range(8)
+
+    dma("s", T.KI[:, 0:128], T.kid0[:], w=["K0"])
+    dma("a", T.KI[:, 128:256], T.kid1[:], w=["K1"])
+    dma("s", T.KI[:, 256:384], T.belts[:], w=["BI"])
+    dma("a", T.FI[0:8, :], T.flip[:], w=["FI"])
+    dma("s", T.FT[:, 3072:4096], T.faces[:, 0:1024], w=["FTa"])
+    dma("s", T.FT[:, 4096:5120], T.faces[:, 1024:2048], w=["FTb"])
+    dma("s", T.FT[:, 5120:6144], T.faces[:, 0:1024], r=["FTa"], w=["FTe0", "FTe1", "FTe2"])
 
     ms(T.ZB[:], 0.0, ["Z"])
+    iota(T.IK[:, 0:4], [[-4, 4]], 16, 1, ["IK"], False)
+    iota(T.KM[:], [[-1, 152]], 12, 1, ["KM"])
+    point(T.WD[:], T.ZB[:], [[-4, 33], [-1000, 4], [-1, 4]], 3000, 1.0, ["WD"])
+    step(col(RED), T.ZB[:, 0:1], 1.0, ["Z"], ["RED", "LUT"], more=1300)
     ms(T.ONE[:], 1.0, ["ONE"])
-    iota(T.IK[:, 0:5], [[-1, 5]], 4, 1, ["IK"], False)
-    iota(T.KM[:], [[-1, 128]], 0, 1, ["KM"])
-    iota(T.CI[:], [[1024, 6], [16, 64]], C0, 0, ["CI"])
-    point(T.WD[:], T.ZB[:], [[-16, 9], [-1000, 4], [-1, 16]], 3000, 1.0, ["WD"])
-    band(T.BM[:], [[-16, 9], [1000, 16]], -15000, 16, ["BM"])
-    iota(T.ZF[:], [[0, 128]], 0, 0, ["ZF"])
-    for k in range(4):
-        sel(T.RT[:, 128 * k:128 * k + 128], T.ZF[:], [[-16, 8], [-1000, 2], [-2, 8]], A.not_equal, 1.0,
-            1000 * (k // 2) - k % 2, 1, ["ZF"], ["RT%d" % k])
+    ms(T.NEG[:], -1.0, ["NEG"])
+    ms(T.HLF[:], 0.5, ["HLF"])
+    for z, keys, after in ((T.QM, ["QM", "QM0"], "BI"), (T.WU, ["WU%d" % q for q in range(4)], "BI"),
+                           (T.WW, ["WW%d" % q for q in range(4)], "BI"), (T.WK, ["WK"], "FTe0")):
+        dma("s", z[:], T.ZB[:, 0:z.shape[1]], r=["Z", after], w=keys)
+    point(T.RM[:], T.ZB[:, 0:288], [[-16, 9], [-1000, 2], [-1, 16]], 1000, 1.0, ["RM"])
     point(T.FF[0:8, :], T.ZB[0:8, 0:144], [[-1, 9], [-1000, 4], [0, 4]], 3000, 1.0, ["FF"])
     iota(T.D2[:, 0::2], [[0, 64]], 0, 0, ["D2z"])
-    iota(T.M2[:], [[0, 64], [-2, 2]], 0, 0, ["M2"])
-    band(T.B4[:], [[-4, 32], [0, 4]], 0, 4, ["B4"])
-    band(T.WB[:], [[-4, 33], [1000, 4]], -3000, 4, ["WB"])
-    iota(T.D0[:, 0::4], [[0, 64]], 0, 0, ["D0z"])
-    sel(T.Q4[:], T.ZB[:, 0:64], [[0, 64]], A.not_equal, 0.25, 0, 0, ["Z"], ["Q4"])
+    band(T.BM[:], T.ONE, [[-16, 9], [1000, 16]], -15000, 16, ["BM"])
+    sel(T.MD[:], T.ZB[:, 0:128], [[0, 64], [1, 2]], A.is_equal, -0.5, 0, 0, ["Z"], ["MD"])
+    ID, IB, KM = T.ID[:, 12:140], T.IB[:, 12:140], T.KM[:, 12:140]
 
-    ts(T.IJ[:, 0:4], T.IK[:, 0:4], 3, None, A.bitwise_and, r=["IK"], w=["IJ0"])
-    ts(T.IJ[:, 4:5], T.IK[:, 4:5], 8, None, A.bitwise_and, r=["IK"], w=["IJ1"])
-    ts(T.IJ[:, 5:6], T.IK[:, 4:5], 15, None, A.bitwise_and, r=["IK"], w=["IJ2"])
-    ts(T.I32[:], T.KM[:], 0.0, None, A.is_equal, r=["KM"], w=["I32"])
-    ts(T.UP[:], T.KM[:], 1.0, None, A.is_equal, r=["KM"], w=["UP"])
-    ts(T.DN[:], T.KM[:], -1.0, None, A.is_equal, r=["KM"], w=["DN"])
-    ts(T.UP[:, 3::4], T.KM[:, 3::4], -3.0, None, A.is_equal, r=["KM"], w=["UP"])
-    ts(T.DN[:, 0::4], T.KM[:, 0::4], 3.0, None, A.is_equal, r=["KM"], w=["DN"])
-    ts(T.MK[:, 0:4], T.IJ[:, 0:4], 0.0, None, A.is_equal, r=["IJ0"], w=["MKe"])
-    ts(col(SG), T.IJ[:, 4:5], -0.25, 1.0, A.mult, A.add, r=["IJ1"], w=["SG"])
-    ts(col(R16), T.IJ[:, 5:6], 1.0 / KS, None, A.mult, r=["IJ2"], w=["R16"])
-    ts(col(RM), T.IJ[:, 5:6], 2.0, 4095.5 - 2 * C0, A.mult, A.add, r=["IJ2"], w=["RM"])
-    tt(col(ODD), T.MK[:, 1:2], T.MK[:, 3:4], A.add, r=["MKe"], w=["ODD"])
-    ts(T.MK[:, 4:8], T.MK[:, 0:4], col(SG), None, A.mult, r=["MKe", "SG"], w=["MKo"])
-    act(T.N32[:], T.I32[:], -1.0, r=["I32"], w=["N32"])
-    step(T.IB[:], T.I32[:], 1000.0, -500.0, ["I32"], ["IB"])
-    act(T.I2[:], T.I32[:], 2.0, r=["I32"], w=["I2"])
-    act(T.NB[:], T.I32[:], -1.0, r=["I32"], w=["NB"])
-    mm(T.PG[:, 0:128], [(T.I32[:], T.DN[:], ["I32", "DN"]), (T.I32[:], T.N32[:], ["N32"])], ["PG0"], ["G"])
-    mm(T.PG[:, 128:256], [(T.N32[:], T.UP[:], ["UP"]), (T.I32[:], T.I32[:], [])], ["PG1"], ["G"])
+    ts(T.IJ[:, 0:4], T.IK[:, 0:4], 12, None, A.bitwise_and, r=["IK"], w=["IJ0"])
+    ts(T.IJ[:, 4:5], T.IK[:, 0:1], 2, None, A.bitwise_and, r=["IK"], w=["IJ1"])
+    ts(T.IJ[:, 5:6], T.IK[:, 0:1], 15, None, A.bitwise_and, r=["IK"], w=["IJ2"])
+    ts(T.IJ[:, 7:8], T.IK[:, 0:1], 3, None, A.bitwise_and, r=["IK"], w=["IJ4"])
+    ts(T.ID[:], T.KM[:], 0.0, None, A.is_equal, r=["KM"], w=["ID"])
+    ts(T.NDN[:], KM, -1.0, -1.0, A.is_equal, A.mult, r=["KM"], w=["NDN"])
+    ts(T.UP[:], KM, 1.0, None, A.is_equal, r=["KM"], w=["UP"])
+    ts(T.MK[:, 4:8], T.IJ[:, 0:4], 0.0, None, A.is_equal, r=["IJ0"], w=["MKo"])
+    ts(col(SG), T.IJ[:, 4:5], -1.0, 1.0, A.mult, A.add, r=["IJ1"], w=["SG"])
+    ts(T.NDN[:, 0::4], T.KM[:, 12:140:4], 3.0, -1.0, A.is_equal, A.mult, r=["KM"], w=["NDN"])
+    ts(T.UP[:, 3::4], T.KM[:, 15:140:4], -3.0, None, A.is_equal, r=["KM"], w=["UP"])
+    ts(col(YH), T.IJ[:, 7:8], 3.0, 0.5, A.is_equal, A.mult, r=["IJ4"], w=["YH"])
+    act(T.NI[:], ID, -1.0, r=["ID", "LUT"], w=["NI"])
+    act(T.MK[:, 0:4], T.MK[:, 4:8], col(SG), r=["MKo", "SG"], w=["MKe"])
+    act(T.IB[:], T.ID[:], r=["ID"], w=["IB"])
+    act(T.NB[:], ID, -1.0, r=["ID"], w=["NB"])
+    act(T.I2[:], ID, 2.0, r=["ID"], w=["I2"])
+    act(T.I3[:], ID, 3.0, r=["ID"], w=["I3"])
+    act(col(SH), col(SG), -0.5, r=["SG"], w=["SH"])
     mm(T.PH[:, 0::2], [(T.ZB[:, 0:128], T.ZB[:, 0:256], ["Z"])], ["PH0"], ["H"])
-    act(T.CC[:, 0::2], T.CI[:, 64:384], 1.0 / KS, col(R16), r=["CI", "R16"], w=["CC"])
-    act(T.CC[:, 1:128:2], T.CI[:, 0:64], 1.0 / KS, col(R16), r=["CI", "R16"], w=["LOC"])
-    act(T.MH[:], T.CI[:, 0:64], 2.0, col(RM), r=["CI", "RM"], w=["MH"])
-    act(T.DI[:], T.PG[:, 0:128], r=["PG0"], w=["DI"], b=["G"])
-    act(T.IU[:], T.PG[:, 128:256], r=["PG1"], w=["IU"], b=["G"])
-    act(col(AL), col(ODD), -2.0, r=["ODD"], w=["AL"])
-    act(col(GA), col(ODD), 1.0, -0.5, r=["ODD"], w=["GA"])
+    mm(T.PB[:, 128:256:2], [(T.ZB[:, 0:128], T.ZB[:, 0:64], ["Z"])], ["PBz"], ["B"])
+    mm(T.PG[:, 0:128], [(T.NI[:], ID, ["ID"]), (T.NI[:], T.NDN[:], ["NDN"])], ["PG"], ["G"])
+    mm(T.PG[:, 128:256], [(ID, ID, []), (T.NI[:], T.UP[:], ["UP"])], ["PG"], ["G"])
 
-    ts(T.KO[:], T.K1[:], 1, None, A.bitwise_and, r=["K1"], w=["KO"])
-    ts(T.PC[:, 0:128], T.KO[:], -2.0, 1.0, A.mult, A.add, r=["KO"], w=["PC0"], b=["C"])
-    tt(T.PC[:, 128:256], T.PC[:, 0:128], T.K1[:], A.add, r=["PC0", "K1"], w=["PC1"], b=["C"])
-    cp(T.BF[:], T.BI[:], r=["BI"], w=["BF"])
-    tt(T.PD[:, 0:128], T.PC[:, 128:256], T.K0[:], A.add, r=["PC1", "K0"], w=["PD0"], b=["C", "D"])
-    tt(T.PD[:, 128:256], T.PC[:, 128:256], T.K0[:], A.subtract, r=["PC1", "K0"], w=["PD1"], b=["C", "D"])
-    ts(T.HI[:, 0:128], T.PD[:, 0:128], B64, B64, A.add, A.subtract, r=["PD0"], w=["HIa"], b=["D"])
-    ts(T.HI[:, 128:256], T.PD[:, 128:256], B64, B64, A.add, A.subtract, r=["PD1"], w=["HI"], b=["D"])
-    tt(T.LO[:, 0:128], T.PD[:, 0:128], T.HI[:, 0:128], A.subtract, r=["PD0", "HIa"], w=["LOa"], b=["D"])
-    tt(T.LO[:, 128:256], T.PD[:, 128:256], T.HI[:, 128:256], A.subtract, r=["PD1", "HI", "LOa"], w=["LO"], b=["D"])
-    act(T.FT[:, 1:2048:2], T.FA[:, 0:1024], -1.0, 255.0, r=["FA0"], w=["FTs1"])
-    cp(T.FT[:, 0:2048:2], T.FA[:, 0:1024], r=["FA0"], w=["FTs0"])
+
+    kw = 384 if KB else 256
+    ts(T.KO[:, 0:kw], T.KI[:, 0:kw], 1, None, A.bitwise_and, r=["K0", "K1"] + ["BI"] * KB, w=["KO"])
+    ts(T.E5[:, 0:kw], T.KI[:, 0:kw], 0.5, None, A.add, r=["K0", "K1"] + ["BI"] * KB, w=["E5"])
+    ts(T.PC[:, 0:kw], T.KO[:, 0:kw], -1.0, 0.5, A.mult, A.add, r=["KO"], w=["PC0"], b=["C"])
+    if not KB:
+        ts(T.KO[:, 256:384], T.KI[:, 256:384], 1, None, A.bitwise_and, r=["BI", "KO"], w=["KOb"])
+    tt(T.PC[:, 384:512], T.PC[:, 0:128], T.E5[:, 0:128], A.mult, r=["PC0", "E5"], w=["PC1"], b=["C"])
+    tt(T.BF[:, 0:kw - 128], T.PC[:, 128:kw], T.E5[:, 128:kw], A.mult, r=["PC0", "E5"], w=["BK"] + ["BF"] * KB, b=["C"])
+    if not KB:
+        ts(T.E5[:, 256:384], T.KI[:, 256:384], 0.5, None, A.add, r=["BI", "PC0"], w=["E5b"])
+    tt(T.PD[:, 0:128], T.PC[:, 384:512], T.BF[:, 0:128], A.subtract, r=["PC1", "BK"], w=["PD0"], b=["C", "D"])
+    tt(T.PD[:, 128:256], T.PC[:, 384:512], T.BF[:, 0:128], A.add, r=["PC1", "BK"], w=["PD1"], b=["C", "D"])
+    ts(T.HI[:, 0:128], T.PD[:, 0:128], B64, B64, A.add, A.subtract, r=["PD0"], w=["HI", "HIw"], b=["D"])
+    ts(T.HI[:, 128:256], T.PD[:, 128:256], B64, B64, A.add, A.subtract, r=["PD1"], w=["HId"], b=["D"])
+    tt(T.LO[:, 0:128], T.PD[:, 0:128], T.HI[:, 0:128], A.subtract, r=["PD0", "HI"], w=["LO", "LOw"], b=["D"])
+    tt(T.LO[:, 128:256], T.PD[:, 128:256], T.HI[:, 128:256], A.subtract, r=["PD1", "HId"], w=["LOd"], b=["D"])
+    if not KB:
+        ts(T.PC[:, 256:384], T.KO[:, 256:384], -1.0, 0.5, A.mult, A.add, r=["KOb"], w=["PC2"], b=["C"])
     cp(T.FB[0:8, :], T.FI[0:8, :], r=["FI"], w=["FB"])
-    dma("s", T.FT[:, 4096:6144], T.FT[:, 0:2048], r=["FTs0", "FTs1"], w=["FTd0", "FTd1", "FTd2", "FTd3", "FTd4"])
-    act(T.FT[:, 2049:4096:2], T.FA[:, 1024:2048], -1.0, 255.0, r=["FA1"], w=["FTs3"])
+    if not KB:
+        tt(T.BF[:, 128:256], T.PC[:, 256:384], T.E5[:, 256:384], A.mult, r=["PC2", "E5b"], w=["BF"], b=["C"])
+    act(T.FT[:, rev(3071, 1024, 1)], T.FT[:, 3072:4096], -1.0, 255.0, r=["FTa"], w=["FTc"])
+    dma("s", T.FT[:, 0:1024], T.FT[:, 2048:3072], r=["FTc"], w=["FTo0", "FTo1"])
+    act(T.FT[:, rev(2047, 1024, 1)], T.FT[:, 4096:5120], -1.0, 255.0, r=["FTb"], w=["FTd"])
 
-    def digit(dd, w):
-        src = T.HI if dd % 2 == 0 else T.LO
-        return src[:, w * (dd // 2):w * (dd // 2) + w], ["HI" if dd % 2 == 0 else "LO"]
-
-    for b in range(4):
-        terms = []
-        for dd in (0, 2, 1, 3):
-            s0 = 4 * (12 - 4 * dd) + b
-            rh, rr = digit(dd, 128)
-            terms.append((T.WD[:, s0:s0 + 509:4], rh, rr + ["WD"]))
-        mm(T.PF[:, 128 * b:128 * b + 128], terms, ["PF%d" % b], ["F"])
+    wd = lambda b, dd: T.WD[:, 12 + b - 4 * dd:12 + b - 4 * dd + 509:4]
+    halves = [(T.PF, "F", ["PY"]), (T.PE, "E", ["PE0", "PE1", "PE2", "PE3"])]
+    for pb, bk, key in halves:
+        mm(pb[:, 0:256], [(T.ZB[:, 0:128], T.ZB[:, 0:256], [])], key, [bk], stop=False)
+    for dd, src, k in ((0, T.HI[:, 0:128], "HI"), (2, T.HI[:, 128:256], "HId"), (1, T.LO[:, 0:128], "LO"), (3, T.LO[:, 128:256], "LOd")):
+        for b in range(4):
+            pb, bk, key = halves[b // 2]
+            mm(pb[:, 128 * (b % 2):128 * (b % 2) + 128], [(wd(b, dd), src, [k])], key, [bk], start=False, stop=dd == 3 and b % 2 == 1)
+    act(T.YS[:, 0:256], T.PF[:, 0:256], 1.0, col(YH), r=["PY", "YH"], w=["YS0"], b=["F"])
+    ts(T.YS[:, 256:512], T.PE[:, 0:256], col(YH), None, A.add, r=["PE0", "PE1", "PE2", "PE3", "YH"], w=["YS1"], b=["E"])
     for e in range(2):
         mm(T.PB[:, 64 * e:64 * e + 64],
-           [(T.RT[:, 128 * (2 * h + e):128 * (2 * h + e) + 128], T.BF[:, h::2], ["BF", "RT%d" % (2 * h + e)]) for h in range(2)],
-           ["PB%d" % e], ["B"])
-    mm(T.PA[:, 0:64], [(T.FF[0:8, 12 - 4 * q:140 - 4 * q], T.FB[0:8, q::4], ["FF", "FB"]) for q in range(4)], ["PA0"], ["A"])
-    act(T.YS[:], T.PF[:], r=["PF0", "PF1", "PF2", "PF3"], w=["YS"], b=["F"])
-    act(T.AB[:], T.PB[:, 0:128], r=["PB0", "PB1"], w=["AB"], b=["B"])
-    aa, bb = T.AB[:, 0:64], T.AB[:, 64:128]
-    mm(T.PE[:, 0:128:2], [(T.I32[:], bb, ["I32", "AB"]), (T.N32[:], aa, ["N32"])], ["PE0"], ["E"])
-    mm(T.PE[:, 1:128:2], [(T.I32[:], aa, [])], ["PE1"], ["E"])
-    mm(T.PE[:, 128:256:2], [(T.UP[:], aa, ["UP"]), (T.N32[:], bb, [])], ["PE2"], ["E"])
-    mm(T.PE[:, 129:256:2], [(T.I32[:], bb, [])], ["PE3"], ["E"])
-    cp(T.FT[:, 2048:4096:2], T.FA[:, 1024:2048], r=["FA1"], w=["FTs2"])
-    ts(T.WA[:], T.BM[:], col(SG), None, A.mult, r=["BM", "SG"], w=["WA"])
-    cp(T.K0F[:], T.K0[:], r=["K0"], w=["KF0"])
+           [(T.RM[:, 16 + e - 16 * h:16 + e - 16 * h + 255:2], T.BF[:, 128 + h::2], ["BF"]) for h in range(2)], ["PB%d" % e], ["B"])
+    aa, bb = T.AB[:, 1:128:2], T.AB[:, 129:256:2]
+    mm(T.PA[:, 0:64], [(T.FF[0:8, 12 - 4 * q:140 - 4 * q], T.FB[0:8, q::4], ["FB"]) for q in range(4)], ["PA0"], ["A"])
+    belts = [
+        lambda: ts(T.AB[:, 1::2], T.PB[:, 0:128], 0.25, None, A.add, r=["PB0", "PB1"], w=["AB"], b=["B"]),
+        lambda: cp(T.D2[:, 1::2], T.PA[:, 0:64], r=["PA0", "D2z"], w=["D2"], b=["A"]),
+        lambda: tt(T.AB[:, 0:128:2], bb, aa, A.subtract, r=["AB"], w=["AB0"]),
+        lambda: mm(T.PB[:, 0:64], [(T.UP[:], aa, ["AB"])], ["PB0"], ["B"]),
+        None,
+        lambda: scan(T.SE[:, 0:128], T.D2[:], T.AB[:, 0:128], r=["D2", "AB", "AB0"], w=["SE"]),
+        lambda: tt(T.AB[:, 128:256:2], T.PB[:, 0:64], bb, A.subtract, r=["AB", "PB0"], w=["AB1"], b=["B"]),
+        lambda: ts(T.SE[:, 0:128:2], T.SE[:, 1:128:2], B4K, B4K, A.add, A.subtract, r=["SE"], w=["SEj"]),
+        lambda: scan(T.SE[:, 128:256], T.D2[:], T.AB[:, 128:256], r=["D2", "AB", "AB1"], w=["SW"]),
+        lambda: scan(T.TN[:], T.MD[:], T.SE[:, 0:128], r=["MD", "SE", "SEj"], w=["TN"]),
+        lambda: ts(T.MI0[:], T.SE[:, 1:256:2], MID, None, A.add, r=["SE", "SW"], w=["MI0e", "MI0w"]),
+        lambda: ts(T.E0[:], T.TN[:, 1::2], MID - 1024, None, A.add, r=["TN"], w=["E0"]),
+        None,
+    ]
+    act(T.DNI[:], T.PG[:, 0:128], r=["PG"], w=["DNI"], b=["G"])
+    act(T.IUP[:], T.PG[:, 128:256], r=["PG"], w=["IUP"], b=["G"])
 
-    mm(T.PG[:, 3:256:4], [(T.I32[:], T.MH[:], ["MH"])], ["PG3", "PG0", "PG1"], ["G"])
-
-    def expand(q, out, src, j, t, r, w):
+    def expand(out, src, j, t, r, w):
         m = T.MK[:, 4 * t + j:4 * t + j + 1]
-        if q == "v":
-            ts(out, src, m, None, A.mult, r=r + ["MKe", "MKo"], w=w)
-        else:
-            act(out, src, m, r=r + ["MKe", "MKo"], w=w)
+        ts(out, src, m, None, A.mult, r=r + ["MKe", "MKo"], w=w, stepped=H5 >= (1 if src.name != "YS" else 2 if t else 3))
+        act(out, src, m, r=r + ["MKe", "MKo"], w=w)
+        either()
 
     kts = ["KTs%d" % k for k in range(8)]
-    ktd = ["KTd%d" % k for k in range(9)]
+    ktd = ["KTd%d" % k for k in range(8)]
     for k in range(8):
         a, t = k // 2, k % 2
-        if k == 2:
-            cp(T.D2[:, 1::2], T.PA[:, 0:64], r=["PA0", "D2z"], w=["D2"], b=["A"])
-            cp(T.MI0[:, 128:192], T.PA[:, 0:64], r=["PA0"], w=["MI0f"], b=["A"])
-        if k == 3:
-            scan(T.SE[:, 0:128], T.D2[:], T.PE[:, 0:128], r=["D2", "PE0", "PE1"], w=["SE"], b=["E"])
-            scan(T.SE[:, 128:256], T.D2[:], T.PE[:, 128:256], r=["D2", "PE2", "PE3"], w=["SE2"], b=["E"])
-            ts(T.TM[:, 0:64], T.SE[:, 1:128:2], 4096.0, -4096.0, A.is_ge, A.mult, r=["SE"], w=["TM"])
-            cp(T.MI0[:, 0:128], T.SE[:, 1:256:2], r=["SE", "SE2"], w=["MI0e", "MI0w"])
-            tt(T.TM[:, 64:128], T.TM[:, 0:64], T.SE[:, 1:128:2], A.add, r=["SE", "TM"], w=["TM2"])
-        expand("a" if k >= 4 else "v", T.KT[:, 1024 * a + t:1024 * a + 1024:2], T.YS[:], a, t, ["YS"], [kts[k]])
-    cp(T.E0[:], T.TM[:, 64:128], r=["TM2"], w=["E0"])
+        out = T.KT[:, rev(3071 - 512 * a, 512, 1)] if t else T.KT[:, 3072 + 512 * a:3584 + 512 * a]
+        while k in BK and belts[0]:
+            belts.pop(0)()
+        if k in BK:
+            belts.pop(0)
+        expand(out, T.YS[:], a, t, ["YS0", "YS1"], [kts[k]])
+
+    part[0] = "const"
+    band(T.NB4[:], T.NEG, [[-4, 32], [0, 4]], 0, 4, ["NB4"])
+    iota(T.TA[:], [[16, 64], [-1024, 2]], C0 + 1024, 1, ["TAe", "TAo"])
+    const(T.QM[:, 0::4], 8.0, ["QM0"])
+    const(T.QM[:, 3::4], -0.8125, ["QM"])
+    iota(T.ALT[:], [[0, 32], [2, 2]], -1, 0, ["ALT"])
+    for q in range(4):
+        pat = [[-16, 8], [-1, 4], [0, 2]]
+        sel(T.WU[:, 4 + q:516:8], T.HLF[:], pat, A.is_equal, 0.0, -4 * q, 1, ["HLF"], ["WU%d" % q])
+        sel(T.WW[:, 4 + q:516:8], T.ALT[:], pat, A.is_equal, 0.0, -4 * q, 1, ["ALT"], ["WW%d" % q])
+    sel(T.ZM[:], T.NB4[:], [[-1, 128]], A.not_equal, 2.0, 0, 1, ["NB4"], ["ZM"])
 
     for q in range(4):
-        point(T.W2[:, 144 * q:144 * q + 144], T.ZB[:, 0:144], [[-16, 9], [-1000, 4], [-1, 4]], 3000 - 4 * q, 1.0, ["W2%d" % q])
-    for q in range(4):
-        point(T.RP[:, 128 * q:128 * q + 128], T.ZB[:, 0:128], [[-16, 8], [0, 4], [-1, 4]], -4 * q, -1.0, ["RP%d" % q])
+        point(T.RP[:, 128 * q:128 * q + 128], T.ZB[:, 0:128], [[-16, 8], [-1, 4], [0, 4]], -4 * q, 1.0, ["RP%d" % q])
 
-    ybuf = [T.Y0, T.Y1]
+    ybuf, tbuf = [T.Y0, T.Y1], [(T.TA, "TA"), (T.TB, "TB")]
+    ft = ["FTa", "FTb", "FTc", "FTd", "FTe0", "FTe1", "FTe2", "FTo0", "FTo1"]
     for t in range(RO):
+        part[0] = ""
         last = t == RO - 1
         MI = T["MI%d" % t]
-        e_, w_, f_ = "MI%de" % t, "MI%dw" % t, "MI%df" % t
+        e_, w_, f_ = "MI%de" % t, "MI%dw" % t, "GI%d" % t
         yo, yn = ybuf[t % 2], ybuf[(t + 1) % 2]
         yok, ynk = "Y%d" % (t % 2), "Y%d" % ((t + 1) % 2)
-        if t > 0:
-            add("g", None, w=[e_], kind="arr", sem="ae%d" % t, inc=n_in)
-            add("g", None, w=[w_, f_], kind="arr", sem="aw%d" % t, inc=n_in)
-        ft = ["FTs0", "FTs1", "FTs2", "FTs3", "FTd0", "FTd1", "FTd2", "FTd3", "FTd4"]
         if t == 0:
-            kw, eo, kr = T.KT[:, 0:4096], T.E0, kts + ["E0"]
+            kw, eo, kr = T.KT[:, 1024:5120], T.E0, kts + ["E0"]
+            xE, xW, ke, kh = T.SE[:, 1:128:2], T.SE[:, 129:256:2], ["SE"], ["SW"]
+            fp, kf = T.D2[:, 1::2], ["D2"]
         else:
+            arrive([e_, w_], "ae%d" % t)
             kw, eo, kr = T.KT[:, 0:6144], MI, kts + ktd + [e_]
-        if t == 0:
-            mm(T.PH[:, 1::2], [(T.WB[:, 3 - j:131 - j], T.KT[:, 2 * j:2048:8], ["WB"] + kts) for j in range(4)], ["PH1"], ["H"])
-        cp(T.GK[:, 0:512], kw.indirect(eo[:, 0:32]), r=kr, w=["GK0"])
-        act(T.GK[:, 512:1024], kw.indirect(eo[:, 32:64]), r=kr, w=["GK1"])
+            xE, xW, ke, kh = T.EW[:, 0:64], T.EW[:, 64:128], ["EW"], ["EW"]
+            fp, kf = T.F1[:], ["F1"]
+        sk = lambda s: T.PE[:, s:256:4]
+        sh = lambda s: T.PE[:, 256 + s:512:4]
+        zero = (T.ZB[:, 0:128], T.ZB[:, 0:64], [])
+        pe, ne, pw, nw = (ID, xE, ke), (T.NI[:], xE, ke), (ID, xW, kh), (T.NI[:], xW, kh)
+        if last:
+            slots_k = [[ne], [pe, pe], [ne], [zero]]
+            slots_h = [[nw], [pw, pw], [nw], [zero]]
+        else:
+            slots_k = [[(T.NDN[:], xW, kh)], [(T.DNI[:], xW, kh)], [pe, pw], [ne]]
+            slots_h = [[ne], [(T.IUP[:], xE, ke)], [(T.UP[:], xE, ke), pw], [nw]]
+        slots_h[0].insert(0, (ID, T.MH[:], ["MH"]))
+        vs = 2 if last else 3
+
+        def slots():
+            for s in (3,) if last else (1, 2):
+                mm(sh(s), slots_h[s][0:1], ["PE%d" % (4 + s)], ["E"])
+            for s in (3, 0) if last else (1, 0):
+                mm(sk(s), slots_k[s], ["PE%d" % s], ["E"], stop=s > 0)
+
+        def slots_v():
+            tt(sh(0), T.MH[:], xW if last else xE, A.subtract, r=["MH"] + ke + kh, w=["PE4"], b=["E"])
+            if last:
+                ts(T.PE[:, 1::4], MI[:, 0:128], 2.0, -2 * MID, A.mult, A.add, r=[e_, w_], w=["PE1", "PE5"], b=["E"])
+            else:
+                tt(sk(2), xW, sk(3), A.subtract, r=kh + ["PE3"], w=["PE2"], b=["E"])
+                tt(sh(2), sh(2), xW, A.add, r=kh, w=["PE6"], b=["E"])
+
+        part[0] = ""
+        if EARLY:
+            if t > 0:
+                ts(T.EW[:], MI[:, 0:128], -MID, None, A.add, r=[e_, w_], w=["EW"])
+            if EARLY == 1:
+                slots()
+                mm(T.PA[:, 64:128], [pw], ["PA1"], ["A"])
+        cp(T.GK[:, 0:16 * GCUT], kw.indirect(eo[:, 0:GCUT]), r=kr, w=["GK0"], gather=True)
+        act(T.GK[:, 16 * GCUT:1024], kw.indirect(eo[:, GCUT:64]), r=kr, w=["GK1"], gather=True)
         mm(T.PA[:, 0:64], [(T.BM[:, 15 - r:143 - r], T.GK[:, r::16], ["BM", "GK0", "GK1"]) for r in range(16)], ["PA0"], ["A"])
-        for h in range(2):
-            act(T.FW[:, 512 * h:512 * h + 512], T.FT[:, 0:6144].indirect(MI[:, 64 + 32 * h:96 + 32 * h]), r=ft + [w_], w=["FW%d" % h])
+        if EARLY == 2:
+            slots()
+        part[0] = "slots"
+        if t > 0 and not EARLY:
+            ts(T.EW[:], MI[:, 0:128], -MID, None, A.add, r=[e_, w_], w=["EW"])
+        if t == 1:
+            arrive(["F0"], "af")
+            cp(T.F2[:], MI[:, 128:192], r=[e_], w=["F2"])
+            tt(T.F1[:], T.F0[:, 1::2], T.F2[:], A.not_equal, r=["F0", "F2"], w=["F1"])
+        elif t > 1:
+            cp(fp, MI[:, 128:192], r=[e_], w=kf)
+        part[0] = ""
+        fw = [[], []]
+        for c0, c1 in zip(FWCUT, FWCUT[1:]):
+            src = T.FT[:, 0:6144].indirect(MI[:, 64 + c0:64 + c1])
+            (cp if c0 == 0 and FWV else act)(T.FW[:, 16 * c0:16 * c1], src, r=ft + [w_], w=["FW%d" % c0], gather=True)
+            for h in range(2):
+                if c0 < 32 * h + 32 and c1 > 32 * h:
+                    fw[h].append("FW%d" % c0)
+        ts(T.UO[:], T.PA[:, 0:64], 0.5, MID, A.mult, A.add, r=["PA0"], w=["UO"], b=["A"])
+        ts(T.PE[:, vs::4], MI[:, 0:128], -1.0, MID, A.mult, A.add, r=[e_, w_], w=["PE%d" % vs, "PE%d" % (4 + vs)], b=["E"])
+        if EARLY == 2 or WC:
+            mm(T.PA[:, 64:128], [pw], ["PA1"], ["A"])
+        xs = 16 * XS
+        for h, (c0, c1) in enumerate([(0, 32), (32, XS)]):
+            tt(T.DD[:, 16 * c0:16 * c1], T.FT[:, 0:6144].indirect(T.UO[:, c0:c1]), T.FW[:, 16 * c0:16 * c1], A.subtract,
+               r=ft + ["UO"] + ["FW%d" % a for a, b in zip(FWCUT, FWCUT[1:]) if a < c1 and b > c0], w=["DD%d" % h], gather=True)
+        if XS < 64:
+            act(T.DD[:, xs:1024], T.FT[:, 0:6144].indirect(T.UO[:, XS:64]), r=ft + ["UO"], w=["FU"], gather=True)
+            mm(T.PA[:, xs - 512:512], [(T.NB[:], T.FW[:, xs:1024], fw[1]), (IB, T.DD[:, xs:1024], ["FU"])], ["PAd"], ["A"])
+        ns = NS if t > 0 else 0
+        if ns:
+            act(T.NR[:, 0:ns], T.DD[:, 0:ns], r=["DD0"], w=["NRa"], f=AF.Abs)
+            act(T.NR[:, 0:ns], T.NR[:, 0:ns], -1000.0, 16500.0, ["NRa"], ["NRa"], f=AF.Sigmoid)
+        if XS < 64:
+            ts(T.NR[:, ns:xs], T.DD[:, ns:xs], B32, B32, A.add, A.is_equal, r=["DD0", "DD1"], w=["NRb"] + ["NRa"] * (ns == 0))
+            for x in range(2):
+                ts(T.NR[:, xs + x::2], T.PA[:, xs - 512 + x:512:2], B32, B32, A.add, A.is_equal, r=["PAd"], w=["NR%d" % x], b=["A"])
+        def digits():
+            ts(T.HI[:, 0:128], T.PA[:, 0:128], 2 * B64, 2 * B64, A.add, A.subtract, r=["PA0", "PA1"], w=["HI", "HIw"], b=["A"])
+
+        if EARLY == 1:
+            digits()
+        if PAR == 2:
+            ts(T.NR[:, ns:512], T.DD[:, ns:512], B32, B32, A.add, A.is_equal, r=["DD0"], w=["NRb"] + ["NRa"] * (ns == 0))
+            ns = 512
+        for x in range(2 * (XS == 64 and PAR > 0)):
+            ts(T.NR[:, ns + x::2], T.DD[:, ns + x::2], B32, B32, A.add, A.is_equal, r=["DD0", "DD1"],
+               w=["NR%d" % x] + ["NRa"] * (ns == 0 and x == 0))
+        if XS == 64 and not PAR:
+            ts(T.NR[:, ns:1024], T.DD[:, ns:1024], B32, B32, A.add, A.is_equal, r=["DD0", "DD1"], w=["NR0", "NR1"] + ["NRa"] * (ns == 0))
+        if EARLY == 2 or WC:
+            digits()
+        part[0] = "count"
         if t > 0:
-            mm(T.PB[:, 64:128], [(T.O4[:], T.D0[:, 2::4], ["O4", "D0x"])], ["PBa"], ["B"])
-        mm(T.PB[:, 0:64], [(T.WA[:, 15 - r:143 - r], T.GK[:, r::16], ["WA", "GK0", "GK1"]) for r in range(16)], ["PB0"], ["B"])
-        ts(T.NL[:, 1::2], MI[:, 0:128], -1.0, 0.5, A.mult, A.add, r=[e_, w_], w=["NL1"])
-        ts(T.NL[:, 0::2], T.NL[:, 1::2], B2, B2, A.add, A.subtract, r=["NL1"], w=["NL0"])
-        scan(T.XX[:, 128:256], T.M2[:], T.NL[:, 128:256], r=["M2", "NL0", "NL1"], w=["XW"])
-        ts(T.UO[:], T.PA[:, 0:64], 0.5, None, A.mult, r=["PA0"], w=["UO"], b=["A"])
-        for h in range(2):
-            tt(T.DD[:, 512 * h:512 * h + 512], T.FT[:, 0:6144].indirect(T.UO[:, 32 * h:32 * h + 32]),
-               T.FW[:, 512 * h:512 * h + 512], A.subtract, r=ft + ["UO", "FW%d" % h], w=["DD%d" % h])
-        for h, (c0, c1) in enumerate([(0, 512), (512, 1024)]):
-            ts(T.NR[:, c0:c1], T.DD[:, c0:c1], B32, B32, A.add, A.is_equal, r=["DD%d" % h], w=["NR%d" % h])
-        act(T.UU[:, 0:64], T.PA[:, 0:64], 0.5, 0.5, r=["PA0"], w=["UU0"], b=["A"])
-        act(T.UU[:, 64:128], T.PA[:, 0:64], -0.5, 0.5, r=["PA0"], w=["UU1"], b=["A"])
-        act(T.AH[:], T.PB[:, 0:64], 0.5, -0.5, r=["PB0"], w=["AH"], b=["B"])
-        if t > 0:
-            act(T.CC[:, 128 * t + 1:128 * t + 128:2], T.TM[:, 1::2], r=["TM"], w=["LOC"])
-        if t > 0:
-            add("a", lambda: S.activation(T.TN[:, 0:64], T.PB[:, 64:128], AF.Copy, accum_out=col(RED)), ["PBa"], ["RED", "TN"], ["B"])
+            add("a", lambda: S.activation(T.TN[:, 0:64], T.PB[:, 256:320], AF.Identity, bias=-1.0 / 128, accum_out=col(RED)),
+                140, ["PFa"], ["RED", "TN"], ["B"])
         if t == 0:
-            act(T.Z1[:], T.B4[:], 0.5, r=["B4"], w=["Z1"])
+            ts(col(G16), T.IJ[:, 5:6], T.TA[:, 1:2], None, A.subtract, r=["IJ2", "TAo"], w=["G16"])
+            act(col(RM5), col(G16), -1.0, -2048.5, r=["G16"], w=["RM5"])
+            act(T.MH[:], T.TA[:, 1::2], -1.0, col(RM5), r=["TAo", "RM5"], w=["MH"])
+        mm(T.PG[:, 0:256], [(T.NB4[:], T.QM[:], ["QM0", "QM"])], ["PG"], ["G"], stop=False)
+        part[0] = "kids"
+        if t == 0:
+            for a in range(2):
+                mm(T.PH[:, 1 + 256 * a:256 + 256 * a:2],
+                   [(T.IB[:, 12 + 4 * (a - j):140 + 4 * (a - j)], T.KT[:, 3072 + 512 * a + j:3584 + 512 * a:4], [kts[2 * a]])
+                    for j in range(4)], ["PH1"], ["H"])
+            act(yo[:, 1::2], T.PH[:, 1::2], col(SG), r=["PH1"], w=[yok + "o"], b=["H"])
+            part[0] = "first"
+            act(T.Z1[:], T.NB4[:], -0.5, r=["NB4"], w=["Z1"])
+            act(T.WA[:], T.BM[:], col(SH), r=["BM", "SH"], w=["WA"])
             sel(T.Z1[:], T.Z1[:], [[-1, 128]], A.not_equal, 1.5, 0, 1, ["Z1"], ["Z1"])
-            add("g", lambda: g.remote_dma(T.F0[:], T.D2[:], T.sem.af, T.sem.sent, pid, rid, mask), r=["D2", "D2z"],
-                kind="rem", sem="sent", inc=n_out)
-            act(T.VW[:, 0:1024], T.FA[:, 0:1024], 1.0, BIG, r=["FA0"], w=["VW0"])
-        nE, nW = T.NL[:, 1:128:2], T.NL[:, 129:256:2]
-        xE, xW = T.XX[:, 1:128:2], T.XX[:, 129:256:2]
-        if last:
-            mm(T.PE[:, 0:256:4], [(T.ZB[:, 0:128], T.ZB[:, 0:64], [])], ["PE0"], ["E"])
-            mm(T.PG[:, 0:256:4], [(T.ZB[:, 0:128], T.ZB[:, 0:64], [])], ["PG0"], ["G"])
-        else:
-            mm(T.PE[:, 0:256:4], [(T.DI[:], xW, ["DI", "XW"])], ["PE0"], ["E"])
-        if last:
-            mm(T.PG[:, 1:256:4], [(T.I32[:], xW, ["XW"]), (T.I32[:], nW, ["NL1"])], ["PG1"], ["G"])
-        else:
-            mm(T.PE[:, 1:256:4], [(T.I32[:], xW, ["I32", "XW"]), (T.I32[:], nE, ["NL1"])], ["PE1"], ["E"])
-        mm(T.PG[:, 2:256:4], [(T.N32[:], nW, ["NL1"]), (T.N32[:], T.MH[:], ["MH"])], ["PG2"], ["G"])
-        if t == 0:
-            act(yo[:, 1::2], T.PH[:, 1::2], r=["PH1"], w=[yok + "o"], b=["H"])
+            send(T.F0[:], T.D2[:], ["D2", "RP3"], "af")
+
 
         def half_sum(h, first):
             pb, bk = (T.PC, "C") if h == 0 else (T.PD, "D")
-            lh, src, k = (T.I2, T.FW, "FW%d" % h) if first else (T.IB, T.DD, "DD%d" % h)
-            rh = src[:, 512 * h:512 * h + 512]
-            add("p", lambda: PE.matmul(pb[:], lh[:], rh, first, not first), ["I2", "IB", k], ["S%d" % h], [bk])
+            lh, src, k = (T.I2[:], T.FW, fw[h]) if first else (IB, T.DD, ["DD%d" % h])
+            if first and h == 1 and XS < 64:
+                mm(pb[:], [(lh, src[:, 512:1024], k)], ["S1"], [bk], True, False)
+                mm(pb[:, xs - 512:512], [(T.NB[:], src[:, xs:1024], k)], ["S1"], [bk], False, False)
+            else:
+                mm(pb[:], [(lh, src[:, 512 * h:512 * h + 512], k + ["FU"] * h)], ["S%d" % h], [bk], first, not first)
             if not first:
                 c0 = 1024 * (t + 1) + 512 * h
                 act(T.VW[:, c0:c0 + 512], pb[:], 0.5 - 2.0 ** -10, BIG, r=["S%d" % h], w=["VW%d_%d" % (t + 1, h)], b=[bk])
 
-        half_sum(0, True)
-        half_sum(0, False)
-        act(T.PE[:, 3:256:4], T.AH[:], r=["AH"], w=["PE3"], b=["E"])
-        for hh in range(2):
-            mm(T.PF[:, 64 * hh:64 * hh + 64],
-               [(T.I32[:], xW, ["XW"]), (T.I32[:], T.UU[:, 64 * hh:64 * hh + 64], ["UU%d" % hh])], ["PF%d" % hh], ["F"])
-        half_sum(1, True)
-        half_sum(1, False)
-        mm(T.PA[:, 64:128], [(T.B4[:], T.Q9[:], ["Q9"])] * (t > 0)
-           + [(T.BM[:, 15 - r:143 - r], T.NR[:, r::16], ["NR0", "NR1"]) for r in range(16)], ["PA1"], ["A"])
-        if t > 0:
-            ts(col(RND), col(RED), B2, B2, A.add, A.subtract, r=["RED"], w=["RND"])
-        scan(T.XX[:, 0:128], T.M2[:], T.NL[:, 0:128], r=["M2", "NL0", "NL1"], w=["XE"])
-        if t > 0:
-            ts(col(THR), col(RED), col(RND), 1000.0, A.is_equal, A.mult, r=["RED", "RND"], w=["THR"])
-        ts(T.HI[:, 0:128], T.PF[:, 0:128], B64, B64, A.add, A.subtract, r=["PF0", "PF1"], w=["HI", "HIa"], b=["F"])
-        if t == 1:
-            cp(T.D3[:], MI[:, 128:192], r=[f_], w=["D3"])
-        else:
-            cp(T.D0[:, 1::4], MI[:, 128:192], r=[f_], w=["D0f"])
-        if t == 0:
-            ts(T.SP[:], T.PA[:, 64:128], 9.0, None, A.is_ge, r=["PA1"], w=["SP"], b=["A"])
-        tt(T.LO[:, 0:128], T.PF[:, 0:128], T.HI[:, 0:128], A.subtract, r=["PF0", "PF1", "HI"], w=["LO", "LOa"], b=["F"])
-        if t == 1:
-            add("g", None, w=["F0"], kind="arr", sem="af", inc=n_in)
-            tt(T.D0[:, 1::4], T.F0[:, 1::2], T.D3[:], A.not_equal, r=["F0", "D3"], w=["D0f"])
-        if t == 0:
-            cp(T.K1F[:], T.K1[:], r=["K1"], w=["KF1"])
-            dma("s", T.y0[:, 0:2048], T.K0F[:], r=["KF0", "KF1"])
-            dma("s", T.y1[:, 0:2048], T.K1F[:], r=["KF1"])
-        else:
-            step(T.SP[:], T.PA[:, 64:128], 1000.0, col(THR), ["PA1", "THR"], ["SP"], ["A"])
-        if last:
-            mm(T.PE[:, 1:256:4], [(T.I32[:], xE, ["I32", "XE"]), (T.I32[:], nE, ["NL1"])], ["PE1"], ["E"])
-        else:
-            mm(T.PG[:, 1:256:4], [(T.UP[:], xE, ["UP", "XE"]), (T.I32[:], nW, ["NL1"])], ["PG1"], ["G"])
-        if t == 0:
-            mm(T.PA[:, 128:256:2], [(T.Z1[:], T.SP[:], ["Z1", "SP"])], ["PA2"], ["A"])
-        mm(T.PA[:, 129:256:2], [(T.Z1[:], T.SP[:], ["Z1", "SP"])], ["PA3"], ["A"])
-        mm(T.PB[:, 128:192], [(T.B4[:], T.SP[:], ["B4", "SP"])], ["PB2"], ["B"])
-        if t > 0:
-            mm(T.PB[:, 192:256], [(T.Z1[:], T.SP[:], ["Z1", "SP"])], ["PB3"], ["B"])
-        mm(T.PE[:, 2:256:4], [(T.N32[:], nE, ["N32", "NL1"]), (T.N32[:], T.AH[:], ["AH"])], ["PE2"], ["E"])
-        if not last:
-            mm(T.PG[:, 0:256:4], [(T.IU[:], xE, ["IU", "XE"])], ["PG0"], ["G"])
-        cc = T.CC[:, 128 * t:128 * t + 128]
-        add("v", lambda cc=cc: V.tensor_tensor_scan(T.TM[:], T.PA[:, 128:256], cc, 0.0, A.min, A.max),
-            ["PA2", "PA3", "CC", "LOC"], ["TM", "TM2"], ["A"])
-        if t == 0:
-            ts(T.D0[:, 3::4], T.PA[:, 129:256:2], 2.0, None, A.is_lt, r=["PA3"], w=["D0g"], b=["A"])
-        ts(T.LC[:], T.TM[:, 1::2], KS, -float(C0), A.mult, A.add, r=["TM"], w=["LC"])
-        if t == 0:
-            ts(T.D0[:, 2::4], T.PB[:, 128:192], 2.0, None, A.is_lt, r=["PB2"], w=["D0x"], b=["B"])
-        else:
-            step(T.D0[:, 3::4], T.PB[:, 192:256], -1000.0, 1750.0, ["PB3", "PB2"], ["D0g"], ["B"])
-            step(T.D0[:, 2::4], T.PB[:, 128:192], -1000.0, 1500.0, ["PB2"], ["D0x"], ["B"])
-
         def y_cands():
-            for q in range(4):
-                terms = [(T.NB[:], yo[:, 1 + 2 * q::8], ["NB", yok + "o"])]
-                for dd in range(4):
-                    rh, rr = digit(dd, 64)
-                    terms.append((T.W2[:, 144 * q + 12 - 4 * dd:144 * q + 140 - 4 * dd], rh, rr + ["W2%d" % q]))
-                mm(T.PF[:, 256 + q:512:4], terms, ["PY%d" % q], ["F"])
-            if 0 < t < RO - 1:
-                mm(T.PA[:, 256:320], [(T.IB[:], T.D0[:, 1::4], ["D0f"]), (T.IB[:], T.D0[:, 2::4], ["D0x"])], ["PA4"], ["A"])
-            for q in range(4):
-                mm(T.PH[:, 1 + 2 * q::8], [(T.B4[:], T.Q4[:, 0:64], ["Q4"]),
-                                           (T.RP[:, 128 * q:128 * q + 128], T.D0[:, 3::4], ["RP%d" % q, "D0g"])], ["PH1"], ["H"])
+            mm(T.PF[:, 256:512], [(T.NB[:], yo[:, 1::2], [yok + "o"])], ["PY"], ["F"], stop=False)
+            for wt, c, z in ((T.WW, 64, "w"), (T.WU, 0, "")):
+                for x, src in enumerate([T.HI, T.LO]):
+                    for q in range(4):
+                        c0 = q + 4 - 4 * x
+                        mm(T.PF[:, 256 + q:512:4], [(wt[:, c0:c0 + 509:4], src[:, c:c + 64], [src.name + z, "%s%d" % (wt.name, q)])],
+                           ["PY"], ["F"], start=False, stop=(c, x, q) == (0, 1, 3))
+            if YD == 0:
+                y_diff()
 
         def y_diff():
-            act(yo[:, 0::2], T.PF[:, 256:512], r=["PY0", "PY1", "PY2", "PY3"], w=[yok + "e"], b=["F"])
+            act(yo[:, 0::2], T.PF[:, 256:512], r=["PY"], w=[yok + "e"], b=["F"])
+            if YD == 2:
+                cp(yo[:, 0::2], T.PF[:, 256:512], r=["PY"], w=[yok + "e"], b=["F"])
+                either()
+
+        def sums():
+            for first in (True, False):
+                for h in range(2):
+                    half_sum(h, first)
+
+        if SUMS == 0 or last:
+            sums()
+        part[0] = "first"
+        if t == 0:
+            act(T.ZK[:], T.Z1[:], KS, r=["Z1"], w=["ZK"])
+        part[0] = ""
+        mm(T.PB[:, 0:64], [(T.NB4[:], T.Q9[:], ["Q9"])] * (t > 0)
+           + [(T.BM[:, 15 - r:143 - r], T.NR[:, r::16], ["NRa", "NRb", "NR%d" % x]) for x in range(2) for r in range(x, 16, 2)],
+           ["PB0"], ["B"])
+        if SUMS == 1:
+            sums()
+        part[0] = "spare"
+        if t == 3:
+            act(T.KF[:], T.E5[:, 0:256], 1.0, -0.5, r=["E5"], w=["KF"])
+            dma("s", T.y0[:, 0:2048], T.KF[:, 0:128], r=["KF", "DD0"])
+            dma("s", T.y1[:, 0:2048], T.KF[:, 128:256], r=["KF", "DD0"])
+        if t in (1, 2):
+            dma("s", T.yx[:, 1024 * t - 1024:1024 * t], T.FT[:, 2048 + 1024 * t:3072 + 1024 * t], r=["DD0"])
+        if t in (1, 2):
+            k = t - 1
+            for j in range(4):
+                act(T.WK[:, 68 * j + 32 * k + 3:68 * j + 32 * k + 32:4], T.WA[:, 15:128:16], T.MK[:, 4 + j:5 + j],
+                    r=["WA", "WK"], w=["WK%d%d" % (j, k)], f=AF.Identity if k else AF.Abs)
+        part[0] = "slots"
+        if t > 0:
+            ts(col(RND), col(RED), B2, B2, A.add, A.subtract, r=["RED"], w=["RND"])
+        part[0] = ""
+        if t == 0:
+            ts(T.SP[:], T.PB[:, 0:64], 9.0, None, A.is_ge, r=["PB0"], w=["SP"], b=["B"])
+        else:
+            ts(T.SP[:], T.PB[:, 0:64], col(RND), col(RED), A.add, A.is_ge, r=["PB0", "RND", "RED"], w=["SP"], b=["B"])
+        mm(T.PG[:, 3 if last else 2:256:4], [(T.I3[:], fp, ["I3"] + kf)], ["PG"], ["G"], start=False, stop=False)
+        mm(T.PG[:, 1:256:4], [(T.Z1[:], T.SP[:], ["Z1", "SP"])], ["PG"], ["G"], start=False, stop=False)
+        if not last:
+            mm(T.PG[:, 2:256:4], [(T.Z1[:], T.SP[:], [])], ["PG"], ["G"], start=False, stop=False)
+        mm(T.PG[:, 2 if last else 3:256:4], [(T.ZM[:], T.SP[:], ["ZM"])], ["PG"], ["G"], start=False)
+        mm(T.PB[:, 129:256:2], [(T.ZK[:], T.SP[:], ["ZK", "SP"])], ["PBz"], ["B"])
+        step(T.D0[:], T.PG[:, 0:256], 1.75, ["PG"], ["D0"], ["G"])
+
+        def scan_k():
+            scan(T.SE[:, 0:256], T.D0[:], T.PE[:, 0:256], r=["D0", "PE0", "PE1", "PE2", "PE3"], w=["SE", "SW", "SEj"], b=["E"])
+
+        def scan_h():
+            scan(T.SE[:, 256:512], T.D0[:], T.PE[:, 256:512], r=["D0", "PE4", "PE5", "PE6", "PE7"], w=["SH2"], b=["E"])
+
+        def versions():
+            (ti, tik), (to, tok) = tbuf[t % 2], tbuf[(t + 1) % 2]
+            scan(to[:], T.PB[:, 128:256], ti[:], ["PBz", tik + "e", tik + "o"], [tok + "e", tok + "o"], ["B"], A.min, A.max)
+            ts(T.LC[:], to[:, 1::2], col(G16), None, A.add, r=[tok + "o", "G16"], w=["LC"])
+            return to, tok
+
+        mm(T.PB[:, 320:384], [(T.I3[:], fp, kf)] * (t > 0) + [(T.NB4[:], T.SP[:], ["SP"])], ["PBf"], ["B"])
+        if last or TMF == 1:
+            to, tok = versions()
+        if not EARLY:
+            slots()
+        slots_v()
+        mm(sk(0), [(T.WA[:, 15 - r:143 - r], T.GK[:, r::16], ["GK0", "GK1"]) for r in range(16)], ["PE0"], ["E"], start=False)
+        if not EARLY and not WC:
+            mm(T.PA[:, 64:128], [pw], ["PA1"], ["A"])
+        if not last:
+            u = t + 1
+            MO = T["MO%d" % u]
+            if t == 0:
+                ts(MO[:, 128:192], T.PB[:, 320:384], -1.5, None, A.is_ge, r=["PBf"], w=["GO%d" % u], b=["B"])
+            else:
+                ts(MO[:, 128:192], T.PB[:, 320:384], B4, B4, A.add, A.is_equal, r=["PBf"], w=["GO%d" % u], b=["B"])
+            scan_h()
+            if TMF == 2:
+                to, tok = versions()
+            scan_k()
+            if MO2:
+                ts(MO[:, 64:128], T.SE[:, 259::4], -1.0, MID, A.mult, A.add, r=["SH2"], w=["MOw%d" % u])
+                ts(MO[:, 0:64], T.SE[:, 3:256:4], -1.0, MID, A.mult, A.add, r=["SE"], w=["MOe%d" % u])
+            else:
+                ts(MO[:, 0:128], T.SE[:, 3::4], -1.0, MID, A.mult, A.add, r=["SE", "SH2"], w=["MOe%d" % u])
+            send(T["MI%d" % u][:], MO[:], ["MOw%d" % u, "MOe%d" % u, "GO%d" % u], "ae%d" % u)
+            if not TMF:
+                to, tok = versions()
+            iota(to[:, 0::2], [[16, 64]], C0 + 1024 * (t + 2), 1, [tok + "e"])
+        if SUMS == 2 and not last:
+            sums()
+        if not EARLY and not WC:
+            digits()
+        tt(T.LO[:, 0:128], T.PA[:, 0:128], T.HI[:, 0:128], A.subtract, r=["PA0", "PA1", "HI"], w=["LO", "LOw"], b=["A"])
+        y_cands()
+        for q in range(4):
+            mm(T.PH[:, 1 + 2 * q::8], [(T.RP[:, 128 * q:128 * q + 128], T.D0[:, 1::4], ["RP%d" % q, "D0"])], ["PH1"], ["H"])
 
         def y_scan():
             scan(yn[:], T.PH[:], yo[:], r=["PH0", "PH1", yok + "e", yok + "o"], w=[ynk + "e", ynk + "o"], b=["H"])
 
-        if last:
-            y_cands()
-            y_diff()
-        d0 = ["D0z", "D0f", "D0x", "D0g"]
-        scan(T.SE[:, 0:256], T.D0[:], T.PE[:, 0:256], r=d0 + ["PE0", "PE1", "PE2", "PE3"], w=["SE", "SE2"], b=["E"])
-
-        def send(c0, c1, key, sem):
-            src, dst = T["MO%d" % (t + 1)][:, c0:c1], T["MI%d" % (t + 1)][:, c0:c1]
-            rs = T.sem[sem]
-            add("g", lambda: g.remote_dma(dst, src, rs, T.sem.sent, pid, rid, mask), r=key, kind="rem", sem="sent", inc=n_out)
-
-        if not last:
-            y_cands()
-            ts(T["MO%d" % (t + 1)][:, 0:64], T.SE[:, 3:256:4], 0.5, None, A.add, r=["SE"], w=["MOe%d" % t])
-            send(0, 64, ["MOe%d" % t], "ae%d" % (t + 1))
-            scan(T.SE[:, 256:512], T.D0[:], T.PG[:, 0:256], r=d0 + ["PG0", "PG1", "PG2", "PG3"], w=["SW"], b=["G"])
-        vw = ["VW0"] + ["VW%d_%d" % (k + 1, h) for k in range(t + 1) for h in range(2)]
-        win = T.VW[:, 0:1024 * (t + 2)]
-        cut = 32 if last else CUT
-        for h, (c0, c1) in enumerate([(0, cut), (cut, 64)]):
-            out = T.YX[:, 16 * c0:16 * c1] if last else T.FT[:, 4096 + 32 * c0:4096 + 32 * c1:2]
-            act(out, win.indirect(T.LC[:, c0:c1]), 1.0, -BIG, r=vw + ["LC"], w=[("YX%d" if last else "FTd%d") % h])
-            if last:
-                dma("s", T.yx[:, 2048 + 16 * c0:2048 + 16 * c1], out, r=["YX%d" % h])
-            elif h == 0:
-                y_diff()
-        if last:
-            scan(T.SE[:, 256:512], T.D0[:], T.PG[:, 0:256], r=d0 + ["PG0", "PG1", "PG2", "PG3"], w=["SW"], b=["G"])
-        if not last:
-            if t == 0:
-                cp(T.MO1[:, 128:192], T.D0[:, 2::4], r=["D0x"], w=["MOf0"])
-            else:
-                ts(T["MO%d" % (t + 1)][:, 128:192], T.PA[:, 256:320], 1.0, None, A.is_equal, r=["PA4"], w=["MOf%d" % t], b=["A"])
-            ts(T["MO%d" % (t + 1)][:, 64:128], T.SE[:, 259::4], 0.5, None, A.add, r=["SW"], w=["MOw%d" % t])
-            send(64, 192, ["MOw%d" % t, "MOf%d" % t], "aw%d" % (t + 1))
-
-            def turn(c0, c1, r, w):
-                ts(T.FT[:, c0 + 1:c1:2], T.FT[:, c0:c1:2], -1.0, 255.0, A.mult, A.add, r=[r], w=[w])
-
-            y_scan()
-            turn(4096, 4096 + 32 * CUT, "FTd0", "FTd2")
-            for k in range(8):
-                if k == NV1:
-                    turn(4096 + 32 * CUT, 6144, "FTd1", "FTd3")
-                if k == NV:
-                    expand("v", T.KT[:, 4096 + k:5120:8], yn[:, 1:256:2], k // 2, k % 2, [ynk + "o"], [ktd[8]])
-                    expand("a", T.KT[:, 5120 + k::8], yn[:, 257::2], k // 2, k % 2, [ynk + "o"], [ktd[k]])
-                else:
-                    expand("v" if k < NV else "a", T.KT[:, 4096 + k::8], yn[:, 1::2], k // 2, k % 2, [ynk + "o"], [ktd[k]])
         if t == 0:
-            dma("s", T.yx[:, 0:2048], T.FA[:], r=["FA0", "FA1", "FW1"])
-            sel(T.O4[:], T.ZB[:, 0:128], [[0, 128]], A.not_equal, 0.25, 0, 0, ["Z"], ["O4"])
-            sel(T.Q9[:], T.ZB[:, 0:64], [[0, 64]], A.not_equal, -2.375, 0, 0, ["Z"], ["Q9"])
-            iota(T.WO[:], [[0, 144]], 0, 0, ["WO"])
-            for c0 in (14, 15):
-                wo = T.WO[:, c0::16]
-                sel(wo, T.ZB[:, 0:9], [[0, 9]], A.not_equal, -0.5, 0, 0, ["Z"], ["WO"])
-                if c0 == 14:
-                    sel(wo, wo, [[-16, 9]], A.is_ge, 0.5, -8, 1, ["WO"], ["WO"])
-                sel(wo, wo, [[-16, 9]], A.is_ge, 0.0, 0, 1, ["WO"], ["WO"])
-                sel(wo, wo, [[16, 9]], A.is_ge, 0.0, 15, -1, ["WO"], ["WO"])
-            sel(T.Q8[:], T.ZB[:, 0:128], [[0, 128]], A.not_equal, 0.125, 0, 0, ["Z"], ["Q8"])
+            for h in range(2):
+                act(T.VW[:, 512 * h:512 * h + 512], T.FT[:, 3072 + 512 * h:3584 + 512 * h], 1.0, BIG, r=["FTa"], w=["VW0_%d" % h])
+        vw = ["VW%d_%d" % (k, h) for k in range(t + 2) for h in range(2)]
+        win = T.VW[:, 0:1024 * (t + 2)]
+
+        cut = FCUT[last]
+
+        def faces(h):
+            c0, c1 = cut[h], cut[h + 1]
+            if c0 == c1:
+                return
+            out = T.YX[:, 16 * c0:16 * c1] if last else T.FT[:, 5120 + 16 * c0:5120 + 16 * c1]
+            src, key = win.indirect(T.LC[:, c0:c1]), [("YX%d" if last else "FTe%d") % h]
+            if h < 2:
+                act(out, src, 1.0, -BIG, r=vw + ["LC"], w=key, gather=True)
+            elif c1 > c0:
+                ts(out, src, -BIG, None, A.add, r=vw + ["LC"], w=key, gather=True)
+            if last and c1 > c0:
+                dma("s", T.yx[:, 2048 + 16 * c0:2048 + 16 * c1], out, r=key)
+
+        def turn(h):
+            c0, c1 = (0, 16 * cut[1]) if h == 0 else (16 * cut[1], 1024)
+            ts(T.FT[:, rev(1023 - c0, c1 - c0, 1)], T.FT[:, 5120 + c0:5120 + c1], -1.0, 255.0, A.mult, A.add,
+               r=["FTe0"] if h == 0 else ["FTe1", "FTe2"], w=["FTo%d" % h], stepped=H5 >= 2)
+
+        if last:
+            break
+        if t == 0:
+            const(T.O4[:], 0.25, ["O4"])
+            const(T.N4[:], -0.25, ["N4"])
+            const(T.Q9[:], 2.25, ["Q9"])
+        mm(T.PB[:, 256:320], [(T.O4[:], T.D0[:, 3:256:4], ["D0"]), (T.N4[:], T.D0[:, 1:256:4], [])], ["PFa"], ["B"])
+        faces(0)
+        if YD:
+            y_diff()
+        y_scan()
+        faces(1)
+        faces(2)
+        for k in range(8):
+            j, tn = k // 2, k % 2
+            out = T.KT[:, rev(1023 - j, 256, 4)] if tn else T.KT[:, 5120 + j::4]
+            expand(out, yn[:, 1::2], j, tn, [ynk + "o"], [ktd[k]])
+            if k == 1:
+                turn(0)
+        turn(1)
+        part[0] = "const"
+        if t == 0:
             point(T.FQ[:], T.ZB[:, 0:32], [[-4, 4], [-16, 8]], 0, 1.0, ["FQ"])
+            iota(T.ZF[:], [[0, 128]], 0, 0, ["ZF"])
         if t in (1, 2):
             h = t - 1
             p3, p2 = [[-16, 8], [-1, 8], [-1000, 2]], [[-16, 8], [-1, 8]]
@@ -550,37 +754,41 @@ def rank_program(g, core, T, topo):
             sel(T.RR[:, c[3]:c[3] + 128:2], T.ZF[:, 0:64], p2, A.not_equal, 1.0, 1 - 8 * h, 1, ["ZF"], [key[3]])
             sel(T.RR[:, c[3]:c[3] + 128:8], T.ZF[:, 0:16], [[-16, 8], [-4, 2]], A.not_equal, 1.0, -3 - 8 * h, 1, ["ZF"], [key[3]])
             sel(T.RR[:, c[3] + 1:c[3] + 128:2], T.ZF[:, 0:64], p2, A.not_equal, -1.0, -8 * h, 1, ["ZF"], [key[3]])
+        if t == RO - 2:
+            const(T.QM[:, 3::4], 0.0, ["QM"])
+            const(T.QM[:, 2::4], -0.8125, ["QM"])
 
-    eh, wh = T.SE[:, 3:256:4], T.SE[:, 259:512:4]
-    tt(T.NL[:, 0:64], eh, T.D0[:, 1::4], A.mult, r=["SE", "D0f"], w=["NL0", "NL1"])
+    part[0] = ""
+    faces(0)
+    if YD:
+        y_diff()
+    faces(1)
+    ts(T.F2[:], T.PB[:, 320:384], B4, B4, A.add, A.is_equal, r=["PBf"], w=["F2"], b=["B"])
+    scan_k()
+    scan_h()
     y_scan()
-    tt(T.NL[:, 64:128], wh, T.D0[:, 1::4], A.mult, r=["SW", "D0f"], w=["NL2"])
+    faces(2)
+    srcs = [(0, T.SE[:, 2:256:4], "SE"), (2, T.SE[:, 3:256:4], "SE"), (1, T.SE[:, 258::4], "SH2"), (3, T.SE[:, 259::4], "SH2")]
+    back = [(T.PB, "B"), (T.PD, "D")]
+    for z in range(2):
+        for h, (pb, bk) in enumerate(back):
+            mm(pb[:, 256:320], [(T.RR[:, 128 * (4 * h + k):128 * (4 * h + k) + 128], rh, ["RR%d" % (4 * h + k), rk])
+                                for k, rh, rk in srcs[2 * z:2 * z + 2]], ["PBo%d" % h], [bk], z == 0, z == 1)
+    for h, (pb, bk) in enumerate(back):
+        act(T.OB[:, h::2], pb[:, 256:320], -2.0, -0.5, r=["PBo%d" % h], w=["OB%d" % h], b=[bk], f=AF.Abs)
+
     for j in range(4):
-        expand("v", T.GK[:, j::4], yn[:, 1::2], j, 0, [ynk + "o"], ["GX%d" % j] + ["GK0", "GK1"] * (j == 0))
-    tt(T.D3[:], T.D0[:, 1::4], T.D0[:, 2::4], A.not_equal, r=d0, w=["D3"])
-    back = [[(T.RR[:, 128 * (4 * h + k):128 * (4 * h + k) + 128], rh, ["RR%d" % (4 * h + k), rk])
-             for k, (rh, rk) in enumerate([(eh, "SE"), (wh, "SW"), (T.NL[:, 0:64], "NL1"), (T.NL[:, 64:128], "NL2")])]
-            for h in range(2)]
-    for h, (pb, bk) in enumerate([(T.PB, "B"), (T.PD, "D")]):
-        for i in range(3):
-            lh, rh, r = back[h][i]
-            add("p", lambda pb=pb, lh=lh, rh=rh, i=i: PE.matmul(pb[:, 256:320], lh, rh, i == 0, False), r, ["PBo%d" % h], [bk])
-    for h, (pb, bk) in enumerate([(T.PB, "B"), (T.PD, "D")]):
-        lh, rh, r = back[h][3]
-        add("p", lambda pb=pb, lh=lh, rh=rh: PE.matmul(pb[:, 256:320], lh, rh, False, True), r, ["PBo%d" % h], [bk])
-    gx = ["GX%d" % j for j in range(4)]
-    mm(T.PC[:, 0:128], [(T.B4[:], T.Q8[:], ["Q8"])]
-       + [(T.WO[:, 14 - 2 * ib:142 - 2 * ib], T.GK[:, 128 * ib:128 * ib + 128], ["WO"] + gx) for ib in range(8)], ["PC0"], ["C"])
+        mm(T.PF[0:64, j:256:4], [(T.WK[:, 68 * j + 3 - ib:68 * j + 67 - ib], yn[:, 1 + 128 * ib:128 + 128 * ib:2],
+                                  ["WK%d0" % j, "WK%d1" % j, ynk + "o"]) for ib in range(4)], ["PK"], ["F"])
+
+    act(T.OUT[0:64, :], T.PF[0:64, 0:256], 2.0, -0.5, r=["PK"], w=["OUT"], b=["F"], f=AF.Abs)
+    ts(T.OU2[0:64, :], T.OUT[0:64, :], -0.5, None, A.add, r=["OUT"], w=["OU2"])
+    dma("s", T.y0[:, 2048:3072], T.OU2[0:32, :], r=["OU2"])
+    dma("a", T.y1[:, 2048:3072], T.OU2[32:64, :], r=["OU2"])
     for q in range(4):
-        mm(T.PA[0:8, 256 + q:512:4], [(T.FQ[:, 8 * q:8 * q + 8], T.D3[:], ["FQ", "D3"])], ["PAf%d" % q], ["A"])
-    act(T.OB[:, 0::2], T.PB[:, 256:320], 1.0, 0.5, r=["PBo0"], w=["OB0"], b=["B"])
-    act(T.OB[:, 1::2], T.PD[:, 256:320], 1.0, 0.5, r=["PBo1"], w=["OB1"], b=["D"])
-    dma("s", T.yb[:], T.OB[:], r=["OB0", "OB1"])
-    act(T.FO[0:8, :], T.PA[0:8, 256:512], r=["PAf%d" % q for q in range(4)], w=["FO"], b=["A"])
+        mm(T.PA[0:8, 256 + q:512:4], [(T.FQ[:, 8 * q:8 * q + 8], T.F2[:], ["F2"])], ["PGf%d" % q], ["A"])
+    ts(T.OB2[:], T.OB[:], -0.5, None, A.add, r=["OB0", "OB1"], w=["OB2"])
+    dma("s", T.yb[:], T.OB2[:], r=["OB2"])
+    cp(T.FO[0:8, :], T.PA[0:8, 256:512], r=["PGf%d" % q for q in range(4)], w=["FO"], b=["A"])
     dma("s", T.yf[:], T.FO[0:8, :], r=["FO"])
-    ts(T.TM[:], T.PC[:, 0:128], B2, B2, A.add, A.subtract, r=["PC0"], w=["TM", "TM2"], b=["C"])
-    ts(T.TN[:], T.TM[:], col(AL), col(GA), A.mult, A.add, r=["TM", "AL", "GA"], w=["TN"])
-    tt(T.OUT[:], T.PC[:, 0:128], T.TN[:], A.add, r=["PC0", "TN"], w=["OUT"], b=["C"])
-    dma("s", T.y0[:, 2048:3072], T.OUT[0::2, :], r=["OUT"])
-    dma("a", T.y1[:, 2048:3072], T.OUT[1::2, :], r=["OUT"])
     emit(g, T, ops)

from concourse.mybir import AluOpType, AxisListType, ActivationFunctionType

RO = 5
F32, B16, I32, U16 = "float32", "bfloat16", "int32", "uint16"
SCRATCH = {}
for _dt, _bufs in (
    (B16, {"FT": 6144, "KT": 6144, "GK": 1024, "FW": 1024, "DD": 1024, "NR": 1024, "YX": 1024, "FB": 256, "HI": 256,
           "LO": 256, "YS": 512, "Y0": 512, "Y1": 512, "D0": 256, "D2": 128, "F0": 128, "F1": 64, "F2": 64, "N4": 128, "SP": 64, "ZB": 528,
           "ONE": 144, "NEG": 128, "ALT": 64, "HLF": 64, "MD": 128, "IB": 152, "I2": 128, "I3": 128, "NB": 128, "BM": 144,
           "WA": 144, "NB4": 128, "Z1": 128, "ZK": 128, "ZM": 128, "WD": 528, "WU": 528, "WW": 528,
           "RP": 512, "FF": 144, "FQ": 32, "QM": 256, "O4": 128, "Q9": 64, "WK": 272}),
    (F32, {"VW": 6144, "E5": 384, "KF": 256, "BF": 256, "AB": 256, "FO": 256, "SE": 512, "TA": 128, "TB": 128,
           "TN": 128, "OUT": 256, "OU2": 256, "OB": 128, "OB2": 128, "MH": 64, "MK": 8, "COL": 16, "KM": 152,
           "RM": 288, "RR": 1024, "ZF": 128, "ID": 152, "NI": 128, "NDN": 128, "UP": 128, "DNI": 128, "IUP": 128,
           "EW": 128, "UU": 64}),
    (I32, {"KI": 384, "KO": 384, "FI": 256, "IK": 8, "IJ": 8}),
    (U16, {"UO": 64, "LC": 64, "E0": 64, "MI0": 128}),
):
    for _n, _c in _bufs.items():
        SCRATCH[_n] = ("sbuf", [128, _c], _dt)
for _t in range(1, RO):
    for _n, _c, _dt in (("MI", 192, U16), ("MO", 192, U16)):
        SCRATCH["%s%d" % (_n, _t)] = ("sbuf", [128, _c], _dt)
for _b in "ABCDEFGH":
    SCRATCH["P" + _b] = ("psum", [128, 512], F32)
SEMAPHORES = (["sv", "sa", "sp", "sg", "sent", "af"] + ["d%d" % _i for _i in range(24)]
              + ["a%s%d" % (_k, _t) for _k in "e" for _t in range(1, RO)])

BIG = 1.5 * 2 ** 23
B2 = 1.5 * 2 ** 24
B4 = 1.5 * 2 ** 25 + 4
B32 = 1.5 * 2 ** 28
B64 = 1.5 * 2 ** 29
B4K = 1.5 * 2 ** 35
OFF = 12288.0
MID = 3071.5
KS, C0 = 16384.0, 24576
CYC, GATHER, PCYC, WAKE, HOP, FIRST = 0.83, 1.4, 0.5, 160, 1000, 1900
SFIX, GCUT, FWV, FWCUT, FCUT = 15, 32, False, (0, 32, 64), ((0, 32, 64, 64), (0, 32, 64, 64))
XS = 64
SUMS = 0
KB = True
BK = (0, 1)
YD = 0
EARLY = 0
PAR = 2
H5 = 0
TMF = 2
WC = True
MO2 = True
PASSES = 1
NS = 0
LAZY = ("spare",)
QSEM = {"v": "sv", "a": "sa", "p": "sp", "g": "sg"}


def order(ops):
    writers, readers, sent = {}, {}, {}
    for op in ops:
        r = op["r"] + ["#" + b for b in op["b"] if op["q"] != "p" and b != "E"]
        w = op["w"] + ["#" + b for b in op["b"] if op["q"] == "p"]
        pre = [writers[k] for k in r + w if k in writers] + [o for k in w for o in readers.get(k, [])]
        if op["kind"] == "arr":
            pre.append(sent[op["sem"]])
        if op["kind"] == "rem":
            sent[op["to"]] = op
        op["pre"], op["rest"] = [o for o in pre if o is not op], 0.0
        for k in r:
            readers.setdefault(k, []).append(op)
        for k in w:
            writers[k], readers[k] = op, []
    for op in ops:
        op["post"] = []
        op["alt"].append((op["q"], op["f"], op["ns"]))
    for op in reversed(ops):
        op["rest"] += op["ns"] + op["lat"]
        for o in op["pre"]:
            o["post"].append(op)
            o["rest"] = max(o["rest"], op["rest"] + (0 if o["q"] == op["q"] == "p" else WAKE))

    def place(back):
        busy = {q: [] for q in "vapgs"}
        for op in sorted(ops, key=lambda z: (-z["rest"], -z["n"] if back else z["n"])):
            best = None
            for q, f, ns in op["alt"]:
                t0 = max([o["end"] + (0 if o["q"] == q == "p" else WAKE) for o in op["post" if back else "pre"]] + [0.0])
                t0 += op["lat"] if back else 0
                if op["kind"] != "arr":
                    for s, e in busy[q]:
                        if t0 + ns <= s:
                            break
                        t0 = max(t0, e)
                if best is None or t0 + ns < best[0] + best[3]:
                    best = (t0, q, f, ns)
            op["at"], op["q"], op["f"], op["ns"] = best
            op["end"] = op["at"] + op["ns"] + (0 if back else op["lat"])
            if op["kind"] != "arr":
                busy[op["q"]].append((op["at"], op["at"] + op["ns"]))
                busy[op["q"]].sort()
        for op in ops:
            op["rest"] = op["end"]
        return max(op["end"] for op in ops)

    kept = None
    for op in reversed(ops):
        op["rest"] = max(o["rest"] for o in op["post"]) + 1e-6 if op["lazy"] and op["post"] else -op["n"]
    for _ in range(PASSES):
        total = place(False)
        if kept is None or total < kept[0]:
            kept = (total, [(op["at"], op["q"], op["f"], op["ns"]) for op in ops])
        place(True)
    for op, k in zip(ops, kept[1]):
        op["at"], op["q"], op["f"], op["ns"] = k
    ops.sort(key=lambda z: (z["at"], z["n"]))
    for i, op in enumerate(ops):
        op["n"] = i


def emit(g, T, ops):
    order(ops)
    queue = {"v": g.vector, "a": g.scalar, "p": g.tensor, "g": g, "s": g.sync}
    clock = {q: {} for q in queue}
    writers, readers, bank = {}, {}, {}
    seq = {}
    for op in ops:
        q, kind = op["q"], op["kind"]
        op["key"] = q if kind == "c" else op["sem"]
        seq[op["key"]] = seq.get(op["key"], 0) + 1
        op["seq"] = seq[op["key"]]
        deps = []
        for r in op["r"]:
            deps += [(o, True) for o in writers.get(r, [])]
        for w in op["w"]:
            deps += [(o, True) for o in writers.get(w, []) + readers.get(w, [])]
        for b in op["b"]:
            deps += [(o, False) for o in bank.get(b, {}).values()]
        need = {}
        if kind != "arr":
            for o, data in deps:
                if kind == "c" and o["kind"] == "c" and o["q"] == q and (not data or q == "p"):
                    continue
                if clock[q].get(o["key"], 0) < o["seq"] and (o["key"] not in need or need[o["key"]]["seq"] < o["seq"]):
                    need[o["key"]] = o
            waits = []
            for o in sorted(need.values(), key=lambda z: -z["n"]):
                if clock[q].get(o["key"], 0) >= o["seq"]:
                    continue
                waits.append(o)
                o["used"] = True
                for k, s in o["clk"].items():
                    clock[q][k] = max(clock[q].get(k, 0), s)
            op["waits"] = waits
            op["clk"] = dict(clock[q])
        else:
            op["clk"] = {}
        op["clk"][op["key"]] = op["seq"]
        for r in op["r"]:
            readers.setdefault(r, []).append(op)
        for w in op["w"]:
            writers[w] = [op]
            readers[w] = []
        for b in op["b"]:
            bank.setdefault(b, {})[q] = op
    count = {}
    for op in ops:
        kind = op["kind"]
        if kind == "c":
            if op["q"] == "p" and not op.get("used"):
                continue
            s = QSEM[op["q"]]
            count[s] = count.get(s, 0) + 1
            op["done"] = (s, count[s])
        else:
            count[op["sem"]] = count.get(op["sem"], 0) + op["inc"]
            op["done"] = (op["sem"], count[op["sem"]])
    for op in ops:
        if op["kind"] == "arr":
            continue
        e = queue[op["q"]]
        for o in op["waits"]:
            e.wait_ge(T.sem[o["done"][0]], o["done"][1])
        ins = op["f"]()
        if op["kind"] == "c" and "done" in op:
            ins.then_inc(T.sem[op["done"][0]], 1)
        elif op["kind"] == "dma":
            ins.then_inc(T.sem[op["sem"]], 16)
    for s in count:
        g.wait_ge(T.sem[s], count[s])


def rank_program(g, core, T, topo):
    rank = T.rank_of(core)
    if rank is None:
        return
    n = len(T.cores)
    nxt = T.cores[(rank + 1) % n]
    prv = T.cores[(rank - 1) % n]
    rid, pid = topo.addr(nxt, core)
    mask = topo.mask(core, nxt)
    n_out, n_in = len(topo.engines(core, nxt)), len(topo.engines(prv, core))
    A, AF = AluOpType, ActivationFunctionType
    V, S, PE = g.vector, g.scalar, g.tensor
    ops, nd, part = [], [0], [""]

    def add(q, f, ns, r=(), w=(), b=(), kind="c", sem=None, inc=0, lat=0.0, to=None):
        ops.append({"q": q, "f": f, "r": list(r), "w": list(w), "b": list(b), "kind": kind, "sem": sem, "inc": inc,
                    "n": len(ops), "ns": ns, "lat": lat, "to": to, "alt": [], "lazy": part[0] in LAZY})

    def either():
        o = ops.pop()
        ops[-1]["alt"].append((o["q"], o["f"], o["ns"]))

    wide = lambda *aps: any(SCRATCH[a.name][2] in (F32, I32) for a in aps)

    def vns(out, per, gather=False):
        return 50 + CYC * (GATHER * out.shape[1] if gather else max(64, per * out.shape[1]))

    def dma(q, out, in_, r=(), w=()):
        e = {"s": g.sync, "a": g.scalar}[q]
        add(q, lambda: e.dma_start(out, in_), 50, r, w, kind="dma", sem="d%d" % nd[0], inc=16, lat=1600 + out.shape[1])
        nd[0] += 1

    def send(dst, src, r, sem):
        add("g", lambda: g.remote_dma(dst, src, T.sem[sem], T.sem.sent, pid, rid, mask), FIRST if sem == "af" else 1200, r=r,
            kind="rem", sem="sent", inc=n_out, lat=HOP, to=sem)

    def arrive(w, sem):
        add("g", None, 1, w=w, kind="arr", sem=sem, inc=n_in)

    def ts(out, in0, s1, s2, o0, o1=None, r=(), w=(), b=(), gather=False, stepped=False):
        ns = vns(out, 1 if gather or stepped or wide(out, in0) else 0.5, gather)
        if o1 is None:
            add("v", lambda: V.tensor_scalar(out, in0, s1, None, o0), ns, r, w, b)
        else:
            add("v", lambda: V.tensor_scalar(out, in0, s1, s2, o0, o1), ns, r, w, b)

    def tt(out, in0, in1, o, r=(), w=(), b=(), gather=False):
        psum = any(SCRATCH[a.name][0] == "psum" for a in (out if gather else in0, in1))
        add("v", lambda: V.tensor_tensor(out, in0, in1, o), vns(out, 1 if psum else 2, gather), r, w, b)

    def cp(out, in_, r=(), w=(), b=(), gather=False):
        add("v", lambda: V.tensor_copy(out, in_), vns(out, 1, gather), r, w, b)

    def ms(ap, val, w=(), b=()):
        add("v", lambda: V.memset(ap, val), vns(ap, 1 if wide(ap) else 0.5), (), w, b)

    def scan(out, d0, d1, r=(), w=(), b=(), o0=A.mult, o1=A.add):
        add("v", lambda: V.tensor_tensor_scan(out, d0, d1, 0.0, o0, o1), vns(out, 1 if wide(out, d0, d1) else 0.5), r, w, b)

    def act(out, in_, scale=1.0, bias=0.0, r=(), w=(), b=(), f=None, gather=False, more=0):
        ns = (15 if gather else SFIX) + more + vns(out, 1, gather)
        if f is None:
            f = AF.Copy if isinstance(bias, float) and bias == 0.0 else AF.Identity
        if f == AF.Copy:
            add("a", lambda: S.activation(out, in_, f, scale=scale), ns, r, w, b)
        else:
            add("a", lambda: S.activation(out, in_, f, bias=bias, scale=scale), ns, r, w, b)

    def step(out, in_, thr, r, w, b=(), more=0):
        act(out, in_, 1000.0, -1000.0 * thr, r, w, b, AF.Sigmoid, more=more)

    def mm(out, terms, w, b, start=True, stop=True):
        for i, (lh, rh, r) in enumerate(terms):
            st, sp = start and i == 0, stop and i == len(terms) - 1
            add("p", lambda lh=lh, rh=rh, st=st, sp=sp: PE.matmul(out, lh, rh, st, sp),
                PCYC * max(64, out.shape[1]) * (4 if wide(lh) else 1), r + [lh.name, "Z"], w, b)

    def iota(out, pat, base, cm, w, flt=True):
        ns = 130 + 2 * CYC * out.shape[1]
        if flt:
            add("g", lambda: g.iota(out, pat, base, cm, allow_small_or_imprecise_dtypes=True), ns, (), w)
        else:
            add("g", lambda: g.iota(out, pat, base, cm), ns, (), w)

    def sel(out, in_, pat, op, fill, base, cm, r, w):
        add("g", lambda: g.affine_select(out, in_, pat, op, fill, base, cm), 170 + 2 * CYC * out.shape[1], r, w)

    def point(out, zero, pat, base, val, w):
        sel(out, zero, pat, A.not_equal, val, base, 1, ["Z", "ZF"], w)

    def const(out, val, w):
        c = out.shape[1]
        sel(out, T.ZB[:, 0:c], [[0, c]], A.not_equal, val, 0, 0, ["Z"], w)

    def band(out, src, pat, base, width, w):
        cols = pat[0][1] * pat[1][1]
        sel(out, src[:, 0:cols], pat, A.is_ge, 0.0, base, 1, [src.name], w)
        sel(out, out, [[-s, c] for s, c in pat], A.is_ge, 0.0, width - 1 - base, -1, w, w)

    def rev(hi, cnt, st):
        lo = hi - cnt * st
        return slice(hi, lo if lo >= 0 else None, -st)

    col = lambda j: T.COL[:, j:j + 1]
    SG, SH, G16, RM5, RED, RND, YB, YH = range(8)

    dma("s", T.KI[:, 0:128], T.kid0[:], w=["K0"])
    dma("a", T.KI[:, 128:256], T.kid1[:], w=["K1"])
    dma("s", T.KI[:, 256:384], T.belts[:], w=["BI"])
    dma("a", T.FI[0:8, :], T.flip[:], w=["FI"])
    dma("s", T.FT[:, 3072:4096], T.faces[:, 0:1024], w=["FTa"])
    dma("s", T.FT[:, 4096:5120], T.faces[:, 1024:2048], w=["FTb"])
    dma("s", T.FT[:, 5120:6144], T.faces[:, 0:1024], r=["FTa"], w=["FTe0", "FTe1", "FTe2"])

    ms(T.ZB[:], 0.0, ["Z"])
    iota(T.IK[:, 0:4], [[-4, 4]], 16, 1, ["IK"], False)
    iota(T.KM[:], [[-1, 152]], 12, 1, ["KM"])
    point(T.WD[:], T.ZB[:], [[-4, 33], [-1000, 4], [-1, 4]], 3000, 1.0, ["WD"])
    step(col(RED), T.ZB[:, 0:1], 1.0, ["Z"], ["RED", "LUT"], more=1300)
    ms(T.ONE[:], 1.0, ["ONE"])
    ms(T.NEG[:], -1.0, ["NEG"])
    ms(T.HLF[:], 0.5, ["HLF"])
    for z, keys, after in ((T.QM, ["QM", "QM0"], "BI"), (T.WU, ["WU%d" % q for q in range(4)], "BI"),
                           (T.WW, ["WW%d" % q for q in range(4)], "BI"), (T.WK, ["WK"], "FTe0")):
        dma("s", z[:], T.ZB[:, 0:z.shape[1]], r=["Z", after], w=keys)
    point(T.RM[:], T.ZB[:, 0:288], [[-16, 9], [-1000, 2], [-1, 16]], 1000, 1.0, ["RM"])
    point(T.FF[0:8, :], T.ZB[0:8, 0:144], [[-1, 9], [-1000, 4], [0, 4]], 3000, 1.0, ["FF"])
    iota(T.D2[:, 0::2], [[0, 64]], 0, 0, ["D2z"])
    band(T.BM[:], T.ONE, [[-16, 9], [1000, 16]], -15000, 16, ["BM"])
    sel(T.MD[:], T.ZB[:, 0:128], [[0, 64], [1, 2]], A.is_equal, -0.5, 0, 0, ["Z"], ["MD"])
    ID, IB, KM = T.ID[:, 12:140], T.IB[:, 12:140], T.KM[:, 12:140]

    ts(T.IJ[:, 0:4], T.IK[:, 0:4], 12, None, A.bitwise_and, r=["IK"], w=["IJ0"])
    ts(T.IJ[:, 4:5], T.IK[:, 0:1], 2, None, A.bitwise_and, r=["IK"], w=["IJ1"])
    ts(T.IJ[:, 5:6], T.IK[:, 0:1], 15, None, A.bitwise_and, r=["IK"], w=["IJ2"])
    ts(T.IJ[:, 7:8], T.IK[:, 0:1], 3, None, A.bitwise_and, r=["IK"], w=["IJ4"])
    ts(T.ID[:], T.KM[:], 0.0, None, A.is_equal, r=["KM"], w=["ID"])
    ts(T.NDN[:], KM, -1.0, -1.0, A.is_equal, A.mult, r=["KM"], w=["NDN"])
    ts(T.UP[:], KM, 1.0, None, A.is_equal, r=["KM"], w=["UP"])
    ts(T.MK[:, 4:8], T.IJ[:, 0:4], 0.0, None, A.is_equal, r=["IJ0"], w=["MKo"])
    ts(col(SG), T.IJ[:, 4:5], -1.0, 1.0, A.mult, A.add, r=["IJ1"], w=["SG"])
    ts(T.NDN[:, 0::4], T.KM[:, 12:140:4], 3.0, -1.0, A.is_equal, A.mult, r=["KM"], w=["NDN"])
    ts(T.UP[:, 3::4], T.KM[:, 15:140:4], -3.0, None, A.is_equal, r=["KM"], w=["UP"])
    ts(col(YH), T.IJ[:, 7:8], 3.0, 0.5, A.is_equal, A.mult, r=["IJ4"], w=["YH"])
    act(T.NI[:], ID, -1.0, r=["ID", "LUT"], w=["NI"])
    act(T.MK[:, 0:4], T.MK[:, 4:8], col(SG), r=["MKo", "SG"], w=["MKe"])
    act(T.IB[:], T.ID[:], r=["ID"], w=["IB"])
    act(T.NB[:], ID, -1.0, r=["ID"], w=["NB"])
    act(T.I2[:], ID, 2.0, r=["ID"], w=["I2"])
    act(T.I3[:], ID, 3.0, r=["ID"], w=["I3"])
    act(col(SH), col(SG), -0.5, r=["SG"], w=["SH"])
    mm(T.PH[:, 0::2], [(T.ZB[:, 0:128], T.ZB[:, 0:256], ["Z"])], ["PH0"], ["H"])
    mm(T.PB[:, 128:256:2], [(T.ZB[:, 0:128], T.ZB[:, 0:64], ["Z"])], ["PBz"], ["B"])
    mm(T.PG[:, 0:128], [(T.NI[:], ID, ["ID"]), (T.NI[:], T.NDN[:], ["NDN"])], ["PG"], ["G"])
    mm(T.PG[:, 128:256], [(ID, ID, []), (T.NI[:], T.UP[:], ["UP"])], ["PG"], ["G"])


    kw = 384 if KB else 256
    ts(T.KO[:, 0:kw], T.KI[:, 0:kw], 1, None, A.bitwise_and, r=["K0", "K1"] + ["BI"] * KB, w=["KO"])
    ts(T.E5[:, 0:kw], T.KI[:, 0:kw], 0.5, None, A.add, r=["K0", "K1"] + ["BI"] * KB, w=["E5"])
    ts(T.PC[:, 0:kw], T.KO[:, 0:kw], -1.0, 0.5, A.mult, A.add, r=["KO"], w=["PC0"], b=["C"])
    if not KB:
        ts(T.KO[:, 256:384], T.KI[:, 256:384], 1, None, A.bitwise_and, r=["BI", "KO"], w=["KOb"])
    tt(T.PC[:, 384:512], T.PC[:, 0:128], T.E5[:, 0:128], A.mult, r=["PC0", "E5"], w=["PC1"], b=["C"])
    tt(T.BF[:, 0:kw - 128], T.PC[:, 128:kw], T.E5[:, 128:kw], A.mult, r=["PC0", "E5"], w=["BK"] + ["BF"] * KB, b=["C"])
    if not KB:
        ts(T.E5[:, 256:384], T.KI[:, 256:384], 0.5, None, A.add, r=["BI", "PC0"], w=["E5b"])
    tt(T.PD[:, 0:128], T.PC[:, 384:512], T.BF[:, 0:128], A.subtract, r=["PC1", "BK"], w=["PD0"], b=["C", "D"])
    tt(T.PD[:, 128:256], T.PC[:, 384:512], T.BF[:, 0:128], A.add, r=["PC1", "BK"], w=["PD1"], b=["C", "D"])
    ts(T.HI[:, 0:128], T.PD[:, 0:128], B64, B64, A.add, A.subtract, r=["PD0"], w=["HI", "HIw"], b=["D"])
    ts(T.HI[:, 128:256], T.PD[:, 128:256], B64, B64, A.add, A.subtract, r=["PD1"], w=["HId"], b=["D"])
    tt(T.LO[:, 0:128], T.PD[:, 0:128], T.HI[:, 0:128], A.subtract, r=["PD0", "HI"], w=["LO", "LOw"], b=["D"])
    tt(T.LO[:, 128:256], T.PD[:, 128:256], T.HI[:, 128:256], A.subtract, r=["PD1", "HId"], w=["LOd"], b=["D"])
    if not KB:
        ts(T.PC[:, 256:384], T.KO[:, 256:384], -1.0, 0.5, A.mult, A.add, r=["KOb"], w=["PC2"], b=["C"])
    cp(T.FB[0:8, :], T.FI[0:8, :], r=["FI"], w=["FB"])
    if not KB:
        tt(T.BF[:, 128:256], T.PC[:, 256:384], T.E5[:, 256:384], A.mult, r=["PC2", "E5b"], w=["BF"], b=["C"])
    act(T.FT[:, rev(3071, 1024, 1)], T.FT[:, 3072:4096], -1.0, 255.0, r=["FTa"], w=["FTc"])
    dma("s", T.FT[:, 0:1024], T.FT[:, 2048:3072], r=["FTc"], w=["FTo0", "FTo1"])
    act(T.FT[:, rev(2047, 1024, 1)], T.FT[:, 4096:5120], -1.0, 255.0, r=["FTb"], w=["FTd"])

    wd = lambda b, dd: T.WD[:, 12 + b - 4 * dd:12 + b - 4 * dd + 509:4]
    halves = [(T.PF, "F", ["PY"]), (T.PE, "E", ["PE0", "PE1", "PE2", "PE3"])]
    for pb, bk, key in halves:
        mm(pb[:, 0:256], [(T.ZB[:, 0:128], T.ZB[:, 0:256], [])], key, [bk], stop=False)
    for dd, src, k in ((0, T.HI[:, 0:128], "HI"), (2, T.HI[:, 128:256], "HId"), (1, T.LO[:, 0:128], "LO"), (3, T.LO[:, 128:256], "LOd")):
        for b in range(4):
            pb, bk, key = halves[b // 2]
            mm(pb[:, 128 * (b % 2):128 * (b % 2) + 128], [(wd(b, dd), src, [k])], key, [bk], start=False, stop=dd == 3 and b % 2 == 1)
    act(T.YS[:, 0:256], T.PF[:, 0:256], 1.0, col(YH), r=["PY", "YH"], w=["YS0"], b=["F"])
    ts(T.YS[:, 256:512], T.PE[:, 0:256], col(YH), None, A.add, r=["PE0", "PE1", "PE2", "PE3", "YH"], w=["YS1"], b=["E"])
    for e in range(2):
        mm(T.PB[:, 64 * e:64 * e + 64],
           [(T.RM[:, 16 + e - 16 * h:16 + e - 16 * h + 255:2], T.BF[:, 128 + h::2], ["BF"]) for h in range(2)], ["PB%d" % e], ["B"])
    aa, bb = T.AB[:, 1:128:2], T.AB[:, 129:256:2]
    mm(T.PA[:, 0:64], [(T.FF[0:8, 12 - 4 * q:140 - 4 * q], T.FB[0:8, q::4], ["FB"]) for q in range(4)], ["PA0"], ["A"])
    belts = [
        lambda: ts(T.AB[:, 1::2], T.PB[:, 0:128], 0.25, None, A.add, r=["PB0", "PB1"], w=["AB"], b=["B"]),
        lambda: cp(T.D2[:, 1::2], T.PA[:, 0:64], r=["PA0", "D2z"], w=["D2"], b=["A"]),
        lambda: tt(T.AB[:, 0:128:2], bb, aa, A.subtract, r=["AB"], w=["AB0"]),
        lambda: mm(T.PB[:, 0:64], [(T.UP[:], aa, ["AB"])], ["PB0"], ["B"]),
        None,
        lambda: scan(T.SE[:, 0:128], T.D2[:], T.AB[:, 0:128], r=["D2", "AB", "AB0"], w=["SE"]),
        lambda: tt(T.AB[:, 128:256:2], T.PB[:, 0:64], bb, A.subtract, r=["AB", "PB0"], w=["AB1"], b=["B"]),
        lambda: ts(T.SE[:, 0:128:2], T.SE[:, 1:128:2], B4K, B4K, A.add, A.subtract, r=["SE"], w=["SEj"]),
        lambda: scan(T.SE[:, 128:256], T.D2[:], T.AB[:, 128:256], r=["D2", "AB", "AB1"], w=["SW"]),
        lambda: scan(T.TN[:], T.MD[:], T.SE[:, 0:128], r=["MD", "SE", "SEj"], w=["TN"]),
        lambda: ts(T.MI0[:], T.SE[:, 1:256:2], MID, None, A.add, r=["SE", "SW"], w=["MI0e", "MI0w"]),
        lambda: ts(T.E0[:], T.TN[:, 1::2], MID - 1024, None, A.add, r=["TN"], w=["E0"]),
        None,
    ]
    act(T.DNI[:], T.PG[:, 0:128], r=["PG"], w=["DNI"], b=["G"])
    act(T.IUP[:], T.PG[:, 128:256], r=["PG"], w=["IUP"], b=["G"])

    def expand(out, src, j, t, r, w):
        m = T.MK[:, 4 * t + j:4 * t + j + 1]
        ts(out, src, m, None, A.mult, r=r + ["MKe", "MKo"], w=w, stepped=H5 >= (1 if src.name != "YS" else 2 if t else 3))
        act(out, src, m, r=r + ["MKe", "MKo"], w=w)
        either()

    kts = ["KTs%d" % k for k in range(8)]
    ktd = ["KTd%d" % k for k in range(8)]
    for k in range(8):
        a, t = k // 2, k % 2
        out = T.KT[:, rev(3071 - 512 * a, 512, 1)] if t else T.KT[:, 3072 + 512 * a:3584 + 512 * a]
        while k in BK and belts[0]:
            belts.pop(0)()
        if k in BK:
            belts.pop(0)
        expand(out, T.YS[:], a, t, ["YS0", "YS1"], [kts[k]])

    part[0] = "const"
    band(T.NB4[:], T.NEG, [[-4, 32], [0, 4]], 0, 4, ["NB4"])
    iota(T.TA[:], [[16, 64], [-1024, 2]], C0 + 1024, 1, ["TAe", "TAo"])
    const(T.QM[:, 0::4], 8.0, ["QM0"])
    const(T.QM[:, 3::4], -0.8125, ["QM"])
    iota(T.ALT[:], [[0, 32], [2, 2]], -1, 0, ["ALT"])
    for q in range(4):
        pat = [[-16, 8], [-1, 4], [0, 2]]
        sel(T.WU[:, 4 + q:516:8], T.HLF[:], pat, A.is_equal, 0.0, -4 * q, 1, ["HLF"], ["WU%d" % q])
        sel(T.WW[:, 4 + q:516:8], T.ALT[:], pat, A.is_equal, 0.0, -4 * q, 1, ["ALT"], ["WW%d" % q])
    sel(T.ZM[:], T.NB4[:], [[-1, 128]], A.not_equal, 2.0, 0, 1, ["NB4"], ["ZM"])

    for q in range(4):
        point(T.RP[:, 128 * q:128 * q + 128], T.ZB[:, 0:128], [[-16, 8], [-1, 4], [0, 4]], -4 * q, 1.0, ["RP%d" % q])

    ybuf, tbuf = [T.Y0, T.Y1], [(T.TA, "TA"), (T.TB, "TB")]
    ft = ["FTa", "FTb", "FTc", "FTd", "FTe0", "FTe1", "FTe2", "FTo0", "FTo1"]
    for t in range(RO):
        part[0] = ""
        last = t == RO - 1
        MI = T["MI%d" % t]
        e_, w_, f_ = "MI%de" % t, "MI%dw" % t, "GI%d" % t
        yo, yn = ybuf[t % 2], ybuf[(t + 1) % 2]
        yok, ynk = "Y%d" % (t % 2), "Y%d" % ((t + 1) % 2)
        if t == 0:
            kw, eo, kr = T.KT[:, 1024:5120], T.E0, kts + ["E0"]
            xE, xW, ke, kh = T.SE[:, 1:128:2], T.SE[:, 129:256:2], ["SE"], ["SW"]
            fp, kf = T.D2[:, 1::2], ["D2"]
        else:
            arrive([e_, w_], "ae%d" % t)
            kw, eo, kr = T.KT[:, 0:6144], MI, kts + ktd + [e_]
            xE, xW, ke, kh = T.EW[:, 0:64], T.EW[:, 64:128], ["EW"], ["EW"]
            fp, kf = T.F1[:], ["F1"]
        sk = lambda s: T.PE[:, s:256:4]
        sh = lambda s: T.PE[:, 256 + s:512:4]
        zero = (T.ZB[:, 0:128], T.ZB[:, 0:64], [])
        pe, ne, pw, nw = (ID, xE, ke), (T.NI[:], xE, ke), (ID, xW, kh), (T.NI[:], xW, kh)
        if last:
            slots_k = [[ne], [pe, pe], [ne], [zero]]
            slots_h = [[nw], [pw, pw], [nw], [zero]]
        else:
            slots_k = [[(T.NDN[:], xW, kh)], [(T.DNI[:], xW, kh)], [pe, pw], [ne]]
            slots_h = [[ne], [(T.IUP[:], xE, ke)], [(T.UP[:], xE, ke), pw], [nw]]
        slots_h[0].insert(0, (ID, T.MH[:], ["MH"]))
        vs = 2 if last else 3

        def slots():
            for s in (3,) if last else (1, 2):
                mm(sh(s), slots_h[s][0:1], ["PE%d" % (4 + s)], ["E"])
            for s in (3, 0) if last else (1, 0):
                mm(sk(s), slots_k[s], ["PE%d" % s], ["E"], stop=s > 0)

        def slots_v():
            tt(sh(0), T.MH[:], xW if last else xE, A.subtract, r=["MH"] + ke + kh, w=["PE4"], b=["E"])
            if last:
                ts(T.PE[:, 1::4], MI[:, 0:128], 2.0, -2 * MID, A.mult, A.add, r=[e_, w_], w=["PE1", "PE5"], b=["E"])
            else:
                tt(sk(2), xW, sk(3), A.subtract, r=kh + ["PE3"], w=["PE2"], b=["E"])
                tt(sh(2), sh(2), xW, A.add, r=kh, w=["PE6"], b=["E"])

        part[0] = ""
        if EARLY:
            if t > 0:
                ts(T.EW[:], MI[:, 0:128], -MID, None, A.add, r=[e_, w_], w=["EW"])
            if EARLY == 1:
                slots()
                mm(T.PA[:, 64:128], [pw], ["PA1"], ["A"])
        cp(T.GK[:, 0:16 * GCUT], kw.indirect(eo[:, 0:GCUT]), r=kr, w=["GK0"], gather=True)
        act(T.GK[:, 16 * GCUT:1024], kw.indirect(eo[:, GCUT:64]), r=kr, w=["GK1"], gather=True)
        mm(T.PA[:, 0:64], [(T.BM[:, 15 - r:143 - r], T.GK[:, r::16], ["BM", "GK0", "GK1"]) for r in range(16)], ["PA0"], ["A"])
        if EARLY == 2:
            slots()
        part[0] = "slots"
        if t > 0 and not EARLY:
            ts(T.EW[:], MI[:, 0:128], -MID, None, A.add, r=[e_, w_], w=["EW"])
        if t == 1:
            arrive(["F0"], "af")
            cp(T.F2[:], MI[:, 128:192], r=[e_], w=["F2"])
            tt(T.F1[:], T.F0[:, 1::2], T.F2[:], A.not_equal, r=["F0", "F2"], w=["F1"])
        elif t > 1:
            cp(fp, MI[:, 128:192], r=[e_], w=kf)
        part[0] = ""
        fw = [[], []]
        for c0, c1 in zip(FWCUT, FWCUT[1:]):
            src = T.FT[:, 0:6144].indirect(MI[:, 64 + c0:64 + c1])
            (cp if c0 == 0 and FWV else act)(T.FW[:, 16 * c0:16 * c1], src, r=ft + [w_], w=["FW%d" % c0], gather=True)
            for h in range(2):
                if c0 < 32 * h + 32 and c1 > 32 * h:
                    fw[h].append("FW%d" % c0)
        ts(T.UO[:], T.PA[:, 0:64], 0.5, MID, A.mult, A.add, r=["PA0"], w=["UO"], b=["A"])
        ts(T.PE[:, vs::4], MI[:, 0:128], -1.0, MID, A.mult, A.add, r=[e_, w_], w=["PE%d" % vs, "PE%d" % (4 + vs)], b=["E"])
        if EARLY == 2 or WC:
            mm(T.PA[:, 64:128], [pw], ["PA1"], ["A"])
        xs = 16 * XS
        for h, (c0, c1) in enumerate([(0, 32), (32, XS)]):
            tt(T.DD[:, 16 * c0:16 * c1], T.FT[:, 0:6144].indirect(T.UO[:, c0:c1]), T.FW[:, 16 * c0:16 * c1], A.subtract,
               r=ft + ["UO"] + ["FW%d" % a for a, b in zip(FWCUT, FWCUT[1:]) if a < c1 and b > c0], w=["DD%d" % h], gather=True)
        if XS < 64:
            act(T.DD[:, xs:1024], T.FT[:, 0:6144].indirect(T.UO[:, XS:64]), r=ft + ["UO"], w=["FU"], gather=True)
            mm(T.PA[:, xs - 512:512], [(T.NB[:], T.FW[:, xs:1024], fw[1]), (IB, T.DD[:, xs:1024], ["FU"])], ["PAd"], ["A"])
        ns = NS if t > 0 else 0
        if ns:
            act(T.NR[:, 0:ns], T.DD[:, 0:ns], r=["DD0"], w=["NRa"], f=AF.Abs)
            act(T.NR[:, 0:ns], T.NR[:, 0:ns], -1000.0, 16500.0, ["NRa"], ["NRa"], f=AF.Sigmoid)
        if XS < 64:
            ts(T.NR[:, ns:xs], T.DD[:, ns:xs], B32, B32, A.add, A.is_equal, r=["DD0", "DD1"], w=["NRb"] + ["NRa"] * (ns == 0))
            for x in range(2):
                ts(T.NR[:, xs + x::2], T.PA[:, xs - 512 + x:512:2], B32, B32, A.add, A.is_equal, r=["PAd"], w=["NR%d" % x], b=["A"])
        def digits():
            ts(T.HI[:, 0:128], T.PA[:, 0:128], 2 * B64, 2 * B64, A.add, A.subtract, r=["PA0", "PA1"], w=["HI", "HIw"], b=["A"])

        if EARLY == 1:
            digits()
        if PAR == 2:
            ts(T.NR[:, ns:512], T.DD[:, ns:512], B32, B32, A.add, A.is_equal, r=["DD0"], w=["NRb"] + ["NRa"] * (ns == 0))
            ns = 512
        for x in range(2 * (XS == 64 and PAR > 0)):
            ts(T.NR[:, ns + x::2], T.DD[:, ns + x::2], B32, B32, A.add, A.is_equal, r=["DD0", "DD1"],
               w=["NR%d" % x] + ["NRa"] * (ns == 0 and x == 0))
        if XS == 64 and not PAR:
            ts(T.NR[:, ns:1024], T.DD[:, ns:1024], B32, B32, A.add, A.is_equal, r=["DD0", "DD1"], w=["NR0", "NR1"] + ["NRa"] * (ns == 0))
        if EARLY == 2 or WC:
            digits()
        part[0] = "count"
        if t > 0:
            add("a", lambda: S.activation(T.TN[:, 0:64], T.PB[:, 256:320], AF.Identity, bias=-1.0 / 128, accum_out=col(RED)),
                140, ["PFa"], ["RED", "TN"], ["B"])
        if t == 0:
            ts(col(G16), T.IJ[:, 5:6], T.TA[:, 1:2], None, A.subtract, r=["IJ2", "TAo"], w=["G16"])
            act(col(RM5), col(G16), -1.0, -2048.5, r=["G16"], w=["RM5"])
            act(T.MH[:], T.TA[:, 1::2], -1.0, col(RM5), r=["TAo", "RM5"], w=["MH"])
        mm(T.PG[:, 0:256], [(T.NB4[:], T.QM[:], ["QM0", "QM"])], ["PG"], ["G"], stop=False)
        part[0] = "kids"
        if t == 0:
            for a in range(2):
                mm(T.PH[:, 1 + 256 * a:256 + 256 * a:2],
                   [(T.IB[:, 12 + 4 * (a - j):140 + 4 * (a - j)], T.KT[:, 3072 + 512 * a + j:3584 + 512 * a:4], [kts[2 * a]])
                    for j in range(4)], ["PH1"], ["H"])
            act(yo[:, 1::2], T.PH[:, 1::2], col(SG), r=["PH1"], w=[yok + "o"], b=["H"])
            part[0] = "first"
            act(T.Z1[:], T.NB4[:], -0.5, r=["NB4"], w=["Z1"])
            act(T.WA[:], T.BM[:], col(SH), r=["BM", "SH"], w=["WA"])
            sel(T.Z1[:], T.Z1[:], [[-1, 128]], A.not_equal, 1.5, 0, 1, ["Z1"], ["Z1"])
            send(T.F0[:], T.D2[:], ["D2", "RP3"], "af")


        def half_sum(h, first):
            pb, bk = (T.PC, "C") if h == 0 else (T.PD, "D")
            lh, src, k = (T.I2[:], T.FW, fw[h]) if first else (IB, T.DD, ["DD%d" % h])
            if first and h == 1 and XS < 64:
                mm(pb[:], [(lh, src[:, 512:1024], k)], ["S1"], [bk], True, False)
                mm(pb[:, xs - 512:512], [(T.NB[:], src[:, xs:1024], k)], ["S1"], [bk], False, False)
            else:
                mm(pb[:], [(lh, src[:, 512 * h:512 * h + 512], k + ["FU"] * h)], ["S%d" % h], [bk], first, not first)
            if not first:
                c0 = 1024 * (t + 1) + 512 * h
                act(T.VW[:, c0:c0 + 512], pb[:], 0.5 - 2.0 ** -10, BIG, r=["S%d" % h], w=["VW%d_%d" % (t + 1, h)], b=[bk])

        def y_cands():
            mm(T.PF[:, 256:512], [(T.NB[:], yo[:, 1::2], [yok + "o"])], ["PY"], ["F"], stop=False)
            for wt, c, z in ((T.WW, 64, "w"), (T.WU, 0, "")):
                for x, src in enumerate([T.HI, T.LO]):
                    for q in range(4):
                        c0 = q + 4 - 4 * x
                        mm(T.PF[:, 256 + q:512:4], [(wt[:, c0:c0 + 509:4], src[:, c:c + 64], [src.name + z, "%s%d" % (wt.name, q)])],
                           ["PY"], ["F"], start=False, stop=(c, x, q) == (0, 1, 3))
            if YD == 0:
                y_diff()

        def y_diff():
            act(yo[:, 0::2], T.PF[:, 256:512], r=["PY"], w=[yok + "e"], b=["F"])
            if YD == 2:
                cp(yo[:, 0::2], T.PF[:, 256:512], r=["PY"], w=[yok + "e"], b=["F"])
                either()

        def sums():
            for first in (True, False):
                for h in range(2):
                    half_sum(h, first)

        if SUMS == 0 or last:
            sums()
        part[0] = "first"
        if t == 0:
            act(T.ZK[:], T.Z1[:], KS, r=["Z1"], w=["ZK"])
        part[0] = ""
        mm(T.PB[:, 0:64], [(T.NB4[:], T.Q9[:], ["Q9"])] * (t > 0)
           + [(T.BM[:, 15 - r:143 - r], T.NR[:, r::16], ["NRa", "NRb", "NR%d" % x]) for x in range(2) for r in range(x, 16, 2)],
           ["PB0"], ["B"])
        if SUMS == 1:
            sums()
        part[0] = "spare"
        if t == 3:
            act(T.KF[:], T.E5[:, 0:256], 1.0, -0.5, r=["E5"], w=["KF"])
            dma("s", T.y0[:, 0:2048], T.KF[:, 0:128], r=["KF", "DD0"])
            dma("s", T.y1[:, 0:2048], T.KF[:, 128:256], r=["KF", "DD0"])
        if t in (1, 2):
            dma("s", T.yx[:, 1024 * t - 1024:1024 * t], T.FT[:, 2048 + 1024 * t:3072 + 1024 * t], r=["DD0"])
        if t in (1, 2):
            k = t - 1
            for j in range(4):
                act(T.WK[:, 68 * j + 32 * k + 3:68 * j + 32 * k + 32:4], T.WA[:, 15:128:16], T.MK[:, 4 + j:5 + j],
                    r=["WA", "WK"], w=["WK%d%d" % (j, k)], f=AF.Identity if k else AF.Abs)
        part[0] = "slots"
        if t > 0:
            ts(col(RND), col(RED), B2, B2, A.add, A.subtract, r=["RED"], w=["RND"])
        part[0] = ""
        if t == 0:
            ts(T.SP[:], T.PB[:, 0:64], 9.0, None, A.is_ge, r=["PB0"], w=["SP"], b=["B"])
        else:
            ts(T.SP[:], T.PB[:, 0:64], col(RND), col(RED), A.add, A.is_ge, r=["PB0", "RND", "RED"], w=["SP"], b=["B"])
        mm(T.PG[:, 3 if last else 2:256:4], [(T.I3[:], fp, ["I3"] + kf)], ["PG"], ["G"], start=False, stop=False)
        mm(T.PG[:, 1:256:4], [(T.Z1[:], T.SP[:], ["Z1", "SP"])], ["PG"], ["G"], start=False, stop=False)
        if not last:
            mm(T.PG[:, 2:256:4], [(T.Z1[:], T.SP[:], [])], ["PG"], ["G"], start=False, stop=False)
        mm(T.PG[:, 2 if last else 3:256:4], [(T.ZM[:], T.SP[:], ["ZM"])], ["PG"], ["G"], start=False)
        mm(T.PB[:, 129:256:2], [(T.ZK[:], T.SP[:], ["ZK", "SP"])], ["PBz"], ["B"])
        step(T.D0[:], T.PG[:, 0:256], 1.75, ["PG"], ["D0"], ["G"])

        def scan_k():
            scan(T.SE[:, 0:256], T.D0[:], T.PE[:, 0:256], r=["D0", "PE0", "PE1", "PE2", "PE3"], w=["SE", "SW", "SEj"], b=["E"])

        def scan_h():
            scan(T.SE[:, 256:512], T.D0[:], T.PE[:, 256:512], r=["D0", "PE4", "PE5", "PE6", "PE7"], w=["SH2"], b=["E"])

        def versions():
            (ti, tik), (to, tok) = tbuf[t % 2], tbuf[(t + 1) % 2]
            scan(to[:], T.PB[:, 128:256], ti[:], ["PBz", tik + "e", tik + "o"], [tok + "e", tok + "o"], ["B"], A.min, A.max)
            ts(T.LC[:], to[:, 1::2], col(G16), None, A.add, r=[tok + "o", "G16"], w=["LC"])
            return to, tok

        mm(T.PB[:, 320:384], [(T.I3[:], fp, kf)] * (t > 0) + [(T.NB4[:], T.SP[:], ["SP"])], ["PBf"], ["B"])
        if last or TMF == 1:
            to, tok = versions()
        if not EARLY:
            slots()
        slots_v()
        mm(sk(0), [(T.WA[:, 15 - r:143 - r], T.GK[:, r::16], ["GK0", "GK1"]) for r in range(16)], ["PE0"], ["E"], start=False)
        if not EARLY and not WC:
            mm(T.PA[:, 64:128], [pw], ["PA1"], ["A"])
        if not last:
            u = t + 1
            MO = T["MO%d" % u]
            if t == 0:
                ts(MO[:, 128:192], T.PB[:, 320:384], -1.5, None, A.is_ge, r=["PBf"], w=["GO%d" % u], b=["B"])
            else:
                ts(MO[:, 128:192], T.PB[:, 320:384], B4, B4, A.add, A.is_equal, r=["PBf"], w=["GO%d" % u], b=["B"])
            scan_h()
            if TMF == 2:
                to, tok = versions()
            scan_k()
            if MO2:
                ts(MO[:, 64:128], T.SE[:, 259::4], -1.0, MID, A.mult, A.add, r=["SH2"], w=["MOw%d" % u])
                ts(MO[:, 0:64], T.SE[:, 3:256:4], -1.0, MID, A.mult, A.add, r=["SE"], w=["MOe%d" % u])
            else:
                ts(MO[:, 0:128], T.SE[:, 3::4], -1.0, MID, A.mult, A.add, r=["SE", "SH2"], w=["MOe%d" % u])
            send(T["MI%d" % u][:], MO[:], ["MOw%d" % u, "MOe%d" % u, "GO%d" % u], "ae%d" % u)
            if not TMF:
                to, tok = versions()
            iota(to[:, 0::2], [[16, 64]], C0 + 1024 * (t + 2), 1, [tok + "e"])
        if SUMS == 2 and not last:
            sums()
        if not EARLY and not WC:
            digits()
        tt(T.LO[:, 0:128], T.PA[:, 0:128], T.HI[:, 0:128], A.subtract, r=["PA0", "PA1", "HI"], w=["LO", "LOw"], b=["A"])
        y_cands()
        for q in range(4):
            mm(T.PH[:, 1 + 2 * q::8], [(T.RP[:, 128 * q:128 * q + 128], T.D0[:, 1::4], ["RP%d" % q, "D0"])], ["PH1"], ["H"])

        def y_scan():
            scan(yn[:], T.PH[:], yo[:], r=["PH0", "PH1", yok + "e", yok + "o"], w=[ynk + "e", ynk + "o"], b=["H"])

        if t == 0:
            for h in range(2):
                act(T.VW[:, 512 * h:512 * h + 512], T.FT[:, 3072 + 512 * h:3584 + 512 * h], 1.0, BIG, r=["FTa"], w=["VW0_%d" % h])
        vw = ["VW%d_%d" % (k, h) for k in range(t + 2) for h in range(2)]
        win = T.VW[:, 0:1024 * (t + 2)]

        cut = FCUT[last]

        def faces(h):
            c0, c1 = cut[h], cut[h + 1]
            if c0 == c1:
                return
            out = T.YX[:, 16 * c0:16 * c1] if last else T.FT[:, 5120 + 16 * c0:5120 + 16 * c1]
            src, key = win.indirect(T.LC[:, c0:c1]), [("YX%d" if last else "FTe%d") % h]
            if h < 2:
                act(out, src, 1.0, -BIG, r=vw + ["LC"], w=key, gather=True)
            elif c1 > c0:
                ts(out, src, -BIG, None, A.add, r=vw + ["LC"], w=key, gather=True)
            if last and c1 > c0:
                dma("s", T.yx[:, 2048 + 16 * c0:2048 + 16 * c1], out, r=key)

        def turn(h):
            c0, c1 = (0, 16 * cut[1]) if h == 0 else (16 * cut[1], 1024)
            ts(T.FT[:, rev(1023 - c0, c1 - c0, 1)], T.FT[:, 5120 + c0:5120 + c1], -1.0, 255.0, A.mult, A.add,
               r=["FTe0"] if h == 0 else ["FTe1", "FTe2"], w=["FTo%d" % h], stepped=H5 >= 2)

        if last:
            break
        if t == 0:
            const(T.O4[:], 0.25, ["O4"])
            const(T.N4[:], -0.25, ["N4"])
            const(T.Q9[:], 2.25, ["Q9"])
        mm(T.PB[:, 256:320], [(T.O4[:], T.D0[:, 3:256:4], ["D0"]), (T.N4[:], T.D0[:, 1:256:4], [])], ["PFa"], ["B"])
        faces(0)
        if YD:
            y_diff()
        y_scan()
        faces(1)
        faces(2)
        for k in range(8):
            j, tn = k // 2, k % 2
            out = T.KT[:, rev(1023 - j, 256, 4)] if tn else T.KT[:, 5120 + j::4]
            expand(out, yn[:, 1::2], j, tn, [ynk + "o"], [ktd[k]])
            if k == 1:
                turn(0)
        turn(1)
        part[0] = "const"
        if t == 0:
            point(T.FQ[:], T.ZB[:, 0:32], [[-4, 4], [-16, 8]], 0, 1.0, ["FQ"])
            iota(T.ZF[:], [[0, 128]], 0, 0, ["ZF"])
        if t in (1, 2):
            h = t - 1
            p3, p2 = [[-16, 8], [-1, 8], [-1000, 2]], [[-16, 8], [-1, 8]]
            m = [T.RR[:, 128 * (4 * h + k):128 * (4 * h + k) + 128] for k in range(4)]
            c = [128 * (4 * h + k) for k in range(4)]
            key = ["RR%d" % (4 * h + k) for k in range(4)]
            for e in range(2):
                sel(m[e], T.ZF[:], p3, A.not_equal, 1.0, 1000 * e - 8 * h, 1, ["ZF"], [key[e]])
            sel(m[2], m[1], p3, A.not_equal, -1.0, -8 * h, 1, [key[1]], [key[2]])
            sel(T.RR[:, c[3]:c[3] + 128:2], T.ZF[:, 0:64], p2, A.not_equal, 1.0, 1 - 8 * h, 1, ["ZF"], [key[3]])
            sel(T.RR[:, c[3]:c[3] + 128:8], T.ZF[:, 0:16], [[-16, 8], [-4, 2]], A.not_equal, 1.0, -3 - 8 * h, 1, ["ZF"], [key[3]])
            sel(T.RR[:, c[3] + 1:c[3] + 128:2], T.ZF[:, 0:64], p2, A.not_equal, -1.0, -8 * h, 1, ["ZF"], [key[3]])
        if t == RO - 2:
            const(T.QM[:, 3::4], 0.0, ["QM"])
            const(T.QM[:, 2::4], -0.8125, ["QM"])

    part[0] = ""
    faces(0)
    if YD:
        y_diff()
    faces(1)
    ts(T.F2[:], T.PB[:, 320:384], B4, B4, A.add, A.is_equal, r=["PBf"], w=["F2"], b=["B"])
    scan_k()
    scan_h()
    y_scan()
    faces(2)
    srcs = [(0, T.SE[:, 2:256:4], "SE"), (2, T.SE[:, 3:256:4], "SE"), (1, T.SE[:, 258::4], "SH2"), (3, T.SE[:, 259::4], "SH2")]
    back = [(T.PB, "B"), (T.PD, "D")]
    for z in range(2):
        for h, (pb, bk) in enumerate(back):
            mm(pb[:, 256:320], [(T.RR[:, 128 * (4 * h + k):128 * (4 * h + k) + 128], rh, ["RR%d" % (4 * h + k), rk])
                                for k, rh, rk in srcs[2 * z:2 * z + 2]], ["PBo%d" % h], [bk], z == 0, z == 1)
    for h, (pb, bk) in enumerate(back):
        act(T.OB[:, h::2], pb[:, 256:320], -2.0, -0.5, r=["PBo%d" % h], w=["OB%d" % h], b=[bk], f=AF.Abs)

    for j in range(4):
        mm(T.PF[0:64, j:256:4], [(T.WK[:, 68 * j + 3 - ib:68 * j + 67 - ib], yn[:, 1 + 128 * ib:128 + 128 * ib:2],
                                  ["WK%d0" % j, "WK%d1" % j, ynk + "o"]) for ib in range(4)], ["PK"], ["F"])

    act(T.OUT[0:64, :], T.PF[0:64, 0:256], 2.0, -0.5, r=["PK"], w=["OUT"], b=["F"], f=AF.Abs)
    ts(T.OU2[0:64, :], T.OUT[0:64, :], -0.5, None, A.add, r=["OUT"], w=["OU2"])
    dma("s", T.y0[:, 2048:3072], T.OU2[0:32, :], r=["OU2"])
    dma("a", T.y1[:, 2048:3072], T.OU2[32:64, :], r=["OU2"])
    for q in range(4):
        mm(T.PA[0:8, 256 + q:512:4], [(T.FQ[:, 8 * q:8 * q + 8], T.F2[:], ["F2"])], ["PGf%d" % q], ["A"])
    ts(T.OB2[:], T.OB[:], -0.5, None, A.add, r=["OB0", "OB1"], w=["OB2"])
    dma("s", T.yb[:], T.OB2[:], r=["OB2"])
    cp(T.FO[0:8, :], T.PA[0:8, 256:512], r=["PGf%d" % q for q in range(4)], w=["FO"], b=["A"])
    dma("s", T.yf[:], T.FO[0:8, :], r=["FO"])
    emit(g, T, ops)
